import numpy as np
import ml_dtypes


def mxq(x, axis, fmt="e4m3"):
    dtype, down = {"e4m3": (ml_dtypes.float8_e4m3fn, 7), "e5m2": (ml_dtypes.float8_e5m2, 14)}[fmt]
    v = np.moveaxis(np.asarray(x, np.float32).astype(ml_dtypes.bfloat16).astype(np.float64), axis, -1)
    blocks = v.reshape(v.shape[:-1] + (-1, 32))
    amax = np.abs(blocks).max(-1, keepdims=True)
    byte = np.maximum(np.where(amax > 0, np.frexp(amax)[1] - 1 + 127, 0) - down, 1)
    scale = np.exp2(byte - 127.0)
    codes = (blocks / scale).astype(np.float32).astype(dtype).astype(np.float64)
    return np.moveaxis((codes * scale).reshape(v.shape), -1, axis)


WIDE = False


def mx_kscale(k):
    if not WIDE:
        return np.ones(k)
    levels = np.array([10, -10, 5, -5, 0])
    if k % 512:
        return np.exp2(np.random.permutation(np.resize(levels, k // 32))).repeat(32)
    a = np.empty((k // 512, 16))
    for p in range(k // 512):
        a[p, :8] = np.random.permutation(np.resize(levels, 8))
        for g in range(8):
            far = levels[np.abs(levels - a[p, g]) >= 10]
            a[p, g + 8] = far[np.random.randint(len(far))]
    return np.exp2(a.ravel()).repeat(32)


def f64(x):
    return np.asarray(x).astype(np.float64)


def striped(idx):
    return np.tile(idx.reshape(-1, 16).T, (8, 1)).astype(np.uint16)


def unstriped(offs):
    return offs[:16].T.reshape(-1).astype(np.int64)


E2M1 = np.array([0.0, 0.5, 1.0, 1.5, 2.0, 3.0, 4.0, 6.0, -0.0, -0.5, -1.0, -1.5, -2.0, -3.0, -4.0, -6.0])


def pack_weight(w, fmt):
    k, n = w.shape
    w = f64(np.asarray(w, np.float32).astype(ml_dtypes.bfloat16)).reshape(k // 32, 32, n)
    amax = np.abs(w).max(1)
    if fmt == "e4m3":
        byte = np.frexp(amax)[1] - 1 + 127 - 7
    else:
        mant, ex = np.frexp(amax / 6.0)
        byte = np.where(mant > 0.5, ex, ex - 1) + 127
    byte = np.clip(np.where(amax > 0, byte, 1), 1, 254)
    scaled = (w * np.exp2(127.0 - byte)[:, None, :]).reshape(k, n).astype(np.float32)
    by_word = np.ascontiguousarray(scaled.reshape(k // 512, 128, 4, n).transpose(0, 1, 3, 2))
    if fmt == "e4m3":
        words = by_word.astype(ml_dtypes.float8_e4m3fn).view(np.uint8)
    else:
        c = by_word.astype(ml_dtypes.float4_e2m1fn).view(np.uint8) & 0xF
        words = (c[..., 0::2] | (c[..., 1::2] << 4)).reshape(k // 512, 128, 2 * n)
    return np.ascontiguousarray(words), np.ascontiguousarray(byte.astype(np.uint8).reshape(k // 512, 16, n))


def unpack_weight(words, scales, fmt):
    g, _, n = scales.shape
    words = np.ascontiguousarray(words).reshape(g, 128, n, -1)
    if fmt == "e4m3":
        vals = words.view(ml_dtypes.float8_e4m3fn).astype(np.float64)
    else:
        nib = np.empty((g, 128, n, 4), np.uint8)
        nib[..., 0::2] = words & 0xF
        nib[..., 1::2] = words >> 4
        vals = E2M1[nib]
    vals = vals * np.repeat(np.exp2(scales.astype(np.float64) - 127.0), 8, axis=1)[..., None]
    return vals.transpose(0, 1, 3, 2).reshape(g * 512, n)


def gelu(v):
    return 0.5 * v * (1.0 + np.tanh(np.sqrt(2.0 / np.pi) * (v + 0.044715 * v**3)))


def bf(x):
    return np.asarray(x, np.float32).astype(ml_dtypes.bfloat16)


def planes(Y):
    n, m = Y.shape
    b = f64(bf(Y)).reshape(n // 32, 32, m)
    amax = np.abs(b).max(1)
    byte = np.clip(np.where(amax > 0, np.frexp(amax)[1] - 1 + 127 - 7, 1), 1, 254)
    codes = (b * np.exp2(127.0 - byte)[:, None, :]).reshape(n, m).astype(np.float32).astype(ml_dtypes.float8_e4m3fn).view(np.uint8)
    words = codes.reshape(n // 512, 128, 4, m).transpose(0, 1, 3, 2)
    return np.ascontiguousarray(words), np.ascontiguousarray(byte.astype(np.uint8).reshape(n // 512, 16, m))


K, T, S, T2, P, H, N = 512, 4096, 1024, 2048, 512, 1024, 512

def setup_inputs():
    n = np.random.standard_normal
    s = mx_kscale(K)[:, None]
    u = mx_kscale(H)[:, None]
    size = np.exp(0.8 * n(N))[None, :]
    tab_words, tab_scales = pack_weight(n((K, T)) * s, "e4m3")
    w2_words, w2_scales = pack_weight(n((K, H)) / np.sqrt(K) / s * u.T, "e4m3")
    w3_words, w3_scales = pack_weight(n((K, H)) / np.sqrt(K) / s * u.T, "e2m1")
    w5_words, w5_scales = pack_weight(0.7 * n((H, N)) / np.sqrt(H) / u * size, "e2m1")
    return {
        "tab_words": tab_words, "tab_scales": tab_scales,
        "offs": striped(np.random.permutation(T)[:S]),
        "w1": (n((K, H)) / np.sqrt(K) / s * u.T).astype(np.float32),
        "w2_words": w2_words, "w2_scales": w2_scales,
        "w3_words": w3_words, "w3_scales": w3_scales,
        "offs2": striped(np.random.permutation(T2)[:S]),
        "wgs": np.exp(0.3 * n((128, S))).astype(np.float32),
        "offs3": striped(np.random.permutation(T2)[:P]),
        "offs4": striped(np.random.permutation(T2)[:P]),
        "hiatus": (n((H, P)) * u).astype(np.float32),
        "w4": (0.6 * n((H, N)) / np.sqrt(H) / u).astype(np.float32),
        "w5_words": w5_words, "w5_scales": w5_scales,
        "w6": (n((H, N)) / np.sqrt(H) / u * size).astype(np.float32),
    }

def reference(tab_words, tab_scales, offs, w1, w2_words, w2_scales, w3_words, w3_scales, offs2, wgs, offs3, offs4, hiatus, w4, w5_words, w5_scales, w6):
    v = unpack_weight(tab_words, tab_scales, "e4m3")[:, unstriped(offs)]
    d1 = mxq(f64(w1), 0, "e4m3").T @ v
    d2 = unpack_weight(w2_words, w2_scales, "e4m3").T @ v
    d3 = unpack_weight(w3_words, w3_scales, "e2m1").T @ v
    h = np.maximum(d1, d2) - d3
    page = np.zeros((H, T2))
    page[:, unstriped(offs2)] = np.tile(f64(wgs), (H // 128, 1)) * h
    g = f64(hiatus)
    z = page[:, unstriped(offs3)] - page[:, unstriped(offs4)] + g
    zq = mxq(z, 0, "e4m3")
    a = mxq(f64(w4), 0, "e4m3").T @ zq
    b = unpack_weight(w5_words, w5_scales, "e2m1").T @ zq + mxq(f64(w6), 0, "e4m3").T @ mxq(g, 0, "e4m3")
    y = np.tanh(a) * b
    words, scales = planes(y)
    return y, words, scales

@@ -1,0 +1,349 @@
+from contextlib import ExitStack
+
+import concourse.mybir as mybir
+from concourse.masks import make_identity
+
+K, T, S, T2, M, H, N = 512, 4096, 1024, 2048, 512, 1024, 512
+FLOPS = 2 * (3 * K * H * S + 3 * H * N * M)
+
+F32 = mybir.dt.float32
+BF16 = mybir.dt.bfloat16
+I32 = mybir.dt.int32
+U32 = mybir.dt.uint32
+U16 = mybir.dt.uint16
+U8 = mybir.dt.uint8
+FP8X4 = mybir.dt.float8_e4m3fn_x4
+FP4X4 = mybir.dt.float4_e2m1fn_x4
+ALU = mybir.AluOpType
+ACT = mybir.ActivationFunctionType
+
+P = 128
+HALF = 512
+W1_WIDTHS = (256, 256, 512)
+
+
+def tile_list_strata_contacts_kernel(
+    tc, tab_words, tab_scales, offs, w1, w2_words, w2_scales, w3_words, w3_scales, offs2, wgs,
+    offs3, offs4, hiatus, w4, w5_words, w5_scales, w6, out_0, out_1, out_2,
+):
+    nc = tc.nc
+    with ExitStack() as ctx:
+        keep = ctx.enter_context(tc.tile_pool(name="keep", bufs=1))
+        shared = ctx.enter_context(tc.tile_pool(name="shared", bufs=1))
+        bfp = ctx.enter_context(tc.tile_pool(name="bfp", bufs=3))
+        ring = ctx.enter_context(tc.tile_pool(name="ring", bufs=3))
+        psum = ctx.enter_context(tc.psum_pool(name="psum", bufs=1))
+
+        def held(name, shape, dtype):
+            return keep.tile(shape, dtype, name=name, align_bytes=64)
+
+        def bank(tag):
+            return psum.tile([P, 512], F32, name=tag)
+
+        def load_scale_rows(queue, plane, rows):
+            for q in range(4):
+                queue.dma_start(out=plane[32 * q : 32 * q + 4].bitcast(I32), in_=rows[4 * q : 4 * q + 4].bitcast(I32))
+
+        list1 = held("list1", [P, S // 16], U16)
+        list2 = held("list2", [P, S // 16], U16)
+        list3 = held("list3", [P, M // 16], U16)
+        list4 = held("list4", [P, M // 16], U16)
+        tab_w = shared.tile([P, T], I32, name="tab_w", offset=0)
+        tab_s = shared.tile([P, T], U8, name="tab_s", offset=4 * T)
+        w23_s = held("w23_s", [P, 2 * H], U8)
+        w2_s = w23_s[:, 0:H]
+        w3_s = w23_s[:, H : 2 * H]
+        pages = [held(f"page{i}", [P, T2], F32) for i in range(2)]
+        ident = held("ident", [P, P], F32)
+        warm = held("warm", [P, 2], F32)
+
+        nc.gpsimd.memset(tab_s[:].bitcast(I32)[:, 0:704], 0)
+        nc.vector.memset(tab_s[:].bitcast(I32)[:, 704:1024], 0)
+        load_scale_rows(nc.sync, tab_s, tab_scales[0])
+        nc.vector.memset(w23_s[:].bitcast(I32), 0)
+        nc.vector.memset(warm[:], 0.0)
+        nc.scalar.activation(out=warm[:, 1:2], in_=warm[:, 0:1], func=ACT.Tanh)
+        make_identity(nc, ident[:])
+        for page in pages:
+            nc.vector.memset(page[:], 0.0)
+
+        nc.sync.dma_start(list1[:], offs)
+        staged_loads = []
+
+        def staging(shape, dtype):
+            slot = len(staged_loads) % 2
+            staged_loads.append(slot)
+            return shared.tile(shape, dtype, name=f"staging{slot}", offset=2 * T * slot)
+
+        def load_rows(rows, raw):
+            nc.sync.dma_start(out=raw[:], in_=rows.rearrange("(p j) w -> p j w", j=4))
+            return raw
+
+        def round_and_quantize(raw, name, dealt):
+            width = raw.shape[2]
+            grouped = bfp.tile([P, 4 * width], BF16, name="grouped", align_bytes=64)
+            if dealt:
+                dst = grouped[:].rearrange("p (t m j) -> p m j t", t=4, j=4)
+                src = raw[:].rearrange("p j (m t) -> p m j t", t=4)
+            else:
+                dst = grouped[:].rearrange("p (c i j) -> p c j i", i=4, j=4)
+                src = raw[:].rearrange("p j (c i) -> p c j i", i=4)
+            for c0 in range(0, width // 4, 64):
+                c1 = min(c0 + 64, width // 4)
+                nc.scalar.copy(out=dst[:, c0:c1], in_=src[:, c0:c1])
+            codes = held(name + "_c", [P, width], U32)
+            scales = held(name + "_s", [P, width], U8)
+            nc.vector.quantize_mx(out=codes[:].bitcast(FP8X4), scales=scales[:], in_=grouped[:])
+            return codes, scales
+
+        w1_starts = [sum(W1_WIDTHS[:i]) for i in range(len(W1_WIDTHS))]
+        w1_raw = {0: load_rows(w1[:, 0 : W1_WIDTHS[0]], held("w1_first", [P, 4, W1_WIDTHS[0]], F32))}
+        w3_w = held("w3_w", [P, 2 * H], U8)
+        nc.sync.dma_start(out=w3_w[:].bitcast(I32), in_=w3_words[0].bitcast(I32))
+        nc.sync.dma_start(out=tab_w[:], in_=tab_words[0].rearrange("p t i -> p (t i)").bitcast(I32))
+        load_scale_rows(nc.sync, w3_s, w3_scales[0])
+        w2_w = held("w2_w", [P, H], I32)
+        nc.sync.dma_start(out=w2_w[:], in_=w2_words[0].rearrange("p c i -> p (c i)").bitcast(I32))
+        load_scale_rows(nc.sync, w2_s, w2_scales[0])
+        nc.sync.dma_start(list2[:], offs2)
+        wgs_sb = held("wgs_sb", [P, S], F32)
+        nc.sync.dma_start(out=wgs_sb[:], in_=wgs)
+        nc.sync.dma_start(list3[:], offs3)
+        nc.sync.dma_start(list4[:], offs4)
+
+        v_s = [held(f"v_s{hf}", [P, HALF], U8) for hf in range(2)]
+        v_w = [held(f"v_w{hf}", [P, HALF], U32) for hf in range(2)]
+        nc.vector.tensor_copy(out=v_s[0][:], in_=tab_s[:].indirect(list1[:, 0:32]))
+        w1_q = {0: round_and_quantize(w1_raw[0], "w1q0", False)}
+        nc.vector.tensor_copy(out=v_w[0][:], in_=tab_w[:].bitcast(U32).indirect(list1[:, 0:32]))
+        nc.vector.tensor_copy(out=v_s[1][:], in_=tab_s[:].indirect(list1[:, 32:64]))
+        nc.vector.tensor_copy(out=v_w[1][:], in_=tab_w[:].bitcast(U32).indirect(list1[:, 32:64]))
+
+        w5_wd = held("w5_wd", [P, 2, 2 * N], U8)
+        w5_sd = held("w5_sd", [P, 2, N], U8)
+
+        def deal_w5():
+            both = staging([P, 6 * N], U8)
+            w5_w = both[:, 0 : 4 * N].rearrange("p (a c) -> p a c", a=2)
+            w5_s = both[:, 4 * N : 6 * N].rearrange("p (a c) -> p a c", a=2)
+            nc.vector.memset(both[:, 4 * N : 6 * N].bitcast(I32), 0)
+            load_scale_rows(nc.sync, w5_s, w5_scales.rearrange("a q c -> q a c"))
+            nc.sync.dma_start(out=w5_w[:].bitcast(I32), in_=w5_words.rearrange("a p c -> p a c").bitcast(I32))
+            nc.vector.tensor_copy(
+                out=w5_wd[:].bitcast(U16).rearrange("p a (t m) -> p a t m", t=4),
+                in_=w5_w[:].bitcast(U16).rearrange("p a (m t) -> p a t m", t=4),
+            )
+            nc.vector.tensor_copy(
+                out=w5_sd[:].rearrange("p a (t m) -> p a t m", t=4),
+                in_=w5_s[:].rearrange("p a (m t) -> p a t m", t=4),
+            )
+
+        hi_rows = {}
+        quant = {}
+
+        def w1_piece(i):
+            raw = load_rows(w1[:, w1_starts[i] : w1_starts[i] + W1_WIDTHS[i]], staging([P, 4, W1_WIDTHS[i]], F32))
+            w1_q[i] = round_and_quantize(raw, f"w1q{i}", False)
+
+        def stage2_operand(name, src, a, dealt):
+            raw = load_rows(src[512 * a : 512 * (a + 1), :], staging([P, 4, 512], F32))
+            quant[name, a] = round_and_quantize(raw, f"{name}{a}", dealt)
+
+        def load_hi(b):
+            hi_rows[b] = shared.tile([P, M], F32, name=f"hi_rows{b % 2}", offset=4 * T + 4 * M * (b % 2))
+            nc.sync.dma_start(out=hi_rows[b][:], in_=hiatus[P * b : P * (b + 1), :])
+
+        staged = {}
+
+        def product(u, tag, words, scales):
+            hf = u % 2
+            acc = bank(tag)
+            for c in range(4):
+                nc.tensor.matmul_mx(
+                    out=acc[:, P * c : P * (c + 1)],
+                    lhsT=v_w[hf][:, P * c : P * (c + 1)].bitcast(FP8X4),
+                    lhsT_scale=v_s[hf][:, P * c : P * (c + 1)],
+                    rhs=words, rhs_scale=scales, start=True, stop=True,
+                )
+            return acc
+
+        def products_d1_d3(u):
+            b = u // 2
+            i = max(x for x in range(len(W1_WIDTHS)) if w1_starts[x] <= P * b)
+            w1_cols = slice(P * b - w1_starts[i], P * (b + 1) - w1_starts[i])
+            d1 = product(u, "d1", w1_q[i][0][:, w1_cols].bitcast(FP8X4), w1_q[i][1][:, w1_cols])
+            d3 = product(u, "d3", w3_w[:, 2 * P * b : 2 * P * (b + 1)].bitcast(FP4X4), w3_s[:, P * b : P * (b + 1)])
+            d1_sb = ring.tile([P, 512], F32, name="d1_sb")
+            nc.scalar.copy(out=d1_sb[:], in_=d1[:])
+            minus_d3 = ring.tile([P, 512], F32, name="minus_d3")
+            nc.scalar.activation(out=minus_d3[:], in_=d3[:], func=ACT.Copy, scale=-1.0)
+            staged[u] = (d1_sb, minus_d3)
+
+        def larger_of_d1_d2(u):
+            cols = slice(P * (u // 2), P * (u // 2 + 1))
+            d2 = product(u, "d2", w2_w[:, cols].bitcast(FP8X4), w2_s[:, cols])
+            d1_sb, minus_d3 = staged[u]
+            if u < 2:
+                larger = staging([P, 512], F32)
+            else:
+                larger = ring.tile([P, 512], F32, name="larger")
+            nc.vector.tensor_tensor(out=larger[:], in0=d2[:], in1=d1_sb[:], op=ALU.max)
+            staged[u] = (minus_d3, larger)
+
+        def transposed_sum(acc, terms):
+            chunks = terms[0].shape[1] // P
+            for n, term in enumerate(terms):
+                for c in range(chunks):
+                    nc.tensor.matmul(
+                        acc[:, P * c : P * (c + 1)], term[:, P * c : P * (c + 1)], ident[:], is_transpose=True,
+                        start=(n == 0 and c == 0), stop=(n == len(terms) - 1 and c == chunks - 1),
+                    )
+
+        def turn_h(u):
+            h_ps = bank("h")
+            transposed_sum(h_ps, staged[u])
+            h_sb = ring.tile([P, HALF], F32, name="h_sb")
+            nc.scalar.copy(out=h_sb[:], in_=h_ps[:])
+            staged[u] = h_sb
+
+        def put_in_page(u):
+            b, hf = divmod(u, 2)
+            nc.vector.tensor_tensor(
+                out=pages[b % 2][:].indirect(list2[:, 32 * hf : 32 * (hf + 1)]),
+                in0=staged[u][:], in1=wgs_sb[:, HALF * hf : HALF * (hf + 1)], op=ALU.mult,
+            )
+
+        z_pairs = [[held(f"z_pairs{a}{hf}", [P, 2, 2, 2 * P], BF16) for hf in range(2)] for a in range(2)]
+
+        def fetch(b, parts):
+            page = pages[b % 2]
+            minus_below = ring.tile([P, M], F32, name="minus_below")
+            nc.vector.tensor_scalar(
+                out=minus_below[:], in0=page[:].indirect(list4[:]),
+                scalar1=-1.0, scalar2=0.0, op0=ALU.mult, op1=ALU.add,
+            )
+            width = M // parts
+            a, q = divmod(b, 4)
+            for part in range(parts):
+                cols = slice(width * part, width * (part + 1))
+                above = ring.tile([P, width], F32, name="above")
+                nc.vector.tensor_copy(out=above[:], in_=page[:].indirect(list3[:, width * part // 16 : width * (part + 1) // 16]))
+                z_ps = bank(f"z{part}")
+                transposed_sum(z_ps, (hi_rows[b][:, cols], minus_below[:, cols], above[:]))
+                for x in range(width // 256):
+                    nc.scalar.copy(
+                        out=z_pairs[a][part + x][:, :, :, 64 * q : 64 * (q + 1)].rearrange("m c u (p e) -> m c u p e", e=2),
+                        in_=z_ps[:, 256 * x : 256 * (x + 1)].rearrange("m (c p u e) -> m c u p e", c=2, u=2, e=2),
+                    )
+
+        def quantize_z(a, hf):
+            grouped = held(f"z_grouped{a}{hf}", [P, 4 * 256], BF16)
+            words = z_pairs[a][hf][:].bitcast(F32)
+            back = bank(f"back{hf}")
+            for c in range(2):
+                for u in range(2):
+                    col = P * (2 * c + u)
+                    nc.tensor.transpose(back[:, col : col + P], words[:, c, u, :], ident[:])
+            nc.scalar.copy(
+                out=grouped[:].bitcast(F32).rearrange("p (c m u) -> p c m u", c=2, u=2),
+                in_=back[:].rearrange("p (c u m) -> p c m u", c=2, u=2),
+            )
+            codes = held(f"z_c{a}{hf}", [P, 256], U32)
+            scales = held(f"z_s{a}{hf}", [P, 256], U8)
+            nc.vector.quantize_mx(out=codes[:].bitcast(FP8X4), scales=scales[:], in_=grouped[:])
+            quant["z", a, hf] = (codes, scales)
+
+        side_work = [
+            lambda: w1_piece(1),
+            lambda: w1_piece(2),
+            deal_w5,
+            lambda: stage2_operand("g", hiatus, 0, False),
+            lambda: stage2_operand("g", hiatus, 1, False),
+            lambda: stage2_operand("w6", w6, 0, True),
+            lambda: stage2_operand("w6", w6, 1, True),
+            lambda: stage2_operand("w4", w4, 0, True),
+            lambda: stage2_operand("w4", w4, 1, True),
+        ]
+
+        units = 16
+        products_d1_d3(0)
+        larger_of_d1_d2(0)
+        for u in range(units):
+            if u + 1 < units:
+                products_d1_d3(u + 1)
+                larger_of_d1_d2(u + 1)
+            turn_h(u)
+            if u % 2 == 0 and u > 0:
+                fetch(u // 2 - 1, 1)
+                if u == 8:
+                    quantize_z(0, 0)
+                    quantize_z(0, 1)
+            put_in_page(u)
+            if u % 2 == 1:
+                load_hi(u // 2)
+            if 1 <= u <= len(side_work):
+                side_work[u - 1]()
+
+        def mx_passes(acc, name, a, pair, hf, start, stop):
+            step = P if name == "w5" else 256
+            todo = [(x, m0) for x in range(2) for m0 in range(0, 256, step)]
+            for n, (x, m0) in enumerate(todo):
+                t = 2 * pair + x
+                cols = slice(P * t, P * (t + 1))
+                if name == "w5":
+                    lhsT = w5_wd[:, a, 2 * P * t : 2 * P * (t + 1)].bitcast(FP4X4)
+                    lhsT_scale = w5_sd[:, a, cols]
+                else:
+                    lhsT = quant[name, a][0][:, cols].bitcast(FP8X4)
+                    lhsT_scale = quant[name, a][1][:, cols]
+                if name == "w6":
+                    codes, scales = quant["g", a]
+                    m_cols = slice(256 * hf + m0, 256 * hf + m0 + step)
+                else:
+                    codes, scales = quant["z", a, hf]
+                    m_cols = slice(m0, m0 + step)
+                nc.tensor.matmul_mx(
+                    out=acc[:, 256 * x + m0 : 256 * x + m0 + step], lhsT=lhsT, lhsT_scale=lhsT_scale,
+                    rhs=codes[:, m_cols].bitcast(FP8X4), rhs_scale=scales[:, m_cols],
+                    start=(start and n == 0), stop=(stop and n == len(todo) - 1),
+                )
+
+        quarters = [(hf, pair) for hf in range(2) for pair in range(2)]
+        sums = {}
+        for (hf, pair), tag in zip(quarters, ("d1", "d2", "d3", "h")):
+            sums[hf, pair] = bank(tag)
+            mx_passes(sums[hf, pair], "w6", 0, pair, hf, True, False)
+            mx_passes(sums[hf, pair], "w6", 1, pair, hf, False, False)
+            mx_passes(sums[hf, pair], "w5", 0, pair, hf, False, False)
+        fetch(7, 2)
+        quantize_z(1, 0)
+        quantize_z(1, 1)
+        out_rows = out_0.rearrange("(p t) m -> p t m", t=4)
+        out_words = out_1[0].rearrange("p m t -> p (m t)").bitcast(I32)
+        y = [held(f"y{hf}", [P, 4, 256], F32) for hf in range(2)]
+        for (hf, pair), tag in zip(quarters, ("z0", "z1", "back0", "back1")):
+            gates = bank(tag)
+            mx_passes(gates, "w4", 0, pair, hf, True, False)
+            mx_passes(gates, "w4", 1, pair, hf, False, True)
+            mx_passes(sums[hf, pair], "w5", 1, pair, hf, False, True)
+            gate = ring.tile([P, 512], F32, name="gate")
+            nc.scalar.activation(out=gate[:], in_=gates[:], func=ACT.Tanh)
+            y_part = y[hf][:, 2 * pair : 2 * pair + 2, :]
+            nc.vector.tensor_tensor(
+                out=y_part.rearrange("p t m -> p (t m)"), in0=sums[hf, pair][:], in1=gate[:], op=ALU.mult
+            )
+            nc.sync.dma_start(out=out_rows[:, 2 * pair : 2 * pair + 2, 256 * hf : 256 * (hf + 1)], in_=y_part)
+        y_c = held("y_c", [P, M], U32)
+        y_s = held("y_s", [P, M], U8)
+        for hf, copy in enumerate((nc.scalar.copy, nc.vector.tensor_copy)):
+            cols = slice(256 * hf, 256 * (hf + 1))
+            y_grouped = held(f"y_grouped{hf}", [P, 4 * 256], BF16)
+            copy(
+                out=y_grouped[:].rearrange("p (c i t) -> p c t i", i=4, t=4),
+                in_=y[hf][:].rearrange("p t (c i) -> p c t i", i=4),
+            )
+            nc.vector.quantize_mx(out=y_c[:, cols].bitcast(FP8X4), scales=y_s[:, cols], in_=y_grouped[:])
+            nc.sync.dma_start(out=out_words[:, cols], in_=y_c[:, cols].bitcast(I32))
+        for q in range(4):
+            queue = (nc.scalar, nc.sync)[q % 2]
+            queue.dma_start(out=out_2[0][4 * q : 4 * q + 4].bitcast(I32), in_=y_s[32 * q : 32 * q + 4].bitcast(I32))

@@ -19,7 +19,7 @@ ACT = mybir.ActivationFunctionType
 
 P = 128
 HALF = 512
-W1_WIDTHS = (256, 256, 512)
+W1_WIDTHS = (128, 128, 256, 512)
 
 
 def tile_list_strata_contacts_kernel(
@@ -53,19 +53,20 @@ def tile_list_strata_contacts_kernel(
         w23_s = held("w23_s", [P, 2 * H], U8)
         w2_s = w23_s[:, 0:H]
         w3_s = w23_s[:, H : 2 * H]
+        w5_s = held("w5_s", [P, 2, N], U8)
         pages = [held(f"page{i}", [P, T2], F32) for i in range(2)]
         ident = held("ident", [P, P], F32)
         warm = held("warm", [P, 2], F32)
 
         nc.gpsimd.memset(tab_s[:].bitcast(I32)[:, 0:704], 0)
         nc.vector.memset(tab_s[:].bitcast(I32)[:, 704:1024], 0)
-        load_scale_rows(nc.sync, tab_s, tab_scales[0])
         nc.vector.memset(w23_s[:].bitcast(I32), 0)
+        nc.vector.memset(w5_s[:].bitcast(I32), 0)
         nc.vector.memset(warm[:], 0.0)
         nc.scalar.activation(out=warm[:, 1:2], in_=warm[:, 0:1], func=ACT.Tanh)
         make_identity(nc, ident[:])
-        for page in pages:
-            nc.vector.memset(page[:], 0.0)
+        nc.vector.memset(pages[0][:], 0.0)
+        nc.gpsimd.memset(pages[1][:], 0.0)
 
         nc.sync.dma_start(list1[:], offs)
         staged_loads = []
@@ -83,8 +84,8 @@ def tile_list_strata_contacts_kernel(
             width = raw.shape[2]
             grouped = bfp.tile([P, 4 * width], BF16, name="grouped", align_bytes=64)
             if dealt:
-                dst = grouped[:].rearrange("p (t m j) -> p m j t", t=4, j=4)
-                src = raw[:].rearrange("p j (m t) -> p m j t", t=4)
+                dst = grouped[:].rearrange("p (t m j) -> p m t j", t=4, j=4)
+                src = raw[:].rearrange("p j (m t) -> p m t j", t=4)
             else:
                 dst = grouped[:].rearrange("p (c i j) -> p c j i", i=4, j=4)
                 src = raw[:].rearrange("p j (c i) -> p c j i", i=4)
@@ -97,17 +98,24 @@ def tile_list_strata_contacts_kernel(
             return codes, scales
 
         w1_starts = [sum(W1_WIDTHS[:i]) for i in range(len(W1_WIDTHS))]
-        w1_raw = {0: load_rows(w1[:, 0 : W1_WIDTHS[0]], held("w1_first", [P, 4, W1_WIDTHS[0]], F32))}
-        w3_w = held("w3_w", [P, 2 * H], U8)
-        nc.sync.dma_start(out=w3_w[:].bitcast(I32), in_=w3_words[0].bitcast(I32))
-        nc.sync.dma_start(out=tab_w[:], in_=tab_words[0].rearrange("p t i -> p (t i)").bitcast(I32))
-        load_scale_rows(nc.sync, w3_s, w3_scales[0])
+        tab_w_dram = tab_words[0].rearrange("p t i -> p (t i)").bitcast(I32)
+        nc.sync.dma_start(out=tab_w[:, 0 : T // 2], in_=tab_w_dram[:, 0 : T // 2])
+        load_scale_rows(nc.sync, tab_s, tab_scales[0])
+        w1_raw = {0: load_rows(w1[:, 0:128], held("w1_first", [P, 4, 128], F32))}
+        nc.sync.dma_start(out=tab_w[:, T // 2 : T], in_=tab_w_dram[:, T // 2 : T])
         w2_w = held("w2_w", [P, H], I32)
         nc.sync.dma_start(out=w2_w[:], in_=w2_words[0].rearrange("p c i -> p (c i)").bitcast(I32))
         load_scale_rows(nc.sync, w2_s, w2_scales[0])
+        w3_w = held("w3_w", [P, 2 * H], U8)
+        nc.sync.dma_start(out=w3_w[:].bitcast(I32), in_=w3_words[0].bitcast(I32))
+        load_scale_rows(nc.sync, w3_s, w3_scales[0])
+        w1_raw[1] = load_rows(w1[:, 128:256], held("w1_second", [P, 4, 128], F32))
+        w5_w = held("w5_w", [P, 2, 2 * N], U8)
+        nc.sync.dma_start(out=w5_w[:].bitcast(I32), in_=w5_words.rearrange("a p c -> p a c").bitcast(I32))
         nc.sync.dma_start(list2[:], offs2)
         wgs_sb = held("wgs_sb", [P, S], F32)
         nc.sync.dma_start(out=wgs_sb[:], in_=wgs)
+        load_scale_rows(nc.sync, w5_s, w5_scales.rearrange("a q c -> q a c"))
         nc.sync.dma_start(list3[:], offs3)
         nc.sync.dma_start(list4[:], offs4)
 
@@ -119,24 +127,21 @@ def tile_list_strata_contacts_kernel(
         nc.vector.tensor_copy(out=v_s[1][:], in_=tab_s[:].indirect(list1[:, 32:64]))
         nc.vector.tensor_copy(out=v_w[1][:], in_=tab_w[:].bitcast(U32).indirect(list1[:, 32:64]))
 
-        w5_wd = held("w5_wd", [P, 2, 2 * N], U8)
-        w5_sd = held("w5_sd", [P, 2, N], U8)
-
-        def deal_w5():
-            both = staging([P, 6 * N], U8)
-            w5_w = both[:, 0 : 4 * N].rearrange("p (a c) -> p a c", a=2)
-            w5_s = both[:, 4 * N : 6 * N].rearrange("p (a c) -> p a c", a=2)
-            nc.vector.memset(both[:, 4 * N : 6 * N].bitcast(I32), 0)
-            load_scale_rows(nc.sync, w5_s, w5_scales.rearrange("a q c -> q a c"))
-            nc.sync.dma_start(out=w5_w[:].bitcast(I32), in_=w5_words.rearrange("a p c -> p a c").bitcast(I32))
+        def deal_w5_words():
+            dealt = held("first_d1_0", [P, 2, 2 * N], U8)
             nc.vector.tensor_copy(
-                out=w5_wd[:].bitcast(U16).rearrange("p a (t m) -> p a t m", t=4),
+                out=dealt[:].bitcast(U16).rearrange("p a (t m) -> p a t m", t=4),
                 in_=w5_w[:].bitcast(U16).rearrange("p a (m t) -> p a t m", t=4),
             )
+            return dealt
+
+        def deal_w5_scales():
+            dealt = held("first_d1_1", [P, 2, N], U8)
             nc.vector.tensor_copy(
-                out=w5_sd[:].rearrange("p a (t m) -> p a t m", t=4),
+                out=dealt[:].rearrange("p a (t m) -> p a t m", t=4),
                 in_=w5_s[:].rearrange("p a (m t) -> p a t m", t=4),
             )
+            return dealt
 
         hi_rows = {}
         quant = {}
@@ -167,28 +172,29 @@ def tile_list_strata_contacts_kernel(
                 )
             return acc
 
-        def products_d1_d3(u):
+        def larger_of_d1_d2(u):
             b = u // 2
             i = max(x for x in range(len(W1_WIDTHS)) if w1_starts[x] <= P * b)
             w1_cols = slice(P * b - w1_starts[i], P * (b + 1) - w1_starts[i])
+            cols = slice(P * b, P * (b + 1))
             d1 = product(u, "d1", w1_q[i][0][:, w1_cols].bitcast(FP8X4), w1_q[i][1][:, w1_cols])
-            d3 = product(u, "d3", w3_w[:, 2 * P * b : 2 * P * (b + 1)].bitcast(FP4X4), w3_s[:, P * b : P * (b + 1)])
-            d1_sb = ring.tile([P, 512], F32, name="d1_sb")
-            nc.scalar.copy(out=d1_sb[:], in_=d1[:])
-            minus_d3 = ring.tile([P, 512], F32, name="minus_d3")
-            nc.scalar.activation(out=minus_d3[:], in_=d3[:], func=ACT.Copy, scale=-1.0)
-            staged[u] = (d1_sb, minus_d3)
-
-        def larger_of_d1_d2(u):
-            cols = slice(P * (u // 2), P * (u // 2 + 1))
-            d2 = product(u, "d2", w2_w[:, cols].bitcast(FP8X4), w2_s[:, cols])
-            d1_sb, minus_d3 = staged[u]
+            d2 = product(u, ("d2", "z1")[u % 2], w2_w[:, cols].bitcast(FP8X4), w2_s[:, cols])
             if u < 2:
+                d1_sb = held(f"first_d1_{u}", [P, 512], F32)
                 larger = staging([P, 512], F32)
             else:
+                d1_sb = ring.tile([P, 512], F32, name="d1_sb")
                 larger = ring.tile([P, 512], F32, name="larger")
+            nc.scalar.copy(out=d1_sb[:], in_=d1[:])
             nc.vector.tensor_tensor(out=larger[:], in0=d2[:], in1=d1_sb[:], op=ALU.max)
-            staged[u] = (minus_d3, larger)
+            staged[u] = larger
+
+        def negated_d3(u):
+            b = u // 2
+            d3 = product(u, "d3", w3_w[:, 2 * P * b : 2 * P * (b + 1)].bitcast(FP4X4), w3_s[:, P * b : P * (b + 1)])
+            minus_d3 = ring.tile([P, 512], F32, name="minus_d3")
+            nc.scalar.activation(out=minus_d3[:], in_=d3[:], func=ACT.Copy, scale=-1.0)
+            staged[u] = (minus_d3, staged[u])
 
         def transposed_sum(acc, terms):
             chunks = terms[0].shape[1] // P
@@ -254,9 +260,8 @@ def tile_list_strata_contacts_kernel(
             quant["z", a, hf] = (codes, scales)
 
         side_work = [
-            lambda: w1_piece(1),
             lambda: w1_piece(2),
-            deal_w5,
+            lambda: w1_piece(3),
             lambda: stage2_operand("g", hiatus, 0, False),
             lambda: stage2_operand("g", hiatus, 1, False),
             lambda: stage2_operand("w6", w6, 0, True),
@@ -266,13 +271,19 @@ def tile_list_strata_contacts_kernel(
         ]
 
         units = 16
-        products_d1_d3(0)
         larger_of_d1_d2(0)
+        negated_d3(0)
+        w5_wd = deal_w5_words()
         for u in range(units):
             if u + 1 < units:
-                products_d1_d3(u + 1)
                 larger_of_d1_d2(u + 1)
+            if u == 0:
+                w5_sd = deal_w5_scales()
             turn_h(u)
+            if u == 0:
+                w1_q[1] = round_and_quantize(w1_raw[1], "w1q1", False)
+            if u + 1 < units:
+                negated_d3(u + 1)
             if u % 2 == 0 and u > 0:
                 fetch(u // 2 - 1, 1)
                 if u == 8:

@@ -80,7 +80,7 @@ def tile_list_strata_contacts_kernel(
             nc.sync.dma_start(out=raw[:], in_=rows.rearrange("(p j) w -> p j w", j=4))
             return raw
 
-        def round_and_quantize(raw, name, dealt):
+        def round_and_quantize(raw, name, dealt, negated=False):
             width = raw.shape[2]
             grouped = bfp.tile([P, 4 * width], BF16, name="grouped", align_bytes=64)
             if dealt:
@@ -91,7 +91,10 @@ def tile_list_strata_contacts_kernel(
                 src = raw[:].rearrange("p j (c i) -> p c j i", i=4)
             for c0 in range(0, width // 4, 64):
                 c1 = min(c0 + 64, width // 4)
-                nc.scalar.copy(out=dst[:, c0:c1], in_=src[:, c0:c1])
+                if negated:
+                    nc.scalar.activation(out=dst[:, c0:c1], in_=src[:, c0:c1], func=ACT.Copy, scale=-1.0)
+                else:
+                    nc.scalar.copy(out=dst[:, c0:c1], in_=src[:, c0:c1])
             codes = held(name + "_c", [P, width], U32)
             scales = held(name + "_s", [P, width], U8)
             nc.vector.quantize_mx(out=codes[:].bitcast(FP8X4), scales=scales[:], in_=grouped[:])
@@ -122,13 +125,13 @@ def tile_list_strata_contacts_kernel(
         v_s = [held(f"v_s{hf}", [P, HALF], U8) for hf in range(2)]
         v_w = [held(f"v_w{hf}", [P, HALF], U32) for hf in range(2)]
         nc.vector.tensor_copy(out=v_s[0][:], in_=tab_s[:].indirect(list1[:, 0:32]))
-        w1_q = {0: round_and_quantize(w1_raw[0], "w1q0", False)}
+        w1_q = {0: round_and_quantize(w1_raw[0], "w1q0", False, True)}
         nc.vector.tensor_copy(out=v_w[0][:], in_=tab_w[:].bitcast(U32).indirect(list1[:, 0:32]))
         nc.vector.tensor_copy(out=v_s[1][:], in_=tab_s[:].indirect(list1[:, 32:64]))
         nc.vector.tensor_copy(out=v_w[1][:], in_=tab_w[:].bitcast(U32).indirect(list1[:, 32:64]))
 
         def deal_w5_words():
-            dealt = held("first_d1_0", [P, 2, 2 * N], U8)
+            dealt = shared.tile([P, 2, 2 * N], U8, name="w5_dealt_words", offset=5 * T, align_bytes=64)
             nc.vector.tensor_copy(
                 out=dealt[:].bitcast(U16).rearrange("p a (t m) -> p a t m", t=4),
                 in_=w5_w[:].bitcast(U16).rearrange("p a (m t) -> p a t m", t=4),
@@ -136,7 +139,7 @@ def tile_list_strata_contacts_kernel(
             return dealt
 
         def deal_w5_scales():
-            dealt = held("first_d1_1", [P, 2, N], U8)
+            dealt = shared.tile([P, 2, N], U8, name="w5_dealt_scales", offset=5 * T + 4 * N, align_bytes=64)
             nc.vector.tensor_copy(
                 out=dealt[:].rearrange("p a (t m) -> p a t m", t=4),
                 in_=w5_s[:].rearrange("p a (m t) -> p a t m", t=4),
@@ -148,7 +151,7 @@ def tile_list_strata_contacts_kernel(
 
         def w1_piece(i):
             raw = load_rows(w1[:, w1_starts[i] : w1_starts[i] + W1_WIDTHS[i]], staging([P, 4, W1_WIDTHS[i]], F32))
-            w1_q[i] = round_and_quantize(raw, f"w1q{i}", False)
+            w1_q[i] = round_and_quantize(raw, f"w1q{i}", False, True)
 
         def stage2_operand(name, src, a, dealt):
             raw = load_rows(src[512 * a : 512 * (a + 1), :], staging([P, 4, 512], F32))
@@ -160,41 +163,51 @@ def tile_list_strata_contacts_kernel(
 
         staged = {}
 
-        def product(u, tag, words, scales):
-            hf = u % 2
-            acc = bank(tag)
-            for c in range(4):
-                nc.tensor.matmul_mx(
-                    out=acc[:, P * c : P * (c + 1)],
-                    lhsT=v_w[hf][:, P * c : P * (c + 1)].bitcast(FP8X4),
-                    lhsT_scale=v_s[hf][:, P * c : P * (c + 1)],
-                    rhs=words, rhs_scale=scales, start=True, stop=True,
-                )
-            return acc
-
-        def larger_of_d1_d2(u):
-            b = u // 2
+        def product(u, tag, names):
+            b, hf = divmod(u, 2)
             i = max(x for x in range(len(W1_WIDTHS)) if w1_starts[x] <= P * b)
             w1_cols = slice(P * b - w1_starts[i], P * (b + 1) - w1_starts[i])
             cols = slice(P * b, P * (b + 1))
-            d1 = product(u, "d1", w1_q[i][0][:, w1_cols].bitcast(FP8X4), w1_q[i][1][:, w1_cols])
-            d2 = product(u, ("d2", "z1")[u % 2], w2_w[:, cols].bitcast(FP8X4), w2_s[:, cols])
-            if u < 2:
-                d1_sb = held(f"first_d1_{u}", [P, 512], F32)
-                larger = staging([P, 512], F32)
-            else:
-                d1_sb = ring.tile([P, 512], F32, name="d1_sb")
-                larger = ring.tile([P, 512], F32, name="larger")
-            nc.scalar.copy(out=d1_sb[:], in_=d1[:])
-            nc.vector.tensor_tensor(out=larger[:], in0=d2[:], in1=d1_sb[:], op=ALU.max)
-            staged[u] = larger
+            moving = {
+                "minus_w1": (w1_q[i][0][:, w1_cols].bitcast(FP8X4), w1_q[i][1][:, w1_cols]),
+                "w2": (w2_w[:, cols].bitcast(FP8X4), w2_s[:, cols]),
+                "w3": (w3_w[:, 2 * P * b : 2 * P * (b + 1)].bitcast(FP4X4), w3_s[:, cols]),
+            }
+            acc = bank(tag)
+            for c in range(4):
+                for n, name in enumerate(names):
+                    nc.tensor.matmul_mx(
+                        out=acc[:, P * c : P * (c + 1)],
+                        lhsT=v_w[hf][:, P * c : P * (c + 1)].bitcast(FP8X4),
+                        lhsT_scale=v_s[hf][:, P * c : P * (c + 1)],
+                        rhs=moving[name][0], rhs_scale=moving[name][1],
+                        start=(n == 0), stop=(n == len(names) - 1),
+                    )
+            return acc
 
-        def negated_d3(u):
-            b = u // 2
-            d3 = product(u, "d3", w3_w[:, 2 * P * b : 2 * P * (b + 1)].bitcast(FP4X4), w3_s[:, P * b : P * (b + 1)])
-            minus_d3 = ring.tile([P, 512], F32, name="minus_d3")
-            nc.scalar.activation(out=minus_d3[:], in_=d3[:], func=ACT.Copy, scale=-1.0)
-            staged[u] = (minus_d3, staged[u])
+        def by_relu(u):
+            return u % 2 == 1 and u < 15
+
+        def first_term(u):
+            term = staging([P, 512], F32) if u < 2 else ring.tile([P, 512], F32, name="first_term")
+            if by_relu(u):
+                nc.scalar.activation(out=term[:], in_=product(u, "z1", ("w2", "minus_w1"))[:], func=ACT.Relu)
+            else:
+                minus_d1 = product(u, "d1", ("minus_w1",))
+                d2 = product(u, "d2", ("w2",))
+                if u == 0:
+                    d1_sb = shared.tile([P, 512], F32, name="first_d1", offset=5 * T + 2 * N)
+                else:
+                    d1_sb = ring.tile([P, 512], F32, name="d1_sb")
+                nc.scalar.activation(out=d1_sb[:], in_=minus_d1[:], func=ACT.Copy, scale=-1.0)
+                nc.vector.tensor_tensor(out=term[:], in0=d2[:], in1=d1_sb[:], op=ALU.max)
+            staged[u] = term
+
+        def second_term(u):
+            acc = product(u, "d3", ("w3", "minus_w1") if by_relu(u) else ("w3",))
+            term = ring.tile([P, 512], F32, name="second_term")
+            nc.scalar.activation(out=term[:], in_=acc[:], func=ACT.Copy, scale=-1.0)
+            staged[u] = (term, staged[u])
 
         def transposed_sum(acc, terms):
             chunks = terms[0].shape[1] // P
@@ -271,25 +284,24 @@ def tile_list_strata_contacts_kernel(
         ]
 
         units = 16
-        larger_of_d1_d2(0)
-        negated_d3(0)
+        first_term(0)
+        second_term(0)
         w5_wd = deal_w5_words()
+        w5_sd = deal_w5_scales()
         for u in range(units):
             if u + 1 < units:
-                larger_of_d1_d2(u + 1)
-            if u == 0:
-                w5_sd = deal_w5_scales()
+                first_term(u + 1)
             turn_h(u)
             if u == 0:
-                w1_q[1] = round_and_quantize(w1_raw[1], "w1q1", False)
+                w1_q[1] = round_and_quantize(w1_raw[1], "w1q1", False, True)
             if u + 1 < units:
-                negated_d3(u + 1)
+                second_term(u + 1)
+            put_in_page(u)
             if u % 2 == 0 and u > 0:
                 fetch(u // 2 - 1, 1)
                 if u == 8:
                     quantize_z(0, 0)
                     quantize_z(0, 1)
-            put_in_page(u)
             if u % 2 == 1:
                 load_hi(u // 2)
             if 1 <= u <= len(side_work):

@@ -54,7 +54,7 @@ def tile_list_strata_contacts_kernel(
         w2_s = w23_s[:, 0:H]
         w3_s = w23_s[:, H : 2 * H]
         w5_s = held("w5_s", [P, 2, N], U8)
-        pages = [held(f"page{i}", [P, T2], F32) for i in range(2)]
+        pages = [shared.tile([P, T2], F32, name=f"page{i}", offset=6 * T + 4 * T2 * i) for i in range(2)]
         ident = held("ident", [P, P], F32)
         warm = held("warm", [P, 2], F32)
 
@@ -81,6 +81,9 @@ def tile_list_strata_contacts_kernel(
             return raw
 
         def round_and_quantize(raw, name, dealt, negated=False):
+            return quantize(round_rows(raw, dealt, negated), name)
+
+        def round_rows(raw, dealt, negated=False):
             width = raw.shape[2]
             grouped = bfp.tile([P, 4 * width], BF16, name="grouped", align_bytes=64)
             if dealt:
@@ -95,7 +98,14 @@ def tile_list_strata_contacts_kernel(
                     nc.scalar.activation(out=dst[:, c0:c1], in_=src[:, c0:c1], func=ACT.Copy, scale=-1.0)
                 else:
                     nc.scalar.copy(out=dst[:, c0:c1], in_=src[:, c0:c1])
-            codes = held(name + "_c", [P, width], U32)
+            return grouped
+
+        def quantize(grouped, name, codes_offset=None):
+            width = grouped.shape[1] // 4
+            if codes_offset is None:
+                codes = held(name + "_c", [P, width], U32)
+            else:
+                codes = shared.tile([P, width], U32, name=name + "_c", offset=codes_offset, align_bytes=64)
             scales = held(name + "_s", [P, width], U8)
             nc.vector.quantize_mx(out=codes[:].bitcast(FP8X4), scales=scales[:], in_=grouped[:])
             return codes, scales
@@ -156,6 +166,10 @@ def tile_list_strata_contacts_kernel(
         def stage2_operand(name, src, a, dealt):
             raw = load_rows(src[512 * a : 512 * (a + 1), :], staging([P, 4, 512], F32))
             quant[name, a] = round_and_quantize(raw, f"{name}{a}", dealt)
+
+        def round_w4(a):
+            raw = load_rows(w4[512 * a : 512 * (a + 1), :], staging([P, 4, 512], F32))
+            quant["w4", a] = round_rows(raw, True)
 
         def load_hi(b):
             hi_rows[b] = shared.tile([P, M], F32, name=f"hi_rows{b % 2}", offset=4 * T + 4 * M * (b % 2))
@@ -237,10 +251,15 @@ def tile_list_strata_contacts_kernel(
         def fetch(b, parts):
             page = pages[b % 2]
             minus_below = ring.tile([P, M], F32, name="minus_below")
-            nc.vector.tensor_scalar(
-                out=minus_below[:], in0=page[:].indirect(list4[:]),
-                scalar1=-1.0, scalar2=0.0, op0=ALU.mult, op1=ALU.add,
-            )
+            if parts > 1:
+                nc.vector.tensor_scalar(
+                    out=minus_below[:], in0=page[:].indirect(list4[:]),
+                    scalar1=-1.0, scalar2=0.0, op0=ALU.mult, op1=ALU.add,
+                )
+            else:
+                below = ring.tile([P, M], F32, name="below")
+                nc.vector.tensor_copy(out=below[:], in_=page[:].indirect(list4[:]))
+                nc.scalar.activation(out=minus_below[:], in_=below[:], func=ACT.Copy, scale=-1.0)
             width = M // parts
             a, q = divmod(b, 4)
             for part in range(parts):
@@ -279,8 +298,8 @@ def tile_list_strata_contacts_kernel(
             lambda: stage2_operand("g", hiatus, 1, False),
             lambda: stage2_operand("w6", w6, 0, True),
             lambda: stage2_operand("w6", w6, 1, True),
-            lambda: stage2_operand("w4", w4, 0, True),
-            lambda: stage2_operand("w4", w4, 1, True),
+            lambda: round_w4(0),
+            lambda: round_w4(1),
         ]
 
         units = 16
@@ -289,9 +308,13 @@ def tile_list_strata_contacts_kernel(
         w5_wd = deal_w5_words()
         w5_sd = deal_w5_scales()
         for u in range(units):
-            if u + 1 < units:
+            if by_relu(u + 1):
+                turn_h(u)
                 first_term(u + 1)
-            turn_h(u)
+            else:
+                if u + 1 < units:
+                    first_term(u + 1)
+                turn_h(u)
             if u == 0:
                 w1_q[1] = round_and_quantize(w1_raw[1], "w1q1", False, True)
             if u + 1 < units:
@@ -339,6 +362,8 @@ def tile_list_strata_contacts_kernel(
             mx_passes(sums[hf, pair], "w6", 1, pair, hf, False, False)
             mx_passes(sums[hf, pair], "w5", 0, pair, hf, False, False)
         fetch(7, 2)
+        for a in range(2):
+            quant["w4", a] = quantize(quant["w4", a], f"w4{a}", 6 * T + 4 * T2 + 4 * N * a)
         quantize_z(1, 0)
         quantize_z(1, 1)
         out_rows = out_0.rearrange("(p t) m -> p t m", t=4)

@@ -250,28 +250,29 @@ def tile_list_strata_contacts_kernel(
 
         def fetch(b, parts):
             page = pages[b % 2]
-            minus_below = ring.tile([P, M], F32, name="minus_below")
-            if parts > 1:
-                nc.vector.tensor_scalar(
-                    out=minus_below[:], in0=page[:].indirect(list4[:]),
-                    scalar1=-1.0, scalar2=0.0, op0=ALU.mult, op1=ALU.add,
-                )
-            else:
-                below = ring.tile([P, M], F32, name="below")
-                nc.vector.tensor_copy(out=below[:], in_=page[:].indirect(list4[:]))
-                nc.scalar.activation(out=minus_below[:], in_=below[:], func=ACT.Copy, scale=-1.0)
+            above = ring.tile([P, M], F32, name="above")
+            nc.vector.tensor_tensor(out=above[:], in0=page[:].indirect(list3[:]), in1=hi_rows[b][:], op=ALU.add)
             width = M // parts
             a, q = divmod(b, 4)
             for part in range(parts):
                 cols = slice(width * part, width * (part + 1))
-                above = ring.tile([P, width], F32, name="above")
-                nc.vector.tensor_copy(out=above[:], in_=page[:].indirect(list3[:, width * part // 16 : width * (part + 1) // 16]))
+                minus_z = ring.tile([P, width], F32, name="minus_z")
+                nc.vector.tensor_tensor(
+                    out=minus_z[:], in0=page[:].indirect(list4[:, width * part // 16 : width * (part + 1) // 16]),
+                    in1=above[:, cols], op=ALU.subtract,
+                )
                 z_ps = bank(f"z{part}")
-                transposed_sum(z_ps, (hi_rows[b][:, cols], minus_below[:, cols], above[:]))
+                transposed_sum(z_ps, (minus_z[:],))
                 for x in range(width // 256):
-                    nc.scalar.copy(
-                        out=z_pairs[a][part + x][:, :, :, 64 * q : 64 * (q + 1)].rearrange("m c u (p e) -> m c u p e", e=2),
-                        in_=z_ps[:, 256 * x : 256 * (x + 1)].rearrange("m (c p u e) -> m c u p e", c=2, u=2, e=2),
+                    nc.scalar.activation(
+                        out=z_pairs[a][part + x][:, :, :, 64 * q : 64 * (q + 1)].rearrange("m c u (p e) -> m c u p e", e=2)[:, 0],
+                        in_=z_ps[:, 256 * x : 256 * x + 128].rearrange("m (p u e) -> m u p e", u=2, e=2),
+                        func=ACT.Copy, scale=-1.0,
+                    )
+                    nc.scalar.activation(
+                        out=z_pairs[a][part + x][:, :, :, 64 * q : 64 * (q + 1)].rearrange("m c u (p e) -> m c u p e", e=2)[:, 1],
+                        in_=z_ps[:, 256 * x + 128 : 256 * (x + 1)].rearrange("m (p u e) -> m u p e", u=2, e=2),
+                        func=ACT.Copy, scale=-1.0,
                     )
 
         def quantize_z(a, hf):

@@ -19,7 +19,17 @@ ACT = mybir.ActivationFunctionType
 
 P = 128
 HALF = 512
-W1_WIDTHS = (128, 128, 256, 512)
+W1_WIDTHS = (128, 128, 256, 256, 256)
+GPSIMD_CLEARS = 704
+ROUND_GROUPS = 32
+DEALT_READS_PER_STEP = 4
+FIRST_DEALT_STEP = 4
+
+TAB_LOW, TAB_HIGH, TAB_SCALES = 0, 8192, 16384
+STAGE = 20480
+TERMS = STAGE + 3 * 8192
+Z_UPPER = TERMS + 8 * 2048
+LARGER = Z_UPPER + 4 * 2048
 
 
 def tile_list_strata_contacts_kernel(
@@ -30,12 +40,15 @@ def tile_list_strata_contacts_kernel(
     with ExitStack() as ctx:
         keep = ctx.enter_context(tc.tile_pool(name="keep", bufs=1))
         shared = ctx.enter_context(tc.tile_pool(name="shared", bufs=1))
-        bfp = ctx.enter_context(tc.tile_pool(name="bfp", bufs=3))
         ring = ctx.enter_context(tc.tile_pool(name="ring", bufs=3))
+        pair = ctx.enter_context(tc.tile_pool(name="pair", bufs=2))
         psum = ctx.enter_context(tc.psum_pool(name="psum", bufs=1))
 
         def held(name, shape, dtype):
             return keep.tile(shape, dtype, name=name, align_bytes=64)
+
+        def placed(name, shape, dtype, offset):
+            return shared.tile(shape, dtype, name=name, offset=offset, align_bytes=64)
 
         def bank(tag):
             return psum.tile([P, 512], F32, name=tag)
@@ -44,154 +57,142 @@ def tile_list_strata_contacts_kernel(
             for q in range(4):
                 queue.dma_start(out=plane[32 * q : 32 * q + 4].bitcast(I32), in_=rows[4 * q : 4 * q + 4].bitcast(I32))
 
-        list1 = held("list1", [P, S // 16], U16)
-        list2 = held("list2", [P, S // 16], U16)
-        list3 = held("list3", [P, M // 16], U16)
-        list4 = held("list4", [P, M // 16], U16)
-        tab_w = shared.tile([P, T], I32, name="tab_w", offset=0)
-        tab_s = shared.tile([P, T], U8, name="tab_s", offset=4 * T)
-        w23_s = held("w23_s", [P, 2 * H], U8)
-        w2_s = w23_s[:, 0:H]
-        w3_s = w23_s[:, H : 2 * H]
-        w5_s = held("w5_s", [P, 2, N], U8)
-        pages = [shared.tile([P, T2], F32, name=f"page{i}", offset=6 * T + 4 * T2 * i) for i in range(2)]
-        ident = held("ident", [P, P], F32)
-        warm = held("warm", [P, 2], F32)
-
-        nc.gpsimd.memset(tab_s[:].bitcast(I32)[:, 0:704], 0)
-        nc.vector.memset(tab_s[:].bitcast(I32)[:, 704:1024], 0)
-        nc.vector.memset(w23_s[:].bitcast(I32), 0)
-        nc.vector.memset(w5_s[:].bitcast(I32), 0)
-        nc.vector.memset(warm[:], 0.0)
-        nc.scalar.activation(out=warm[:, 1:2], in_=warm[:, 0:1], func=ACT.Tanh)
-        make_identity(nc, ident[:])
-        nc.vector.memset(pages[0][:], 0.0)
-        nc.gpsimd.memset(pages[1][:], 0.0)
-
-        nc.sync.dma_start(list1[:], offs)
-        staged_loads = []
-
-        def staging(shape, dtype):
-            slot = len(staged_loads) % 2
-            staged_loads.append(slot)
-            return shared.tile(shape, dtype, name=f"staging{slot}", offset=2 * T * slot)
-
         def load_rows(rows, raw):
             nc.sync.dma_start(out=raw[:], in_=rows.rearrange("(p j) w -> p j w", j=4))
             return raw
 
-        def round_and_quantize(raw, name, dealt, negated=False):
-            return quantize(round_rows(raw, dealt, negated), name)
+        list1 = held("list1", [P, S // 16], U16)
+        list2 = held("list2", [P, S // 16], U16)
+        list3 = held("list3", [P, M // 16], U16)
+        list4 = held("list4", [P, M // 16], U16)
+        tab_w = placed("tab_w", [P, T], I32, TAB_LOW)
+        tab_s = placed("tab_s", [P, T], U8, TAB_SCALES)
+        w2_s = held("w2_s", [P, H], U8)
+        w3_s = held("w3_s", [P, H], U8)
+        w5_s = held("w5_s", [P, 2, N], U8)
+        pages = [held(f"page{i}", [P, T2], F32) for i in range(2)]
+        ident = held("ident", [P, P], F32)
 
-        def round_rows(raw, dealt, negated=False):
+        nc.gpsimd.memset(tab_s[:].bitcast(I32)[:, 0:GPSIMD_CLEARS], 0)
+        nc.vector.memset(tab_s[:].bitcast(I32)[:, GPSIMD_CLEARS:], 0)
+        nc.vector.memset(w3_s[:].bitcast(I32), 0)
+        nc.vector.memset(w2_s[:].bitcast(I32), 0)
+        nc.vector.memset(w5_s[:].bitcast(I32), 0)
+        load_scale_rows(nc.gpsimd, w3_s, w3_scales[0])
+        make_identity(nc, ident[:])
+        nc.vector.memset(pages[0][:], 0.0)
+        nc.vector.memset(pages[1][:], 0.0)
+
+        w1_starts = [sum(W1_WIDTHS[:i]) for i in range(len(W1_WIDTHS))]
+
+        def load_w1(i):
+            shape = [P, 4, W1_WIDTHS[i]]
+            raw = placed(f"w1_raw{i}", shape, F32, TAB_LOW + 4096 * (i - 3)) if i >= 3 else held(f"w1_raw{i}", shape, F32)
+            return load_rows(w1[:, w1_starts[i] : w1_starts[i] + W1_WIDTHS[i]], raw)
+
+        tab_w_dram = tab_words[0].rearrange("p t i -> p (t i)").bitcast(I32)
+        w2_dram = w2_words[0].rearrange("p c i -> p (c i)").bitcast(I32)
+        w2_w = held("w2_w", [P, H], I32)
+        w3_w = held("w3_w", [P, 2 * H], U8)
+        w5_w = held("w5_w", [P, 2, 2 * N], U8)
+        wgs_sb = held("wgs_sb", [P, S], F32)
+        nc.sync.dma_start(list1[:], offs)
+        nc.sync.dma_start(out=tab_w[:, 0 : T // 4], in_=tab_w_dram[:, 0 : T // 4])
+        load_scale_rows(nc.sync, tab_s, tab_scales[0])
+        w1_raw = {0: load_w1(0)}
+        nc.sync.dma_start(out=tab_w[:, T // 4 : T], in_=tab_w_dram[:, T // 4 : T])
+        nc.sync.dma_start(out=w2_w[:, 0:256], in_=w2_dram[:, 0:256])
+        nc.sync.dma_start(out=w3_w[:].bitcast(I32), in_=w3_words[0].bitcast(I32))
+        load_scale_rows(nc.sync, w2_s, w2_scales[0])
+        w1_raw[1] = load_w1(1)
+        nc.sync.dma_start(list2[:], offs2)
+        nc.sync.dma_start(out=wgs_sb[:, 0:HALF], in_=wgs[:, 0:HALF])
+        nc.sync.dma_start(out=w5_w[:].bitcast(I32), in_=w5_words.rearrange("a p c -> p a c").bitcast(I32))
+        load_scale_rows(nc.sync, w5_s, w5_scales.rearrange("a q c -> q a c"))
+        nc.sync.dma_start(out=wgs_sb[:, HALF:S], in_=wgs[:, HALF:S])
+        nc.sync.dma_start(out=w2_w[:, 256:H], in_=w2_dram[:, 256:H])
+        w1_raw[2] = load_w1(2)
+        nc.sync.dma_start(list3[:], offs3)
+        nc.sync.dma_start(list4[:], offs4)
+
+        def round_rows(raw, grouped, dealt, negated=False):
             width = raw.shape[2]
-            grouped = bfp.tile([P, 4 * width], BF16, name="grouped", align_bytes=64)
             if dealt:
                 dst = grouped[:].rearrange("p (t m j) -> p m t j", t=4, j=4)
                 src = raw[:].rearrange("p j (m t) -> p m t j", t=4)
             else:
                 dst = grouped[:].rearrange("p (c i j) -> p c j i", i=4, j=4)
                 src = raw[:].rearrange("p j (c i) -> p c j i", i=4)
-            for c0 in range(0, width // 4, 64):
-                c1 = min(c0 + 64, width // 4)
+            for c0 in range(0, width // 4, ROUND_GROUPS):
                 if negated:
-                    nc.scalar.activation(out=dst[:, c0:c1], in_=src[:, c0:c1], func=ACT.Copy, scale=-1.0)
+                    nc.scalar.activation(out=dst[:, c0 : c0 + ROUND_GROUPS], in_=src[:, c0 : c0 + ROUND_GROUPS], func=ACT.Copy, scale=-1.0)
                 else:
-                    nc.scalar.copy(out=dst[:, c0:c1], in_=src[:, c0:c1])
+                    nc.scalar.copy(out=dst[:, c0 : c0 + ROUND_GROUPS], in_=src[:, c0 : c0 + ROUND_GROUPS])
             return grouped
 
-        def quantize(grouped, name, codes_offset=None):
+        def quantize(grouped, name):
             width = grouped.shape[1] // 4
-            if codes_offset is None:
-                codes = held(name + "_c", [P, width], U32)
-            else:
-                codes = shared.tile([P, width], U32, name=name + "_c", offset=codes_offset, align_bytes=64)
+            codes = held(name + "_c", [P, width], U32)
             scales = held(name + "_s", [P, width], U8)
             nc.vector.quantize_mx(out=codes[:].bitcast(FP8X4), scales=scales[:], in_=grouped[:])
             return codes, scales
 
-        w1_starts = [sum(W1_WIDTHS[:i]) for i in range(len(W1_WIDTHS))]
-        tab_w_dram = tab_words[0].rearrange("p t i -> p (t i)").bitcast(I32)
-        nc.sync.dma_start(out=tab_w[:, 0 : T // 2], in_=tab_w_dram[:, 0 : T // 2])
-        load_scale_rows(nc.sync, tab_s, tab_scales[0])
-        w1_raw = {0: load_rows(w1[:, 0:128], held("w1_first", [P, 4, 128], F32))}
-        nc.sync.dma_start(out=tab_w[:, T // 2 : T], in_=tab_w_dram[:, T // 2 : T])
-        w2_w = held("w2_w", [P, H], I32)
-        nc.sync.dma_start(out=w2_w[:], in_=w2_words[0].rearrange("p c i -> p (c i)").bitcast(I32))
-        load_scale_rows(nc.sync, w2_s, w2_scales[0])
-        w3_w = held("w3_w", [P, 2 * H], U8)
-        nc.sync.dma_start(out=w3_w[:].bitcast(I32), in_=w3_words[0].bitcast(I32))
-        load_scale_rows(nc.sync, w3_s, w3_scales[0])
-        w1_raw[1] = load_rows(w1[:, 128:256], held("w1_second", [P, 4, 128], F32))
-        w5_w = held("w5_w", [P, 2, 2 * N], U8)
-        nc.sync.dma_start(out=w5_w[:].bitcast(I32), in_=w5_words.rearrange("a p c -> p a c").bitcast(I32))
-        nc.sync.dma_start(list2[:], offs2)
-        wgs_sb = held("wgs_sb", [P, S], F32)
-        nc.sync.dma_start(out=wgs_sb[:], in_=wgs)
-        load_scale_rows(nc.sync, w5_s, w5_scales.rearrange("a q c -> q a c"))
-        nc.sync.dma_start(list3[:], offs3)
-        nc.sync.dma_start(list4[:], offs4)
+        minus_w1_c = held("minus_w1_c", [P, H], U32)
+        minus_w1_s = held("minus_w1_s", [P, H], U8)
+
+        def quantize_w1(i):
+            shape = [P, 4 * W1_WIDTHS[i]]
+            if i < 2:
+                grouped = held(f"w1_grouped{i}", shape, BF16)
+            else:
+                grouped = placed(f"w1_grouped{i}", shape, BF16, LARGER + 2048 * (i - 2))
+            round_rows(w1_raw[i], grouped, False, True)
+            cols = slice(w1_starts[i], w1_starts[i] + W1_WIDTHS[i])
+            nc.vector.quantize_mx(out=minus_w1_c[:, cols].bitcast(FP8X4), scales=minus_w1_s[:, cols], in_=grouped[:])
 
         v_s = [held(f"v_s{hf}", [P, HALF], U8) for hf in range(2)]
         v_w = [held(f"v_w{hf}", [P, HALF], U32) for hf in range(2)]
         nc.vector.tensor_copy(out=v_s[0][:], in_=tab_s[:].indirect(list1[:, 0:32]))
-        w1_q = {0: round_and_quantize(w1_raw[0], "w1q0", False, True)}
-        nc.vector.tensor_copy(out=v_w[0][:], in_=tab_w[:].bitcast(U32).indirect(list1[:, 0:32]))
         nc.vector.tensor_copy(out=v_s[1][:], in_=tab_s[:].indirect(list1[:, 32:64]))
+        quantize_w1(0)
+        nc.vector.tensor_copy(out=v_w[0][:], in_=tab_w[:].bitcast(U32).indirect(list1[:, 0:32]))
         nc.vector.tensor_copy(out=v_w[1][:], in_=tab_w[:].bitcast(U32).indirect(list1[:, 32:64]))
 
-        def deal_w5_words():
-            dealt = shared.tile([P, 2, 2 * N], U8, name="w5_dealt_words", offset=5 * T, align_bytes=64)
-            nc.vector.tensor_copy(
-                out=dealt[:].bitcast(U16).rearrange("p a (t m) -> p a t m", t=4),
-                in_=w5_w[:].bitcast(U16).rearrange("p a (m t) -> p a t m", t=4),
-            )
-            return dealt
+        quantize_w1(1)
+        w1_raw[3] = load_w1(3)
+        w1_raw[4] = load_w1(4)
+        hiatus_rows = [held(f"hiatus_rows{b}", [P, M], F32) for b in range(4)]
+        for b in range(4):
+            nc.sync.dma_start(out=hiatus_rows[b][:], in_=hiatus[P * b : P * (b + 1), :])
+        raw = {
+            ("g", 0): load_rows(hiatus[0:512, :], placed("g_raw0", [P, 4, M], F32, TAB_HIGH)),
+            ("g", 1): load_rows(hiatus[512:1024, :], held("g_raw1", [P, 4, M], F32)),
+        }
+        wgs_by_t = wgs.rearrange("(i t) j -> t i j", t=4)
 
-        def deal_w5_scales():
-            dealt = shared.tile([P, 2, N], U8, name="w5_dealt_scales", offset=5 * T + 4 * N, align_bytes=64)
-            nc.vector.tensor_copy(
-                out=dealt[:].rearrange("p a (t m) -> p a t m", t=4),
-                in_=w5_s[:].rearrange("p a (m t) -> p a t m", t=4),
-            )
-            return dealt
+        def load_dealt_wgs(t, tile):
+            for q in range(4):
+                nc.sync.dma_start(out=tile[32 * q : 32 * (q + 1), :], in_=wgs_by_t[t])
+            return tile
 
-        hi_rows = {}
-        quant = {}
+        wgs_dealt = {0: load_dealt_wgs(0, held("wgs_dealt0", [P, S], F32))}
+        raw["w6", 0] = load_rows(w6[0:512, :], placed("w6_raw0", [P, 4, N], F32, STAGE))
+        raw["w6", 1] = load_rows(w6[512:1024, :], placed("w6_raw1", [P, 4, N], F32, STAGE + 8192))
+        raw["w4", 0] = load_rows(w4[0:512, :], placed("w4_raw0", [P, 4, N], F32, STAGE + 2 * 8192))
 
-        def w1_piece(i):
-            raw = load_rows(w1[:, w1_starts[i] : w1_starts[i] + W1_WIDTHS[i]], staging([P, 4, W1_WIDTHS[i]], F32))
-            w1_q[i] = round_and_quantize(raw, f"w1q{i}", False, True)
-
-        def stage2_operand(name, src, a, dealt):
-            raw = load_rows(src[512 * a : 512 * (a + 1), :], staging([P, 4, 512], F32))
-            quant[name, a] = round_and_quantize(raw, f"{name}{a}", dealt)
-
-        def round_w4(a):
-            raw = load_rows(w4[512 * a : 512 * (a + 1), :], staging([P, 4, 512], F32))
-            quant["w4", a] = round_rows(raw, True)
-
-        def load_hi(b):
-            hi_rows[b] = shared.tile([P, M], F32, name=f"hi_rows{b % 2}", offset=4 * T + 4 * M * (b % 2))
-            nc.sync.dma_start(out=hi_rows[b][:], in_=hiatus[P * b : P * (b + 1), :])
-
-        staged = {}
-
-        def product(u, tag, names):
-            b, hf = divmod(u, 2)
-            i = max(x for x in range(len(W1_WIDTHS)) if w1_starts[x] <= P * b)
-            w1_cols = slice(P * b - w1_starts[i], P * (b + 1) - w1_starts[i])
-            cols = slice(P * b, P * (b + 1))
+        def product(tag, names, chunks, r0, width):
+            cols = slice(r0, r0 + width)
             moving = {
-                "minus_w1": (w1_q[i][0][:, w1_cols].bitcast(FP8X4), w1_q[i][1][:, w1_cols]),
+                "minus_w1": (minus_w1_c[:, cols].bitcast(FP8X4), minus_w1_s[:, cols]),
                 "w2": (w2_w[:, cols].bitcast(FP8X4), w2_s[:, cols]),
-                "w3": (w3_w[:, 2 * P * b : 2 * P * (b + 1)].bitcast(FP4X4), w3_s[:, cols]),
+                "w3": (w3_w[:, 2 * r0 : 2 * (r0 + width)].bitcast(FP4X4), w3_s[:, cols]),
             }
             acc = bank(tag)
-            for c in range(4):
+            for x, chunk in enumerate(chunks):
+                hf, c = divmod(chunk, 4)
                 for n, name in enumerate(names):
                     nc.tensor.matmul_mx(
-                        out=acc[:, P * c : P * (c + 1)],
+                        out=acc[:, width * x : width * (x + 1)],
                         lhsT=v_w[hf][:, P * c : P * (c + 1)].bitcast(FP8X4),
                         lhsT_scale=v_s[hf][:, P * c : P * (c + 1)],
                         rhs=moving[name][0], rhs_scale=moving[name][1],
@@ -199,143 +200,214 @@ def tile_list_strata_contacts_kernel(
                     )
             return acc
 
-        def by_relu(u):
-            return u % 2 == 1 and u < 15
-
-        def first_term(u):
-            term = staging([P, 512], F32) if u < 2 else ring.tile([P, 512], F32, name="first_term")
-            if by_relu(u):
-                nc.scalar.activation(out=term[:], in_=product(u, "z1", ("w2", "minus_w1"))[:], func=ACT.Relu)
-            else:
-                minus_d1 = product(u, "d1", ("minus_w1",))
-                d2 = product(u, "d2", ("w2",))
-                if u == 0:
-                    d1_sb = shared.tile([P, 512], F32, name="first_d1", offset=5 * T + 2 * N)
-                else:
-                    d1_sb = ring.tile([P, 512], F32, name="d1_sb")
-                nc.scalar.activation(out=d1_sb[:], in_=minus_d1[:], func=ACT.Copy, scale=-1.0)
-                nc.vector.tensor_tensor(out=term[:], in0=d2[:], in1=d1_sb[:], op=ALU.max)
-            staged[u] = term
-
-        def second_term(u):
-            acc = product(u, "d3", ("w3", "minus_w1") if by_relu(u) else ("w3",))
-            term = ring.tile([P, 512], F32, name="second_term")
-            nc.scalar.activation(out=term[:], in_=acc[:], func=ACT.Copy, scale=-1.0)
-            staged[u] = (term, staged[u])
-
         def transposed_sum(acc, terms):
-            chunks = terms[0].shape[1] // P
             for n, term in enumerate(terms):
-                for c in range(chunks):
+                for c in range(4):
                     nc.tensor.matmul(
                         acc[:, P * c : P * (c + 1)], term[:, P * c : P * (c + 1)], ident[:], is_transpose=True,
-                        start=(n == 0 and c == 0), stop=(n == len(terms) - 1 and c == chunks - 1),
+                        start=(n == 0 and c == 0), stop=(n == len(terms) - 1 and c == 3),
                     )
 
-        def turn_h(u):
-            h_ps = bank("h")
-            transposed_sum(h_ps, staged[u])
-            h_sb = ring.tile([P, HALF], F32, name="h_sb")
-            nc.scalar.copy(out=h_sb[:], in_=h_ps[:])
-            staged[u] = h_sb
+        larger, minus_d3, h_lower = {}, {}, {}
 
-        def put_in_page(u):
+        def lower_product(u, tag, name):
             b, hf = divmod(u, 2)
-            nc.vector.tensor_tensor(
-                out=pages[b % 2][:].indirect(list2[:, 32 * hf : 32 * (hf + 1)]),
-                in0=staged[u][:], in1=wgs_sb[:, HALF * hf : HALF * (hf + 1)], op=ALU.mult,
-            )
+            return product(tag, (name,), range(4 * hf, 4 * hf + 4), P * b, P)
 
-        z_pairs = [[held(f"z_pairs{a}{hf}", [P, 2, 2, 2 * P], BF16) for hf in range(2)] for a in range(2)]
-
-        def fetch(b, parts):
-            page = pages[b % 2]
-            above = ring.tile([P, M], F32, name="above")
-            nc.vector.tensor_tensor(out=above[:], in0=page[:].indirect(list3[:]), in1=hi_rows[b][:], op=ALU.add)
-            width = M // parts
-            a, q = divmod(b, 4)
-            for part in range(parts):
-                cols = slice(width * part, width * (part + 1))
-                minus_z = ring.tile([P, width], F32, name="minus_z")
-                nc.vector.tensor_tensor(
-                    out=minus_z[:], in0=page[:].indirect(list4[:, width * part // 16 : width * (part + 1) // 16]),
-                    in1=above[:, cols], op=ALU.subtract,
-                )
-                z_ps = bank(f"z{part}")
-                transposed_sum(z_ps, (minus_z[:],))
-                for x in range(width // 256):
-                    nc.scalar.activation(
-                        out=z_pairs[a][part + x][:, :, :, 64 * q : 64 * (q + 1)].rearrange("m c u (p e) -> m c u p e", e=2)[:, 0],
-                        in_=z_ps[:, 256 * x : 256 * x + 128].rearrange("m (p u e) -> m u p e", u=2, e=2),
-                        func=ACT.Copy, scale=-1.0,
-                    )
-                    nc.scalar.activation(
-                        out=z_pairs[a][part + x][:, :, :, 64 * q : 64 * (q + 1)].rearrange("m c u (p e) -> m c u p e", e=2)[:, 1],
-                        in_=z_ps[:, 256 * x + 128 : 256 * (x + 1)].rearrange("m (p u e) -> m u p e", u=2, e=2),
-                        func=ACT.Copy, scale=-1.0,
-                    )
-
-        def quantize_z(a, hf):
-            grouped = held(f"z_grouped{a}{hf}", [P, 4 * 256], BF16)
-            words = z_pairs[a][hf][:].bitcast(F32)
-            back = bank(f"back{hf}")
-            for c in range(2):
-                for u in range(2):
-                    col = P * (2 * c + u)
-                    nc.tensor.transpose(back[:, col : col + P], words[:, c, u, :], ident[:])
-            nc.scalar.copy(
-                out=grouped[:].bitcast(F32).rearrange("p (c m u) -> p c m u", c=2, u=2),
-                in_=back[:].rearrange("p (c u m) -> p c m u", c=2, u=2),
-            )
-            codes = held(f"z_c{a}{hf}", [P, 256], U32)
-            scales = held(f"z_s{a}{hf}", [P, 256], U8)
-            nc.vector.quantize_mx(out=codes[:].bitcast(FP8X4), scales=scales[:], in_=grouped[:])
-            quant["z", a, hf] = (codes, scales)
-
-        side_work = [
-            lambda: w1_piece(2),
-            lambda: w1_piece(3),
-            lambda: stage2_operand("g", hiatus, 0, False),
-            lambda: stage2_operand("g", hiatus, 1, False),
-            lambda: stage2_operand("w6", w6, 0, True),
-            lambda: stage2_operand("w6", w6, 1, True),
-            lambda: round_w4(0),
-            lambda: round_w4(1),
-        ]
-
-        units = 16
-        first_term(0)
-        second_term(0)
-        w5_wd = deal_w5_words()
-        w5_sd = deal_w5_scales()
-        for u in range(units):
-            if by_relu(u + 1):
-                turn_h(u)
-                first_term(u + 1)
-            else:
-                if u + 1 < units:
-                    first_term(u + 1)
-                turn_h(u)
+        def lower_larger(u):
+            minus_d1 = lower_product(u, "d1", "minus_w1")
+            d2 = lower_product(u, "d2", "w2")
             if u == 0:
-                w1_q[1] = round_and_quantize(w1_raw[1], "w1q1", False, True)
-            if u + 1 < units:
-                second_term(u + 1)
-            put_in_page(u)
-            if u % 2 == 0 and u > 0:
-                fetch(u // 2 - 1, 1)
-                if u == 8:
-                    quantize_z(0, 0)
-                    quantize_z(0, 1)
-            if u % 2 == 1:
-                load_hi(u // 2)
-            if 1 <= u <= len(side_work):
-                side_work[u - 1]()
+                d1_sb = placed("first_d1", [P, 512], F32, TAB_SCALES + 2 * N)
+            else:
+                d1_sb = pair.tile([P, 512], F32, name="d1_sb")
+            nc.scalar.activation(out=d1_sb[:], in_=minus_d1[:], func=ACT.Copy, scale=-1.0)
+            larger[u] = placed(f"larger{u}", [P, 512], F32, LARGER + 2048 * u)
+            nc.vector.tensor_tensor(out=larger[u][:], in0=d2[:], in1=d1_sb[:], op=ALU.max)
 
-        def mx_passes(acc, name, a, pair, hf, start, stop):
-            step = P if name == "w5" else 256
-            todo = [(x, m0) for x in range(2) for m0 in range(0, 256, step)]
-            for n, (x, m0) in enumerate(todo):
-                t = 2 * pair + x
+        def lower_minus_d3(u):
+            d3 = lower_product(u, "d3", "w3")
+            minus_d3[u] = placed(f"minus_d3_{u}", [P, 512], F32, TERMS + 2048 * u)
+            nc.scalar.activation(out=minus_d3[u][:], in_=d3[:], func=ACT.Copy, scale=-1.0)
+
+        def lower_turn(u):
+            h_ps = bank("h_lower")
+            transposed_sum(h_ps, (minus_d3[u], larger[u]))
+            h_lower[u] = ring.tile([P, HALF], F32, name="h_lower_sb")
+            nc.scalar.copy(out=h_lower[u][:], in_=h_ps[:])
+
+        def put_in_page(slab, hf, values, weights):
+            nc.vector.tensor_tensor(
+                out=pages[slab % 2][:].indirect(list2[:, 32 * hf : 32 * (hf + 1)]),
+                in0=values, in1=weights[:, HALF * hf : HALF * (hf + 1)], op=ALU.mult,
+            )
+
+        def fetch_minus(slab, columns, m0, width, other, out):
+            nc.vector.tensor_tensor(
+                out=out, in0=pages[slab % 2][:].indirect(columns[:, m0 // 16 : (m0 + width) // 16]),
+                in1=other, op=ALU.subtract,
+            )
+
+        h_upper = [held(f"h_upper{hf}", [P, 4, HALF], F32) for hf in range(2)]
+        first_term, second_term = {}, {}
+
+        def dealt(acc):
+            return acc[:].rearrange("j (p t) -> j t p", t=4)
+
+        def by_t(tile):
+            return tile[:].rearrange("j (t p) -> j t p", t=4)
+
+        def upper_first(c):
+            first_term[c] = ring.tile([P, 512], F32, name="first_term")
+            if c == 0:
+                minus_d1 = product("first", ("minus_w1",), (c,), 512, 512)
+                d2 = product("spare", ("w2",), (c,), 512, 512)
+                d1_sb = pair.tile([P, 512], F32, name="d1_sb")
+                nc.scalar.activation(out=by_t(d1_sb), in_=dealt(minus_d1), func=ACT.Copy, scale=-1.0)
+                nc.vector.tensor_tensor(out=by_t(first_term[c]), in0=dealt(d2), in1=by_t(d1_sb), op=ALU.max)
+            else:
+                acc = product("first", ("w2", "minus_w1"), (c,), 512, 512)
+                nc.scalar.activation(out=by_t(first_term[c]), in_=dealt(acc), func=ACT.Relu)
+
+        def upper_second(c):
+            acc = product("second", ("w3",) if c == 0 else ("w3", "minus_w1"), (c,), 512, 512)
+            second_term[c] = ring.tile([P, 512], F32, name="second_term")
+            nc.scalar.activation(out=by_t(second_term[c]), in_=dealt(acc), func=ACT.Copy, scale=-1.0)
+
+        def upper_turn(c):
+            h_ps = bank("h_upper")
+            transposed_sum(h_ps, (second_term[c], first_term[c]))
+            hf, x = divmod(c, 4)
+            nc.scalar.copy(out=h_upper[hf][:, :, P * x : P * (x + 1)], in_=h_ps[:].rearrange("p (t j) -> p t j", t=4))
+
+        upper_work = []
+        for c in range(8 + 2):
+            if c < 8:
+                upper_work.append((upper_first, c))
+                upper_work.append((upper_second, c))
+            if c >= 2:
+                upper_work.append((upper_turn, c - 2))
+
+        below, z_lower = {}, {}
+
+        def lower_below(b):
+            below[b] = placed(f"below{b}", [P, M], F32, TERMS + 2048 * ((2 * b + 2) % 8))
+            fetch_minus(b, list4, 0, M, hiatus_rows[b][:], below[b][:])
+
+        def lower_z(b):
+            z_lower[b] = placed(f"z_lower{b}", [P, M], F32, TERMS + 2048 * ((2 * b + 3) % 8))
+            fetch_minus(b, list3, 0, M, below[b][:], z_lower[b][:])
+
+        lower_larger(0)
+        lower_minus_d3(0)
+        w5_wd = placed("w5_dealt_words", [P, 2, 2 * N], U8, TAB_SCALES)
+        nc.vector.tensor_copy(
+            out=w5_wd[:].bitcast(U16).rearrange("p a (t m) -> p a t m", t=4),
+            in_=w5_w[:].bitcast(U16).rearrange("p a (m t) -> p a t m", t=4),
+        )
+        w5_sd = placed("w5_dealt_scales", [P, 2, N], U8, TAB_SCALES + 4 * N)
+        nc.vector.tensor_copy(
+            out=w5_sd[:].rearrange("p a (t m) -> p a t m", t=4),
+            in_=w5_s[:].rearrange("p a (m t) -> p a t m", t=4),
+        )
+        done = 0
+        for u in range(8):
+            if u + 1 < 8:
+                lower_larger(u + 1)
+            if u >= FIRST_DEALT_STEP:
+                for work, c in upper_work[done : done + DEALT_READS_PER_STEP]:
+                    work(c)
+                done = done + DEALT_READS_PER_STEP
+            lower_turn(u)
+            if u + 1 < 8:
+                lower_minus_d3(u + 1)
+            if u < 3:
+                quantize_w1(u + 2)
+            if u >= 2 and u % 2 == 0:
+                lower_below(u // 2 - 1)
+            if u >= 3 and u % 2 == 1:
+                lower_z((u - 3) // 2)
+            put_in_page(u // 2, u % 2, h_lower[u][:], wgs_sb)
+        for work, c in upper_work[done:]:
+            work(c)
+        raw["w4", 1] = load_rows(w4[512:1024, :], placed("w4_raw1", [P, 4, N], F32, TAB_LOW))
+
+        quant = {}
+
+        def late_grouped():
+            slot = 3 - len(quant) % 3
+            return placed(f"grouped{len(quant)}", [P, 4 * 512], BF16, LARGER + 4096 * slot)
+
+        def stage2_operand(name, a):
+            quant[name, a] = quantize(round_rows(raw[name, a], late_grouped(), name != "g"), f"{name}{a}")
+
+        z_pairs = [held(f"z_pairs{hf}", [P, 2, 2, 2 * P], BF16) for hf in range(2)]
+
+        def turn_z_lower(b):
+            z_ps = bank("h_lower")
+            transposed_sum(z_ps, (z_lower[b],))
+            for x in range(2):
+                nc.scalar.copy(
+                    out=z_pairs[x][:, :, :, 64 * b : 64 * (b + 1)].rearrange("m c u (p e) -> m c u p e", e=2),
+                    in_=z_ps[:, 256 * x : 256 * (x + 1)].rearrange("m (c p u e) -> m c u p e", c=2, u=2, e=2),
+                )
+
+        def quantize_z_lower():
+            grouped = late_grouped()
+            for hf in range(2):
+                words = z_pairs[hf][:].bitcast(F32)
+                back = bank("h_upper")
+                for c in range(2):
+                    for e in range(2):
+                        col = P * (2 * c + e)
+                        nc.tensor.transpose(back[:, col : col + P], words[:, c, e, :], ident[:])
+                nc.scalar.copy(
+                    out=grouped[:, 1024 * hf : 1024 * (hf + 1)].bitcast(F32).rearrange("p (c m u) -> p c m u", c=2, u=2),
+                    in_=back[:].rearrange("p (c u m) -> p c m u", c=2, u=2),
+                )
+            quant["z", 0] = quantize(grouped, "z0")
+
+        z_upper = [placed(f"z_upper{q}", [P, 4, P], F32, Z_UPPER + 2048 * q) for q in range(4)]
+        upper_below = {}
+
+        def upper_fetch_below(t):
+            upper_below[t] = pair.tile([P, M], F32, name="upper_below")
+            fetch_minus(4 + t, list4, 0, M, raw["g", 1][:, t, :], upper_below[t][:])
+
+        def upper_z(t, q):
+            fetch_minus(4 + t, list3, P * q, P, upper_below[t][:, P * q : P * (q + 1)], z_upper[q][:, t, :])
+
+        for t in range(4):
+            if t == 1:
+                stage2_operand("g", 0)
+                wgs_dealt[1] = load_dealt_wgs(1, placed("wgs_dealt1", [P, S], F32, TAB_HIGH))
+                stage2_operand("g", 1)
+            if t == 2:
+                for b in range(3):
+                    turn_z_lower(b)
+                stage2_operand("w6", 0)
+                stage2_operand("w6", 1)
+                wgs_dealt[2] = load_dealt_wgs(2, placed("wgs_dealt2", [P, S], F32, STAGE + 8192))
+            if t == 3:
+                turn_z_lower(3)
+                quantize_z_lower()
+                stage2_operand("w4", 0)
+                stage2_operand("w4", 1)
+                wgs_dealt[3] = load_dealt_wgs(3, placed("wgs_dealt3", [P, S], F32, TAB_LOW))
+            put_in_page(4 + t, 0, h_upper[0][:, t, :], wgs_dealt[t])
+            if t == 0:
+                lower_below(3)
+            else:
+                upper_fetch_below(t - 1)
+            put_in_page(4 + t, 1, h_upper[1][:, t, :], wgs_dealt[t])
+            if t == 0:
+                lower_z(3)
+            elif t < 3:
+                for q in range(4):
+                    upper_z(t - 1, q)
+
+        def mx_passes(acc, name, a, q, start, stop):
+            for t in range(4):
                 cols = slice(P * t, P * (t + 1))
                 if name == "w5":
                     lhsT = w5_wd[:, a, 2 * P * t : 2 * P * (t + 1)].bitcast(FP4X4)
@@ -343,53 +415,67 @@ def tile_list_strata_contacts_kernel(
                 else:
                     lhsT = quant[name, a][0][:, cols].bitcast(FP8X4)
                     lhsT_scale = quant[name, a][1][:, cols]
-                if name == "w6":
-                    codes, scales = quant["g", a]
-                    m_cols = slice(256 * hf + m0, 256 * hf + m0 + step)
-                else:
-                    codes, scales = quant["z", a, hf]
-                    m_cols = slice(m0, m0 + step)
+                codes, scales = quant["g", a] if name == "w6" else quant["z", a] if a == 0 else quant["z", a, q]
+                m_cols = slice(0, P) if (name != "w6" and a == 1) else slice(P * q, P * (q + 1))
                 nc.tensor.matmul_mx(
-                    out=acc[:, 256 * x + m0 : 256 * x + m0 + step], lhsT=lhsT, lhsT_scale=lhsT_scale,
+                    out=acc[:, cols], lhsT=lhsT, lhsT_scale=lhsT_scale,
                     rhs=codes[:, m_cols].bitcast(FP8X4), rhs_scale=scales[:, m_cols],
-                    start=(start and n == 0), stop=(stop and n == len(todo) - 1),
+                    start=(start and t == 0), stop=(stop and t == 3),
                 )
 
-        quarters = [(hf, pair) for hf in range(2) for pair in range(2)]
-        sums = {}
-        for (hf, pair), tag in zip(quarters, ("d1", "d2", "d3", "h")):
-            sums[hf, pair] = bank(tag)
-            mx_passes(sums[hf, pair], "w6", 0, pair, hf, True, False)
-            mx_passes(sums[hf, pair], "w6", 1, pair, hf, False, False)
-            mx_passes(sums[hf, pair], "w5", 0, pair, hf, False, False)
-        fetch(7, 2)
-        for a in range(2):
-            quant["w4", a] = quantize(quant["w4", a], f"w4{a}", 6 * T + 4 * T2 + 4 * N * a)
-        quantize_z(1, 0)
-        quantize_z(1, 1)
+        sums, gates = {}, {}
+        for q, tag in enumerate(("d1", "d2", "d3", "first")):
+            sums[q] = bank(tag)
+            mx_passes(sums[q], "w6", 0, q, True, False)
+            mx_passes(sums[q], "w6", 1, q, False, False)
+            mx_passes(sums[q], "w5", 0, q, False, False)
+        for q, tag in enumerate(("second", "spare", "h_lower", "h_upper")):
+            gates[q] = bank(tag)
+            mx_passes(gates[q], "w4", 0, q, True, False)
+
+        last_below = {}
+
+        def last_fetch_below(q):
+            if q < 2:
+                last_below[q] = pair.tile([P, P], F32, name="last_below")
+            else:
+                last_below[q] = placed(f"last_below{q}", [P, P], F32, Z_UPPER + 2048 * (q - 2))
+            fetch_minus(7, list4, P * q, P, raw["g", 1][:, 3, P * q : P * (q + 1)], last_below[q][:])
+
+        def last_z(q):
+            fetch_minus(7, list3, P * q, P, last_below[q][:], z_upper[q][:, 3, :])
+            quant["z", 1, q] = quantize(round_rows(z_upper[q], held(f"z_grouped{q}", [P, 4 * P], BF16), False), f"z1{q}")
+
+        upper_z(2, 0)
+        last_fetch_below(0)
+        upper_z(2, 1)
+        last_z(0)
+        last_fetch_below(1)
+        upper_z(2, 2)
+        last_z(1)
+        last_fetch_below(2)
+        upper_z(2, 3)
+        last_z(2)
+        last_fetch_below(3)
+        last_z(3)
+
         out_rows = out_0.rearrange("(p t) m -> p t m", t=4)
         out_words = out_1[0].rearrange("p m t -> p (m t)").bitcast(I32)
-        y = [held(f"y{hf}", [P, 4, 256], F32) for hf in range(2)]
-        for (hf, pair), tag in zip(quarters, ("z0", "z1", "back0", "back1")):
-            gates = bank(tag)
-            mx_passes(gates, "w4", 0, pair, hf, True, False)
-            mx_passes(gates, "w4", 1, pair, hf, False, True)
-            mx_passes(sums[hf, pair], "w5", 1, pair, hf, False, True)
-            gate = ring.tile([P, 512], F32, name="gate")
-            nc.scalar.activation(out=gate[:], in_=gates[:], func=ACT.Tanh)
-            y_part = y[hf][:, 2 * pair : 2 * pair + 2, :]
-            nc.vector.tensor_tensor(
-                out=y_part.rearrange("p t m -> p (t m)"), in0=sums[hf, pair][:], in1=gate[:], op=ALU.mult
-            )
-            nc.sync.dma_start(out=out_rows[:, 2 * pair : 2 * pair + 2, 256 * hf : 256 * (hf + 1)], in_=y_part)
         y_c = held("y_c", [P, M], U32)
         y_s = held("y_s", [P, M], U8)
-        for hf, copy in enumerate((nc.scalar.copy, nc.vector.tensor_copy)):
-            cols = slice(256 * hf, 256 * (hf + 1))
-            y_grouped = held(f"y_grouped{hf}", [P, 4 * 256], BF16)
-            copy(
+        for q in range(4):
+            cols = slice(P * q, P * (q + 1))
+            mx_passes(gates[q], "w4", 1, q, False, True)
+            mx_passes(sums[q], "w5", 1, q, False, True)
+            gate = pair.tile([P, 512], F32, name="gate")
+            nc.scalar.activation(out=gate[:], in_=gates[q][:], func=ACT.Tanh)
+            y = placed(f"y{q}", [P, 4, P], F32, STAGE + 2048 * q)
+            nc.vector.tensor_tensor(out=y[:].rearrange("p t m -> p (t m)"), in0=sums[q][:], in1=gate[:], op=ALU.mult)
+            nc.sync.dma_start(out=out_rows[:, :, cols], in_=y[:])
+            y_grouped = pair.tile([P, 4 * P], BF16, name="y_grouped", align_bytes=64)
+            (nc.scalar.copy if q < 3 else nc.vector.tensor_copy)(
                 out=y_grouped[:].rearrange("p (c i t) -> p c t i", i=4, t=4),
-                in_=y[hf][:].rearrange("p t (c i) -> p c t i", i=4),
+                in_=y[:].rearrange("p t (c i) -> p c t i", i=4),
             )
             nc.vector.quantize_mx(out=y_c[:, cols].bitcast(FP8X4), scales=y_s[:, cols], in_=y_grouped[:])
             nc.sync.dma_start(out=out_words[:, cols], in_=y_c[:, cols].bitcast(I32))

@@ -19,11 +19,12 @@ ACT = mybir.ActivationFunctionType
 
 P = 128
 HALF = 512
-W1_WIDTHS = (128, 128, 256, 256, 256)
-GPSIMD_CLEARS = 704
+W1_WIDTHS = (256, 256, 256, 256)
+W2_FIRST = 256
+GPSIMD_CLEARS = 576
 ROUND_GROUPS = 32
-DEALT_READS_PER_STEP = 4
-FIRST_DEALT_STEP = 4
+DEALT_READS_PER_STEP = 5
+FIRST_DEALT_STEP = 5
 
 TAB_LOW, TAB_HIGH, TAB_SCALES = 0, 8192, 16384
 STAGE = 20480
@@ -73,10 +74,10 @@ def tile_list_strata_contacts_kernel(
         pages = [held(f"page{i}", [P, T2], F32) for i in range(2)]
         ident = held("ident", [P, P], F32)
 
+        nc.gpsimd.memset(w2_s[:].bitcast(I32), 0)
         nc.gpsimd.memset(tab_s[:].bitcast(I32)[:, 0:GPSIMD_CLEARS], 0)
         nc.vector.memset(tab_s[:].bitcast(I32)[:, GPSIMD_CLEARS:], 0)
         nc.vector.memset(w3_s[:].bitcast(I32), 0)
-        nc.vector.memset(w2_s[:].bitcast(I32), 0)
         nc.vector.memset(w5_s[:].bitcast(I32), 0)
         load_scale_rows(nc.gpsimd, w3_s, w3_scales[0])
         make_identity(nc, ident[:])
@@ -87,12 +88,13 @@ def tile_list_strata_contacts_kernel(
 
         def load_w1(i):
             shape = [P, 4, W1_WIDTHS[i]]
-            raw = placed(f"w1_raw{i}", shape, F32, TAB_LOW + 4096 * (i - 3)) if i >= 3 else held(f"w1_raw{i}", shape, F32)
+            raw = placed(f"w1_raw{i}", shape, F32, TAB_LOW + 4096 * (i - 2)) if i >= 2 else held(f"w1_raw{i}", shape, F32)
             return load_rows(w1[:, w1_starts[i] : w1_starts[i] + W1_WIDTHS[i]], raw)
 
         tab_w_dram = tab_words[0].rearrange("p t i -> p (t i)").bitcast(I32)
         w2_dram = w2_words[0].rearrange("p c i -> p (c i)").bitcast(I32)
-        w2_w = held("w2_w", [P, H], I32)
+        w2_first = held("w2_first", [P, W2_FIRST], I32)
+        w2_rest = held("w2_rest", [P, H - W2_FIRST], I32)
         w3_w = held("w3_w", [P, 2 * H], U8)
         w5_w = held("w5_w", [P, 2, 2 * N], U8)
         wgs_sb = held("wgs_sb", [P, S], F32)
@@ -101,17 +103,16 @@ def tile_list_strata_contacts_kernel(
         load_scale_rows(nc.sync, tab_s, tab_scales[0])
         w1_raw = {0: load_w1(0)}
         nc.sync.dma_start(out=tab_w[:, T // 4 : T], in_=tab_w_dram[:, T // 4 : T])
-        nc.sync.dma_start(out=w2_w[:, 0:256], in_=w2_dram[:, 0:256])
+        nc.sync.dma_start(out=w2_first[:], in_=w2_dram[:, 0:W2_FIRST])
         nc.sync.dma_start(out=w3_w[:].bitcast(I32), in_=w3_words[0].bitcast(I32))
         load_scale_rows(nc.sync, w2_s, w2_scales[0])
-        w1_raw[1] = load_w1(1)
         nc.sync.dma_start(list2[:], offs2)
         nc.sync.dma_start(out=wgs_sb[:, 0:HALF], in_=wgs[:, 0:HALF])
         nc.sync.dma_start(out=w5_w[:].bitcast(I32), in_=w5_words.rearrange("a p c -> p a c").bitcast(I32))
         load_scale_rows(nc.sync, w5_s, w5_scales.rearrange("a q c -> q a c"))
         nc.sync.dma_start(out=wgs_sb[:, HALF:S], in_=wgs[:, HALF:S])
-        nc.sync.dma_start(out=w2_w[:, 256:H], in_=w2_dram[:, 256:H])
-        w1_raw[2] = load_w1(2)
+        nc.sync.dma_start(out=w2_rest[:], in_=w2_dram[:, W2_FIRST:H])
+        w1_raw[1] = load_w1(1)
         nc.sync.dma_start(list3[:], offs3)
         nc.sync.dma_start(list4[:], offs4)
 
@@ -142,10 +143,10 @@ def tile_list_strata_contacts_kernel(
 
         def quantize_w1(i):
             shape = [P, 4 * W1_WIDTHS[i]]
-            if i < 2:
+            if i == 0:
                 grouped = held(f"w1_grouped{i}", shape, BF16)
             else:
-                grouped = placed(f"w1_grouped{i}", shape, BF16, LARGER + 2048 * (i - 2))
+                grouped = placed(f"w1_grouped{i}", shape, BF16, LARGER + 2048 * i)
             round_rows(w1_raw[i], grouped, False, True)
             cols = slice(w1_starts[i], w1_starts[i] + W1_WIDTHS[i])
             nc.vector.quantize_mx(out=minus_w1_c[:, cols].bitcast(FP8X4), scales=minus_w1_s[:, cols], in_=grouped[:])
@@ -158,9 +159,8 @@ def tile_list_strata_contacts_kernel(
         nc.vector.tensor_copy(out=v_w[0][:], in_=tab_w[:].bitcast(U32).indirect(list1[:, 0:32]))
         nc.vector.tensor_copy(out=v_w[1][:], in_=tab_w[:].bitcast(U32).indirect(list1[:, 32:64]))
 
-        quantize_w1(1)
+        w1_raw[2] = load_w1(2)
         w1_raw[3] = load_w1(3)
-        w1_raw[4] = load_w1(4)
         hiatus_rows = [held(f"hiatus_rows{b}", [P, M], F32) for b in range(4)]
         for b in range(4):
             nc.sync.dma_start(out=hiatus_rows[b][:], in_=hiatus[P * b : P * (b + 1), :])
@@ -180,13 +180,17 @@ def tile_list_strata_contacts_kernel(
         raw["w6", 1] = load_rows(w6[512:1024, :], placed("w6_raw1", [P, 4, N], F32, STAGE + 8192))
         raw["w4", 0] = load_rows(w4[0:512, :], placed("w4_raw0", [P, 4, N], F32, STAGE + 2 * 8192))
 
-        def product(tag, names, chunks, r0, width):
+        def weights(name, r0, width):
             cols = slice(r0, r0 + width)
-            moving = {
-                "minus_w1": (minus_w1_c[:, cols].bitcast(FP8X4), minus_w1_s[:, cols]),
-                "w2": (w2_w[:, cols].bitcast(FP8X4), w2_s[:, cols]),
-                "w3": (w3_w[:, 2 * r0 : 2 * (r0 + width)].bitcast(FP4X4), w3_s[:, cols]),
-            }
+            if name == "minus_w1":
+                return minus_w1_c[:, cols].bitcast(FP8X4), minus_w1_s[:, cols]
+            if name == "w3":
+                return w3_w[:, 2 * r0 : 2 * (r0 + width)].bitcast(FP4X4), w3_s[:, cols]
+            words = w2_first[:, cols] if r0 < W2_FIRST else w2_rest[:, r0 - W2_FIRST : r0 - W2_FIRST + width]
+            return words.bitcast(FP8X4), w2_s[:, cols]
+
+        def product(tag, names, chunks, r0, width):
+            moving = {name: weights(name, r0, width) for name in names}
             acc = bank(tag)
             for x, chunk in enumerate(chunks):
                 hf, c = divmod(chunk, 4)
@@ -210,23 +214,40 @@ def tile_list_strata_contacts_kernel(
 
         larger, minus_d3, h_lower = {}, {}, {}
 
-        def lower_product(u, tag, name):
+        def lower_product(u, tag, names):
             b, hf = divmod(u, 2)
-            return product(tag, (name,), range(4 * hf, 4 * hf + 4), P * b, P)
+            return product(tag, names, range(4 * hf, 4 * hf + 4), P * b, P)
+
+        def first_unit():
+            d = {}
+            for name, tag in (("minus_w1", "d2"), ("w2", "d1"), ("w3", "d3")):
+                codes, scales = weights(name, 0, P)
+                d[name] = bank(tag)
+                nc.tensor.matmul_mx(
+                    out=d[name][:], lhsT=codes, lhsT_scale=scales,
+                    rhs=v_w[0][:].bitcast(FP8X4), rhs_scale=v_s[0][:], start=True, stop=True,
+                )
+            d1_sb = placed("first_d1", [P, 512], F32, TAB_SCALES + 2 * N)
+            nc.scalar.activation(out=d1_sb[:], in_=d["minus_w1"][:], func=ACT.Copy, scale=-1.0)
+            first_larger = placed("first_larger", [P, 512], F32, TERMS)
+            nc.vector.tensor_tensor(out=first_larger[:], in0=d["w2"][:], in1=d1_sb[:], op=ALU.max)
+            h_lower[0] = ring.tile([P, HALF], F32, name="h_lower_sb")
+            nc.vector.tensor_tensor(out=h_lower[0][:], in0=first_larger[:], in1=d["w3"][:], op=ALU.subtract)
 
         def lower_larger(u):
-            minus_d1 = lower_product(u, "d1", "minus_w1")
-            d2 = lower_product(u, "d2", "w2")
-            if u == 0:
-                d1_sb = placed("first_d1", [P, 512], F32, TAB_SCALES + 2 * N)
-            else:
-                d1_sb = pair.tile([P, 512], F32, name="d1_sb")
-            nc.scalar.activation(out=d1_sb[:], in_=minus_d1[:], func=ACT.Copy, scale=-1.0)
             larger[u] = placed(f"larger{u}", [P, 512], F32, LARGER + 2048 * u)
+            if u == 1:
+                acc = lower_product(u, "d2", ("w2", "minus_w1"))
+                nc.scalar.activation(out=larger[u][:], in_=acc[:], func=ACT.Relu)
+                return
+            minus_d1 = lower_product(u, "d1", ("minus_w1",))
+            d2 = lower_product(u, "d2", ("w2",))
+            d1_sb = pair.tile([P, 512], F32, name="d1_sb")
+            nc.scalar.activation(out=d1_sb[:], in_=minus_d1[:], func=ACT.Copy, scale=-1.0)
             nc.vector.tensor_tensor(out=larger[u][:], in0=d2[:], in1=d1_sb[:], op=ALU.max)
 
         def lower_minus_d3(u):
-            d3 = lower_product(u, "d3", "w3")
+            d3 = lower_product(u, "d1", ("w3", "minus_w1")) if u == 1 else lower_product(u, "d3", ("w3",))
             minus_d3[u] = placed(f"minus_d3_{u}", [P, 512], F32, TERMS + 2048 * u)
             nc.scalar.activation(out=minus_d3[u][:], in_=d3[:], func=ACT.Copy, scale=-1.0)
 
@@ -259,7 +280,7 @@ def tile_list_strata_contacts_kernel(
 
         def upper_first(c):
             first_term[c] = ring.tile([P, 512], F32, name="first_term")
-            if c == 0:
+            if c % 4 == 0:
                 minus_d1 = product("first", ("minus_w1",), (c,), 512, 512)
                 d2 = product("spare", ("w2",), (c,), 512, 512)
                 d1_sb = pair.tile([P, 512], F32, name="d1_sb")
@@ -270,7 +291,7 @@ def tile_list_strata_contacts_kernel(
                 nc.scalar.activation(out=by_t(first_term[c]), in_=dealt(acc), func=ACT.Relu)
 
         def upper_second(c):
-            acc = product("second", ("w3",) if c == 0 else ("w3", "minus_w1"), (c,), 512, 512)
+            acc = product("second", ("w3",) if c % 4 == 0 else ("w3", "minus_w1"), (c,), 512, 512)
             second_term[c] = ring.tile([P, 512], F32, name="second_term")
             nc.scalar.activation(out=by_t(second_term[c]), in_=dealt(acc), func=ACT.Copy, scale=-1.0)
 
@@ -291,27 +312,19 @@ def tile_list_strata_contacts_kernel(
         below, z_lower = {}, {}
 
         def lower_below(b):
-            below[b] = placed(f"below{b}", [P, M], F32, TERMS + 2048 * ((2 * b + 2) % 8))
+            below[b] = placed(f"below{b}", [P, M], F32, TERMS + 2048 * (2 * b + 2) if b < 3 else TAB_SCALES)
             fetch_minus(b, list4, 0, M, hiatus_rows[b][:], below[b][:])
 
         def lower_z(b):
-            z_lower[b] = placed(f"z_lower{b}", [P, M], F32, TERMS + 2048 * ((2 * b + 3) % 8))
+            z_lower[b] = placed(f"z_lower{b}", [P, M], F32, TERMS + 2048 * (2 * b + 3) if b < 3 else TAB_SCALES + 2048)
             fetch_minus(b, list3, 0, M, below[b][:], z_lower[b][:])
 
-        lower_larger(0)
-        lower_minus_d3(0)
-        w5_wd = placed("w5_dealt_words", [P, 2, 2 * N], U8, TAB_SCALES)
-        nc.vector.tensor_copy(
-            out=w5_wd[:].bitcast(U16).rearrange("p a (t m) -> p a t m", t=4),
-            in_=w5_w[:].bitcast(U16).rearrange("p a (m t) -> p a t m", t=4),
-        )
-        w5_sd = placed("w5_dealt_scales", [P, 2, N], U8, TAB_SCALES + 4 * N)
-        nc.vector.tensor_copy(
-            out=w5_sd[:].rearrange("p a (t m) -> p a t m", t=4),
-            in_=w5_s[:].rearrange("p a (m t) -> p a t m", t=4),
-        )
+        first_unit()
+        lower_larger(1)
+        lower_minus_d3(1)
         done = 0
-        for u in range(8):
+        put_in_page(0, 0, h_lower[0][:], wgs_sb)
+        for u in range(1, 8):
             if u + 1 < 8:
                 lower_larger(u + 1)
             if u >= FIRST_DEALT_STEP:
@@ -319,10 +332,21 @@ def tile_list_strata_contacts_kernel(
                     work(c)
                 done = done + DEALT_READS_PER_STEP
             lower_turn(u)
+            if u == 1:
+                w5_wd = placed("w5_dealt_words", [P, 2, 2 * N], U8, TERMS + 1024)
+                nc.vector.tensor_copy(
+                    out=w5_wd[:].bitcast(U16).rearrange("p a (t m) -> p a t m", t=4),
+                    in_=w5_w[:].bitcast(U16).rearrange("p a (m t) -> p a t m", t=4),
+                )
+                w5_sd = placed("w5_dealt_scales", [P, 2, N], U8, TERMS + 3072)
+                nc.vector.tensor_copy(
+                    out=w5_sd[:].rearrange("p a (t m) -> p a t m", t=4),
+                    in_=w5_s[:].rearrange("p a (m t) -> p a t m", t=4),
+                )
             if u + 1 < 8:
                 lower_minus_d3(u + 1)
-            if u < 3:
-                quantize_w1(u + 2)
+            if u < 4:
+                quantize_w1(u)
             if u >= 2 and u % 2 == 0:
                 lower_below(u // 2 - 1)
             if u >= 3 and u % 2 == 1:

@@ -23,14 +23,14 @@ W1_WIDTHS = (256, 256, 256, 256)
 W2_FIRST = 256
 GPSIMD_CLEARS = 576
 ROUND_GROUPS = 32
-DEALT_READS_PER_STEP = 5
-FIRST_DEALT_STEP = 5
 
 TAB_LOW, TAB_HIGH, TAB_SCALES = 0, 8192, 16384
 STAGE = 20480
 TERMS = STAGE + 3 * 8192
 Z_UPPER = TERMS + 8 * 2048
 LARGER = Z_UPPER + 4 * 2048
+EARLY_D1 = LARGER + 8 * 2048
+W1_EARLY = EARLY_D1 + 2 * 2048
 
 
 def tile_list_strata_contacts_kernel(
@@ -88,7 +88,7 @@ def tile_list_strata_contacts_kernel(
 
         def load_w1(i):
             shape = [P, 4, W1_WIDTHS[i]]
-            raw = placed(f"w1_raw{i}", shape, F32, TAB_LOW + 4096 * (i - 2)) if i >= 2 else held(f"w1_raw{i}", shape, F32)
+            raw = placed(f"w1_raw{i}", shape, F32, TAB_LOW + 4096 * (i - 2) if i >= 2 else W1_EARLY + 4096 * i)
             return load_rows(w1[:, w1_starts[i] : w1_starts[i] + W1_WIDTHS[i]], raw)
 
         tab_w_dram = tab_words[0].rearrange("p t i -> p (t i)").bitcast(I32)
@@ -108,11 +108,11 @@ def tile_list_strata_contacts_kernel(
         load_scale_rows(nc.sync, w2_s, w2_scales[0])
         nc.sync.dma_start(list2[:], offs2)
         nc.sync.dma_start(out=wgs_sb[:, 0:HALF], in_=wgs[:, 0:HALF])
+        w1_raw[1] = load_w1(1)
         nc.sync.dma_start(out=w5_w[:].bitcast(I32), in_=w5_words.rearrange("a p c -> p a c").bitcast(I32))
         load_scale_rows(nc.sync, w5_s, w5_scales.rearrange("a q c -> q a c"))
         nc.sync.dma_start(out=wgs_sb[:, HALF:S], in_=wgs[:, HALF:S])
         nc.sync.dma_start(out=w2_rest[:], in_=w2_dram[:, W2_FIRST:H])
-        w1_raw[1] = load_w1(1)
         nc.sync.dma_start(list3[:], offs3)
         nc.sync.dma_start(list4[:], offs4)
 
@@ -146,7 +146,7 @@ def tile_list_strata_contacts_kernel(
             if i == 0:
                 grouped = held(f"w1_grouped{i}", shape, BF16)
             else:
-                grouped = placed(f"w1_grouped{i}", shape, BF16, LARGER + 2048 * i)
+                grouped = placed(f"w1_grouped{i}", shape, BF16, (TAB_SCALES + 2 * N, LARGER + 4096, TERMS + 4096)[i - 1])
             round_rows(w1_raw[i], grouped, False, True)
             cols = slice(w1_starts[i], w1_starts[i] + W1_WIDTHS[i])
             nc.vector.quantize_mx(out=minus_w1_c[:, cols].bitcast(FP8X4), scales=minus_w1_s[:, cols], in_=grouped[:])
@@ -220,7 +220,7 @@ def tile_list_strata_contacts_kernel(
 
         def first_unit():
             d = {}
-            for name, tag in (("minus_w1", "d2"), ("w2", "d1"), ("w3", "d3")):
+            for name, tag in (("minus_w1", "spare"), ("w2", "d1"), ("w3", "d3")):
                 codes, scales = weights(name, 0, P)
                 d[name] = bank(tag)
                 nc.tensor.matmul_mx(
@@ -236,18 +236,17 @@ def tile_list_strata_contacts_kernel(
 
         def lower_larger(u):
             larger[u] = placed(f"larger{u}", [P, 512], F32, LARGER + 2048 * u)
-            if u == 1:
-                acc = lower_product(u, "d2", ("w2", "minus_w1"))
-                nc.scalar.activation(out=larger[u][:], in_=acc[:], func=ACT.Relu)
-                return
             minus_d1 = lower_product(u, "d1", ("minus_w1",))
-            d2 = lower_product(u, "d2", ("w2",))
-            d1_sb = pair.tile([P, 512], F32, name="d1_sb")
+            d2 = lower_product(u, ("d2", "spare")[u % 2], ("w2",))
+            if u < 3:
+                d1_sb = placed(f"early_d1_{u}", [P, 512], F32, EARLY_D1 + 2048 * (u - 1))
+            else:
+                d1_sb = pair.tile([P, 512], F32, name="d1_sb")
             nc.scalar.activation(out=d1_sb[:], in_=minus_d1[:], func=ACT.Copy, scale=-1.0)
             nc.vector.tensor_tensor(out=larger[u][:], in0=d2[:], in1=d1_sb[:], op=ALU.max)
 
         def lower_minus_d3(u):
-            d3 = lower_product(u, "d1", ("w3", "minus_w1")) if u == 1 else lower_product(u, "d3", ("w3",))
+            d3 = lower_product(u, "d3", ("w3",))
             minus_d3[u] = placed(f"minus_d3_{u}", [P, 512], F32, TERMS + 2048 * u)
             nc.scalar.activation(out=minus_d3[u][:], in_=d3[:], func=ACT.Copy, scale=-1.0)
 
@@ -257,10 +256,10 @@ def tile_list_strata_contacts_kernel(
             h_lower[u] = ring.tile([P, HALF], F32, name="h_lower_sb")
             nc.scalar.copy(out=h_lower[u][:], in_=h_ps[:])
 
-        def put_in_page(slab, hf, values, weights):
+        def put_in_page(slab, j0, width, values, weights):
             nc.vector.tensor_tensor(
-                out=pages[slab % 2][:].indirect(list2[:, 32 * hf : 32 * (hf + 1)]),
-                in0=values, in1=weights[:, HALF * hf : HALF * (hf + 1)], op=ALU.mult,
+                out=pages[slab % 2][:].indirect(list2[:, j0 // 16 : (j0 + width) // 16]),
+                in0=values, in1=weights[:, j0 : j0 + width], op=ALU.mult,
             )
 
         def fetch_minus(slab, columns, m0, width, other, out):
@@ -269,7 +268,7 @@ def tile_list_strata_contacts_kernel(
                 in1=other, op=ALU.subtract,
             )
 
-        h_upper = [held(f"h_upper{hf}", [P, 4, HALF], F32) for hf in range(2)]
+        h_upper = held("h_upper", [P, 4, S], F32)
         first_term, second_term = {}, {}
 
         def dealt(acc):
@@ -279,10 +278,13 @@ def tile_list_strata_contacts_kernel(
             return tile[:].rearrange("j (t p) -> j t p", t=4)
 
         def upper_first(c):
-            first_term[c] = ring.tile([P, 512], F32, name="first_term")
-            if c % 4 == 0:
+            if c < 4:
+                first_term[c] = placed(f"first_term{c}", [P, 512], F32, LARGER + 2048 * (c + 4))
+            else:
+                first_term[c] = ring.tile([P, 512], F32, name="first_term")
+            if c == 0:
                 minus_d1 = product("first", ("minus_w1",), (c,), 512, 512)
-                d2 = product("spare", ("w2",), (c,), 512, 512)
+                d2 = product("second", ("w2",), (c,), 512, 512)
                 d1_sb = pair.tile([P, 512], F32, name="d1_sb")
                 nc.scalar.activation(out=by_t(d1_sb), in_=dealt(minus_d1), func=ACT.Copy, scale=-1.0)
                 nc.vector.tensor_tensor(out=by_t(first_term[c]), in0=dealt(d2), in1=by_t(d1_sb), op=ALU.max)
@@ -291,81 +293,86 @@ def tile_list_strata_contacts_kernel(
                 nc.scalar.activation(out=by_t(first_term[c]), in_=dealt(acc), func=ACT.Relu)
 
         def upper_second(c):
-            acc = product("second", ("w3",) if c % 4 == 0 else ("w3", "minus_w1"), (c,), 512, 512)
+            acc = product("first", ("w3",), (c,), 512, 512) if c == 0 else product("second", ("w3", "minus_w1"), (c,), 512, 512)
             second_term[c] = ring.tile([P, 512], F32, name="second_term")
             nc.scalar.activation(out=by_t(second_term[c]), in_=dealt(acc), func=ACT.Copy, scale=-1.0)
 
         def upper_turn(c):
             h_ps = bank("h_upper")
             transposed_sum(h_ps, (second_term[c], first_term[c]))
-            hf, x = divmod(c, 4)
-            nc.scalar.copy(out=h_upper[hf][:, :, P * x : P * (x + 1)], in_=h_ps[:].rearrange("p (t j) -> p t j", t=4))
+            nc.scalar.copy(out=h_upper[:, :, P * c : P * (c + 1)], in_=h_ps[:].rearrange("p (t j) -> p t j", t=4))
 
-        upper_work = []
-        for c in range(8 + 2):
+        def upper_step(c):
             if c < 8:
-                upper_work.append((upper_first, c))
-                upper_work.append((upper_second, c))
-            if c >= 2:
-                upper_work.append((upper_turn, c - 2))
+                upper_first(c)
+                upper_second(c)
+            if c >= 1:
+                upper_turn(c - 1)
 
         below, z_lower = {}, {}
 
         def lower_below(b):
-            below[b] = placed(f"below{b}", [P, M], F32, TERMS + 2048 * (2 * b + 2) if b < 3 else TAB_SCALES)
+            below[b] = placed(f"below{b}", [P, M], F32, TERMS + 2048 * ((2 * b + 3) % 8))
             fetch_minus(b, list4, 0, M, hiatus_rows[b][:], below[b][:])
 
         def lower_z(b):
-            z_lower[b] = placed(f"z_lower{b}", [P, M], F32, TERMS + 2048 * (2 * b + 3) if b < 3 else TAB_SCALES + 2048)
+            z_lower[b] = placed(f"z_lower{b}", [P, M], F32, TERMS + 2048 * (2 * b + 4 if b < 2 else 2 * b - 4))
             fetch_minus(b, list3, 0, M, below[b][:], z_lower[b][:])
 
+        w5_wd = placed("w5_dealt_words", [P, 2, 2 * N], U8, EARLY_D1)
+        w5_sd = placed("w5_dealt_scales", [P, 2, N], U8, EARLY_D1 + 2048)
         first_unit()
         lower_larger(1)
         lower_minus_d3(1)
-        done = 0
-        put_in_page(0, 0, h_lower[0][:], wgs_sb)
-        for u in range(1, 8):
-            if u + 1 < 8:
-                lower_larger(u + 1)
-            if u >= FIRST_DEALT_STEP:
-                for work, c in upper_work[done : done + DEALT_READS_PER_STEP]:
-                    work(c)
-                done = done + DEALT_READS_PER_STEP
+        quantize_w1(1)
+        put_in_page(0, 0, HALF, h_lower[0][:], wgs_sb)
+        nc.vector.tensor_copy(
+            out=w5_wd[:].bitcast(U16).rearrange("p a (t m) -> p a t m", t=4),
+            in_=w5_w[:].bitcast(U16).rearrange("p a (m t) -> p a t m", t=4),
+        )
+        lower_larger(2)
+        nc.vector.tensor_copy(
+            out=w5_sd[:].rearrange("p a (t m) -> p a t m", t=4),
+            in_=w5_s[:].rearrange("p a (m t) -> p a t m", t=4),
+        )
+        lower_larger(3)
+        lower_turn(1)
+        put_in_page(0, HALF, HALF, h_lower[1][:], wgs_sb)
+        lower_minus_d3(2)
+        lower_minus_d3(3)
+        for u in range(2, 8):
+            if u + 2 < 8:
+                lower_larger(u + 2)
             lower_turn(u)
-            if u == 1:
-                w5_wd = placed("w5_dealt_words", [P, 2, 2 * N], U8, TERMS + 1024)
-                nc.vector.tensor_copy(
-                    out=w5_wd[:].bitcast(U16).rearrange("p a (t m) -> p a t m", t=4),
-                    in_=w5_w[:].bitcast(U16).rearrange("p a (m t) -> p a t m", t=4),
-                )
-                w5_sd = placed("w5_dealt_scales", [P, 2, N], U8, TERMS + 3072)
-                nc.vector.tensor_copy(
-                    out=w5_sd[:].rearrange("p a (t m) -> p a t m", t=4),
-                    in_=w5_s[:].rearrange("p a (m t) -> p a t m", t=4),
-                )
-            if u + 1 < 8:
-                lower_minus_d3(u + 1)
-            if u < 4:
-                quantize_w1(u)
-            if u >= 2 and u % 2 == 0:
-                lower_below(u // 2 - 1)
             if u >= 3 and u % 2 == 1:
-                lower_z((u - 3) // 2)
-            put_in_page(u // 2, u % 2, h_lower[u][:], wgs_sb)
-        for work, c in upper_work[done:]:
-            work(c)
+                lower_below((u - 3) // 2)
+            if u >= 4 and u % 2 == 0:
+                lower_z((u - 4) // 2)
+            put_in_page(u // 2, HALF * (u % 2), HALF, h_lower[u][:], wgs_sb)
+            if u == 2:
+                quantize_w1(2)
+                quantize_w1(3)
+            if u >= 4:
+                upper_step(u - 4)
+            if u + 2 < 8:
+                lower_minus_d3(u + 2)
+        lower_z(2)
+        for c in range(4, 9):
+            upper_step(c)
+        for t in (1, 2):
+            wgs_dealt[t] = load_dealt_wgs(t, placed(f"wgs_dealt{t}", [P, S], F32, W1_EARLY + 4096 * (t - 1)))
         raw["w4", 1] = load_rows(w4[512:1024, :], placed("w4_raw1", [P, 4, N], F32, TAB_LOW))
 
         quant = {}
 
         def late_grouped():
-            slot = 3 - len(quant) % 3
-            return placed(f"grouped{len(quant)}", [P, 4 * 512], BF16, LARGER + 4096 * slot)
+            places = (LARGER + 3 * 4096, TAB_HIGH, LARGER + 2 * 4096, LARGER + 4096, STAGE, STAGE + 4096, STAGE + 8192)
+            return placed(f"grouped{len(quant)}", [P, 4 * 512], BF16, places[len(quant)])
 
         def stage2_operand(name, a):
             quant[name, a] = quantize(round_rows(raw[name, a], late_grouped(), name != "g"), f"{name}{a}")
 
-        z_pairs = [held(f"z_pairs{hf}", [P, 2, 2, 2 * P], BF16) for hf in range(2)]
+        z_pairs = [placed(f"z_pairs{hf}", [P, 2, 2, 2 * P], BF16, LARGER + 4096 + 2048 * hf) for hf in range(2)]
 
         def turn_z_lower(b):
             z_ps = bank("h_lower")
@@ -401,34 +408,32 @@ def tile_list_strata_contacts_kernel(
         def upper_z(t, q):
             fetch_minus(4 + t, list3, P * q, P, upper_below[t][:, P * q : P * (q + 1)], z_upper[q][:, t, :])
 
-        for t in range(4):
-            if t == 1:
-                stage2_operand("g", 0)
-                wgs_dealt[1] = load_dealt_wgs(1, placed("wgs_dealt1", [P, S], F32, TAB_HIGH))
-                stage2_operand("g", 1)
-            if t == 2:
-                for b in range(3):
-                    turn_z_lower(b)
-                stage2_operand("w6", 0)
-                stage2_operand("w6", 1)
-                wgs_dealt[2] = load_dealt_wgs(2, placed("wgs_dealt2", [P, S], F32, STAGE + 8192))
-            if t == 3:
-                turn_z_lower(3)
-                quantize_z_lower()
-                stage2_operand("w4", 0)
-                stage2_operand("w4", 1)
-                wgs_dealt[3] = load_dealt_wgs(3, placed("wgs_dealt3", [P, S], F32, TAB_LOW))
-            put_in_page(4 + t, 0, h_upper[0][:, t, :], wgs_dealt[t])
+        for t in range(3):
+            put_in_page(4 + t, 0, HALF, h_upper[:, t, 0:HALF], wgs_dealt[t])
             if t == 0:
                 lower_below(3)
             else:
                 upper_fetch_below(t - 1)
-            put_in_page(4 + t, 1, h_upper[1][:, t, :], wgs_dealt[t])
+            put_in_page(4 + t, HALF, HALF, h_upper[:, t, HALF:S], wgs_dealt[t])
             if t == 0:
                 lower_z(3)
-            elif t < 3:
+            else:
                 for q in range(4):
                     upper_z(t - 1, q)
+        upper_fetch_below(2)
+        for q in range(4):
+            upper_z(2, q)
+        stage2_operand("g", 0)
+        stage2_operand("g", 1)
+        for b in range(4):
+            turn_z_lower(b)
+        quantize_z_lower()
+        stage2_operand("w6", 0)
+        stage2_operand("w6", 1)
+        stage2_operand("w4", 0)
+        stage2_operand("w4", 1)
+        wgs_dealt[3] = load_dealt_wgs(3, placed("wgs_dealt3", [P, S], F32, TAB_LOW))
+        put_in_page(7, 0, S, h_upper[:, 3, :], wgs_dealt[3])
 
         def mx_passes(acc, name, a, q, start, stop):
             for t in range(4):
@@ -460,28 +465,18 @@ def tile_list_strata_contacts_kernel(
         last_below = {}
 
         def last_fetch_below(q):
-            if q < 2:
-                last_below[q] = pair.tile([P, P], F32, name="last_below")
-            else:
-                last_below[q] = placed(f"last_below{q}", [P, P], F32, Z_UPPER + 2048 * (q - 2))
+            last_below[q] = held(f"last_below{q}", [P, P], F32)
             fetch_minus(7, list4, P * q, P, raw["g", 1][:, 3, P * q : P * (q + 1)], last_below[q][:])
 
         def last_z(q):
             fetch_minus(7, list3, P * q, P, last_below[q][:], z_upper[q][:, 3, :])
             quant["z", 1, q] = quantize(round_rows(z_upper[q], held(f"z_grouped{q}", [P, 4 * P], BF16), False), f"z1{q}")
 
-        upper_z(2, 0)
         last_fetch_below(0)
-        upper_z(2, 1)
-        last_z(0)
-        last_fetch_below(1)
-        upper_z(2, 2)
-        last_z(1)
-        last_fetch_below(2)
-        upper_z(2, 3)
-        last_z(2)
-        last_fetch_below(3)
-        last_z(3)
+        for q in range(4):
+            if q < 3:
+                last_fetch_below(q + 1)
+            last_z(q)
 
         out_rows = out_0.rearrange("(p t) m -> p t m", t=4)
         out_words = out_1[0].rearrange("p m t -> p (m t)").bitcast(I32)
@@ -491,7 +486,7 @@ def tile_list_strata_contacts_kernel(
             cols = slice(P * q, P * (q + 1))
             mx_passes(gates[q], "w4", 1, q, False, True)
             mx_passes(sums[q], "w5", 1, q, False, True)
-            gate = pair.tile([P, 512], F32, name="gate")
+            gate = placed(f"gate{q}", [P, 512], F32, TERMS + 2048 * q)
             nc.scalar.activation(out=gate[:], in_=gates[q][:], func=ACT.Tanh)
             y = placed(f"y{q}", [P, 4, P], F32, STAGE + 2048 * q)
             nc.vector.tensor_tensor(out=y[:].rearrange("p t m -> p (t m)"), in0=sums[q][:], in1=gate[:], op=ALU.mult)

@@ -20,6 +20,7 @@ ACT = mybir.ActivationFunctionType
 P = 128
 HALF = 512
 W1_WIDTHS = (256, 256, 256, 256)
+FIRST_PARTS = (slice(0, 256), slice(256, 512))
 W2_FIRST = 256
 GPSIMD_CLEARS = 576
 ROUND_GROUPS = 32
@@ -133,7 +134,10 @@ def tile_list_strata_contacts_kernel(
 
         def quantize(grouped, name):
             width = grouped.shape[1] // 4
-            codes = held(name + "_c", [P, width], U32)
+            if name in ("g0", "g1"):
+                codes = placed(name + "_c", [P, width], U32, LARGER + 4096 + 1024 if name == "g0" else TAB_LOW)
+            else:
+                codes = held(name + "_c", [P, width], U32)
             scales = held(name + "_s", [P, width], U8)
             nc.vector.quantize_mx(out=codes[:].bitcast(FP8X4), scales=scales[:], in_=grouped[:])
             return codes, scales
@@ -228,11 +232,13 @@ def tile_list_strata_contacts_kernel(
                     rhs=v_w[0][:].bitcast(FP8X4), rhs_scale=v_s[0][:], start=True, stop=True,
                 )
             d1_sb = placed("first_d1", [P, 512], F32, TAB_SCALES + 2 * N)
-            nc.scalar.activation(out=d1_sb[:], in_=d["minus_w1"][:], func=ACT.Copy, scale=-1.0)
             first_larger = placed("first_larger", [P, 512], F32, TERMS)
-            nc.vector.tensor_tensor(out=first_larger[:], in0=d["w2"][:], in1=d1_sb[:], op=ALU.max)
             h_lower[0] = ring.tile([P, HALF], F32, name="h_lower_sb")
-            nc.vector.tensor_tensor(out=h_lower[0][:], in0=first_larger[:], in1=d["w3"][:], op=ALU.subtract)
+            for cols in FIRST_PARTS:
+                nc.scalar.activation(out=d1_sb[:, cols], in_=d["minus_w1"][:, cols], func=ACT.Copy, scale=-1.0)
+                nc.vector.tensor_tensor(out=first_larger[:, cols], in0=d["w2"][:, cols], in1=d1_sb[:, cols], op=ALU.max)
+            for cols in FIRST_PARTS:
+                nc.vector.tensor_tensor(out=h_lower[0][:, cols], in0=first_larger[:, cols], in1=d["w3"][:, cols], op=ALU.subtract)
 
         def lower_larger(u):
             larger[u] = placed(f"larger{u}", [P, 512], F32, LARGER + 2048 * u)
@@ -364,10 +370,12 @@ def tile_list_strata_contacts_kernel(
         raw["w4", 1] = load_rows(w4[512:1024, :], placed("w4_raw1", [P, 4, N], F32, TAB_LOW))
 
         quant = {}
+        rounded = []
 
         def late_grouped():
-            places = (LARGER + 3 * 4096, TAB_HIGH, LARGER + 2 * 4096, LARGER + 4096, STAGE, STAGE + 4096, STAGE + 8192)
-            return placed(f"grouped{len(quant)}", [P, 4 * 512], BF16, places[len(quant)])
+            places = (LARGER + 3 * 4096, TAB_HIGH, LARGER + 2 * 4096, TAB_HIGH + 4096, STAGE, STAGE + 4096, STAGE + 8192)
+            rounded.append(placed(f"grouped{len(rounded)}", [P, 4 * 512], BF16, places[len(rounded)]))
+            return rounded[-1]
 
         def stage2_operand(name, a):
             quant[name, a] = quantize(round_rows(raw[name, a], late_grouped(), name != "g"), f"{name}{a}")
@@ -396,17 +404,20 @@ def tile_list_strata_contacts_kernel(
                     out=grouped[:, 1024 * hf : 1024 * (hf + 1)].bitcast(F32).rearrange("p (c m u) -> p c m u", c=2, u=2),
                     in_=back[:].rearrange("p (c u m) -> p c m u", c=2, u=2),
                 )
+            quant["g", 0] = quantize(g_grouped, "g0")
             quant["z", 0] = quantize(grouped, "z0")
 
-        z_upper = [placed(f"z_upper{q}", [P, 4, P], F32, Z_UPPER + 2048 * q) for q in range(4)]
+        z_front = placed("z_front", [P, 2, M], F32, Z_UPPER)
+        z_back = {}
         upper_below = {}
 
         def upper_fetch_below(t):
             upper_below[t] = pair.tile([P, M], F32, name="upper_below")
             fetch_minus(4 + t, list4, 0, M, raw["g", 1][:, t, :], upper_below[t][:])
 
-        def upper_z(t, q):
-            fetch_minus(4 + t, list3, P * q, P, upper_below[t][:, P * q : P * (q + 1)], z_upper[q][:, t, :])
+        def third_z(q):
+            z_back[q] = placed(f"z_back{q}", [P, 2, P], F32, Z_UPPER + 4096 + 1024 * q if q < 2 else TAB_LOW + 1024 * q)
+            fetch_minus(6, list3, P * q, P, upper_below[2][:, P * q : P * (q + 1)], z_back[q][:, 0, :])
 
         for t in range(3):
             put_in_page(4 + t, 0, HALF, h_upper[:, t, 0:HALF], wgs_dealt[t])
@@ -418,22 +429,31 @@ def tile_list_strata_contacts_kernel(
             if t == 0:
                 lower_z(3)
             else:
-                for q in range(4):
-                    upper_z(t - 1, q)
+                fetch_minus(3 + t, list3, 0, M, upper_below[t - 1][:], z_front[:, t - 1, :])
         upper_fetch_below(2)
-        for q in range(4):
-            upper_z(2, q)
-        stage2_operand("g", 0)
-        stage2_operand("g", 1)
+        third_z(0)
+        third_z(1)
+        g_grouped = round_rows(raw["g", 0], late_grouped(), False)
+        stage2_operand("w6", 0)
         for b in range(4):
             turn_z_lower(b)
         quantize_z_lower()
-        stage2_operand("w6", 0)
+        g_grouped = round_rows(raw["g", 1], late_grouped(), False)
         stage2_operand("w6", 1)
         stage2_operand("w4", 0)
         stage2_operand("w4", 1)
         wgs_dealt[3] = load_dealt_wgs(3, placed("wgs_dealt3", [P, S], F32, TAB_LOW))
         put_in_page(7, 0, S, h_upper[:, 3, :], wgs_dealt[3])
+        quant["g", 1] = quantize(g_grouped, "g1")
+
+        def round_pair(grouped, u, planes):
+            nc.scalar.copy(
+                out=grouped[:].rearrange("p (m u e) -> p u m e", u=2, e=2)[:, u], in_=planes.rearrange("p e m -> p m e")
+            )
+
+        z_grouped = [placed(f"z_grouped{q}", [P, 4 * P], BF16, TAB_LOW + 4096 + 1024 * q) for q in range(4)]
+        for q in range(4):
+            round_pair(z_grouped[q], 0, z_front[:, :, P * q : P * (q + 1)])
 
         def mx_passes(acc, name, a, q, start, stop):
             for t in range(4):
@@ -456,35 +476,45 @@ def tile_list_strata_contacts_kernel(
         for q, tag in enumerate(("d1", "d2", "d3", "first")):
             sums[q] = bank(tag)
             mx_passes(sums[q], "w6", 0, q, True, False)
-            mx_passes(sums[q], "w6", 1, q, False, False)
             mx_passes(sums[q], "w5", 0, q, False, False)
         for q, tag in enumerate(("second", "spare", "h_lower", "h_upper")):
             gates[q] = bank(tag)
             mx_passes(gates[q], "w4", 0, q, True, False)
+        for q in range(4):
+            mx_passes(sums[q], "w6", 1, q, False, False)
 
         last_below = {}
 
         def last_fetch_below(q):
-            last_below[q] = held(f"last_below{q}", [P, P], F32)
+            if q < 2:
+                last_below[q] = held(f"last_below{q}", [P, P], F32)
+            else:
+                last_below[q] = placed(f"last_below{q}", [P, P], F32, Z_UPPER + 4096 + 512 * (q - 2))
             fetch_minus(7, list4, P * q, P, raw["g", 1][:, 3, P * q : P * (q + 1)], last_below[q][:])
 
         def last_z(q):
-            fetch_minus(7, list3, P * q, P, last_below[q][:], z_upper[q][:, 3, :])
-            quant["z", 1, q] = quantize(round_rows(z_upper[q], held(f"z_grouped{q}", [P, 4 * P], BF16), False), f"z1{q}")
+            fetch_minus(7, list3, P * q, P, last_below[q][:], z_back[q][:, 1, :])
+            round_pair(z_grouped[q], 1, z_back[q][:])
+            quant["z", 1, q] = quantize(z_grouped[q], f"z1{q}")
 
-        last_fetch_below(0)
-        for q in range(4):
-            if q < 3:
-                last_fetch_below(q + 1)
+        for q in range(2):
+            last_fetch_below(q)
+            third_z(q + 2)
             last_z(q)
+        last_fetch_below(2)
+        last_fetch_below(3)
+        last_z(2)
+        last_z(3)
 
         out_rows = out_0.rearrange("(p t) m -> p t m", t=4)
         out_words = out_1[0].rearrange("p m t -> p (m t)").bitcast(I32)
         y_c = held("y_c", [P, M], U32)
         y_s = held("y_s", [P, M], U8)
+        mx_passes(gates[0], "w4", 1, 0, False, True)
         for q in range(4):
             cols = slice(P * q, P * (q + 1))
-            mx_passes(gates[q], "w4", 1, q, False, True)
+            if q < 3:
+                mx_passes(gates[q + 1], "w4", 1, q + 1, False, True)
             mx_passes(sums[q], "w5", 1, q, False, True)
             gate = placed(f"gate{q}", [P, 512], F32, TERMS + 2048 * q)
             nc.scalar.activation(out=gate[:], in_=gates[q][:], func=ACT.Tanh)

@@ -21,6 +21,7 @@ P = 128
 HALF = 512
 W1_WIDTHS = (256, 256, 256, 256)
 FIRST_PARTS = (slice(0, 256), slice(256, 512))
+RELU_FROM = 5
 W2_FIRST = 256
 GPSIMD_CLEARS = 576
 ROUND_GROUPS = 32
@@ -32,6 +33,8 @@ Z_UPPER = TERMS + 8 * 2048
 LARGER = Z_UPPER + 4 * 2048
 EARLY_D1 = LARGER + 8 * 2048
 W1_EARLY = EARLY_D1 + 2 * 2048
+THIRD_PAGE = W1_EARLY + 8192
+LAST_WGS = STAGE + 2 * 8192
 
 
 def tile_list_strata_contacts_kernel(
@@ -80,10 +83,9 @@ def tile_list_strata_contacts_kernel(
         nc.vector.memset(tab_s[:].bitcast(I32)[:, GPSIMD_CLEARS:], 0)
         nc.vector.memset(w3_s[:].bitcast(I32), 0)
         nc.vector.memset(w5_s[:].bitcast(I32), 0)
-        load_scale_rows(nc.gpsimd, w3_s, w3_scales[0])
         make_identity(nc, ident[:])
-        nc.vector.memset(pages[0][:], 0.0)
-        nc.vector.memset(pages[1][:], 0.0)
+        for page in pages:
+            nc.vector.memset(page[:], 0.0)
 
         w1_starts = [sum(W1_WIDTHS[:i]) for i in range(len(W1_WIDTHS))]
 
@@ -107,6 +109,7 @@ def tile_list_strata_contacts_kernel(
         nc.sync.dma_start(out=w2_first[:], in_=w2_dram[:, 0:W2_FIRST])
         nc.sync.dma_start(out=w3_w[:].bitcast(I32), in_=w3_words[0].bitcast(I32))
         load_scale_rows(nc.sync, w2_s, w2_scales[0])
+        load_scale_rows(nc.sync, w3_s, w3_scales[0])
         nc.sync.dma_start(list2[:], offs2)
         nc.sync.dma_start(out=wgs_sb[:, 0:HALF], in_=wgs[:, 0:HALF])
         w1_raw[1] = load_w1(1)
@@ -135,7 +138,7 @@ def tile_list_strata_contacts_kernel(
         def quantize(grouped, name):
             width = grouped.shape[1] // 4
             if name in ("g0", "g1"):
-                codes = placed(name + "_c", [P, width], U32, LARGER + 4096 + 1024 if name == "g0" else TAB_LOW)
+                codes = placed(name + "_c", [P, width], U32, LARGER + 4096 + 1024 if name == "g0" else LAST_WGS)
             else:
                 codes = held(name + "_c", [P, width], U32)
             scales = held(name + "_s", [P, width], U8)
@@ -150,7 +153,7 @@ def tile_list_strata_contacts_kernel(
             if i == 0:
                 grouped = held(f"w1_grouped{i}", shape, BF16)
             else:
-                grouped = placed(f"w1_grouped{i}", shape, BF16, (TAB_SCALES + 2 * N, LARGER + 4096, TERMS + 4096)[i - 1])
+                grouped = placed(f"w1_grouped{i}", shape, BF16, (TAB_SCALES + 2 * N, LARGER + 2048, TERMS + 2048)[i - 1])
             round_rows(w1_raw[i], grouped, False, True)
             cols = slice(w1_starts[i], w1_starts[i] + W1_WIDTHS[i])
             nc.vector.quantize_mx(out=minus_w1_c[:, cols].bitcast(FP8X4), scales=minus_w1_s[:, cols], in_=grouped[:])
@@ -232,8 +235,8 @@ def tile_list_strata_contacts_kernel(
                     rhs=v_w[0][:].bitcast(FP8X4), rhs_scale=v_s[0][:], start=True, stop=True,
                 )
             d1_sb = placed("first_d1", [P, 512], F32, TAB_SCALES + 2 * N)
-            first_larger = placed("first_larger", [P, 512], F32, TERMS)
-            h_lower[0] = ring.tile([P, HALF], F32, name="h_lower_sb")
+            first_larger = placed("first_larger", [P, 512], F32, THIRD_PAGE)
+            h_lower[0] = ring.tile([P, HALF], F32, name="h_lower_sb", bufs=4)
             for cols in FIRST_PARTS:
                 nc.scalar.activation(out=d1_sb[:, cols], in_=d["minus_w1"][:, cols], func=ACT.Copy, scale=-1.0)
                 nc.vector.tensor_tensor(out=first_larger[:, cols], in0=d["w2"][:, cols], in1=d1_sb[:, cols], op=ALU.max)
@@ -242,6 +245,10 @@ def tile_list_strata_contacts_kernel(
 
         def lower_larger(u):
             larger[u] = placed(f"larger{u}", [P, 512], F32, LARGER + 2048 * u)
+            if u >= RELU_FROM:
+                acc = lower_product(u, ("d2", "spare")[u % 2], ("w2", "minus_w1"))
+                nc.scalar.activation(out=larger[u][:], in_=acc[:], func=ACT.Relu)
+                return
             minus_d1 = lower_product(u, "d1", ("minus_w1",))
             d2 = lower_product(u, ("d2", "spare")[u % 2], ("w2",))
             if u < 3:
@@ -252,25 +259,25 @@ def tile_list_strata_contacts_kernel(
             nc.vector.tensor_tensor(out=larger[u][:], in0=d2[:], in1=d1_sb[:], op=ALU.max)
 
         def lower_minus_d3(u):
-            d3 = lower_product(u, "d3", ("w3",))
+            d3 = lower_product(u, "d3", ("w3", "minus_w1") if u >= RELU_FROM else ("w3",))
             minus_d3[u] = placed(f"minus_d3_{u}", [P, 512], F32, TERMS + 2048 * u)
             nc.scalar.activation(out=minus_d3[u][:], in_=d3[:], func=ACT.Copy, scale=-1.0)
 
         def lower_turn(u):
             h_ps = bank("h_lower")
             transposed_sum(h_ps, (minus_d3[u], larger[u]))
-            h_lower[u] = ring.tile([P, HALF], F32, name="h_lower_sb")
+            h_lower[u] = ring.tile([P, HALF], F32, name="h_lower_sb", bufs=4)
             nc.scalar.copy(out=h_lower[u][:], in_=h_ps[:])
 
         def put_in_page(slab, j0, width, values, weights):
             nc.vector.tensor_tensor(
-                out=pages[slab % 2][:].indirect(list2[:, j0 // 16 : (j0 + width) // 16]),
+                out=pages[slab % 3][:].indirect(list2[:, j0 // 16 : (j0 + width) // 16]),
                 in0=values, in1=weights[:, j0 : j0 + width], op=ALU.mult,
             )
 
         def fetch_minus(slab, columns, m0, width, other, out):
             nc.vector.tensor_tensor(
-                out=out, in0=pages[slab % 2][:].indirect(columns[:, m0 // 16 : (m0 + width) // 16]),
+                out=out, in0=pages[slab % 3][:].indirect(columns[:, m0 // 16 : (m0 + width) // 16]),
                 in1=other, op=ALU.subtract,
             )
 
@@ -284,28 +291,52 @@ def tile_list_strata_contacts_kernel(
             return tile[:].rearrange("j (t p) -> j t p", t=4)
 
         def upper_first(c):
-            if c < 4:
-                first_term[c] = placed(f"first_term{c}", [P, 512], F32, LARGER + 2048 * (c + 4))
-            else:
-                first_term[c] = ring.tile([P, 512], F32, name="first_term")
-            if c == 0:
-                minus_d1 = product("first", ("minus_w1",), (c,), 512, 512)
-                d2 = product("second", ("w2",), (c,), 512, 512)
-                d1_sb = pair.tile([P, 512], F32, name="d1_sb")
-                nc.scalar.activation(out=by_t(d1_sb), in_=dealt(minus_d1), func=ACT.Copy, scale=-1.0)
-                nc.vector.tensor_tensor(out=by_t(first_term[c]), in0=dealt(d2), in1=by_t(d1_sb), op=ALU.max)
-            else:
-                acc = product("first", ("w2", "minus_w1"), (c,), 512, 512)
-                nc.scalar.activation(out=by_t(first_term[c]), in_=dealt(acc), func=ACT.Relu)
+            first_term[c] = placed(f"first_term{c}", [P, 512], F32, LARGER + 2048 * (c % 2 + 3))
+            acc = product("first", ("w2", "minus_w1"), (c,), 512, 512)
+            nc.scalar.activation(out=by_t(first_term[c]), in_=dealt(acc), func=ACT.Relu)
 
         def upper_second(c):
-            acc = product("first", ("w3",), (c,), 512, 512) if c == 0 else product("second", ("w3", "minus_w1"), (c,), 512, 512)
+            acc = product("second", ("w3", "minus_w1"), (c,), 512, 512)
             second_term[c] = ring.tile([P, 512], F32, name="second_term")
             nc.scalar.activation(out=by_t(second_term[c]), in_=dealt(acc), func=ACT.Copy, scale=-1.0)
 
         def upper_turn(c):
             h_ps = bank("h_upper")
             transposed_sum(h_ps, (second_term[c], first_term[c]))
+            nc.scalar.copy(out=h_upper[:, :, P * c : P * (c + 1)], in_=h_ps[:].rearrange("p (t j) -> p t j", t=4))
+
+        turned = {}
+
+        def negated_products(c):
+            terms = (
+                placed(f"d1_upper{c}", [P, 512], F32, LARGER + 2048 * (c + 2)) if c < 6 else held(f"d1_upper{c}", [P, 512], F32),
+                pair.tile([P, 512], F32, name="d1_sb"),
+                ring.tile([P, 512], F32, name="second_term") if c < 7 else held("last_term", [P, 512], F32),
+            )
+            for term, name, tag in zip(terms, ("minus_w1", "w2", "w3"), ("first", "second", "h_lower")):
+                acc = product(tag, (name,), (c,), 512, 512)
+                nc.scalar.activation(out=by_t(term), in_=dealt(acc), func=ACT.Copy, scale=-1.0)
+            turned[c] = terms
+
+        def excess_turned(c):
+            d1, minus_d2, minus_d3_c = turned[c]
+            acc = bank(("d2", "spare")[c % 2])
+            transposed_sum(acc, (d1, minus_d2))
+            excess = placed(f"excess{c}", [P, 512], F32, TAB_SCALES + 2048 * (c % 2))
+            nc.scalar.activation(out=excess[:], in_=acc[:], func=ACT.Relu, scale=-1.0)
+            turned[c] = (d1, minus_d3_c, excess)
+
+        def excess_back(c):
+            d1, minus_d3_c, excess = turned[c]
+            acc = bank(("d3", "d1")[c % 2])
+            transposed_sum(acc, (excess,))
+            back = placed(f"excess_back{c}", [P, 512], F32, LARGER + 2048 * (c % 2))
+            nc.scalar.copy(out=back[:], in_=acc[:])
+            turned[c] = (d1, minus_d3_c, back)
+
+        def sum_turned(c):
+            h_ps = bank("h_upper")
+            transposed_sum(h_ps, turned[c])
             nc.scalar.copy(out=h_upper[:, :, P * c : P * (c + 1)], in_=h_ps[:].rearrange("p (t j) -> p t j", t=4))
 
         def upper_step(c):
@@ -328,6 +359,8 @@ def tile_list_strata_contacts_kernel(
         w5_wd = placed("w5_dealt_words", [P, 2, 2 * N], U8, EARLY_D1)
         w5_sd = placed("w5_dealt_scales", [P, 2, N], U8, EARLY_D1 + 2048)
         first_unit()
+        pages.append(placed("page2", [P, T2], F32, THIRD_PAGE))
+        nc.gpsimd.memset(pages[2][:], 0.0)
         lower_larger(1)
         lower_minus_d3(1)
         quantize_w1(1)
@@ -346,6 +379,8 @@ def tile_list_strata_contacts_kernel(
         put_in_page(0, HALF, HALF, h_lower[1][:], wgs_sb)
         lower_minus_d3(2)
         lower_minus_d3(3)
+        quantize_w1(2)
+        quantize_w1(3)
         for u in range(2, 8):
             if u + 2 < 8:
                 lower_larger(u + 2)
@@ -355,16 +390,16 @@ def tile_list_strata_contacts_kernel(
             if u >= 4 and u % 2 == 0:
                 lower_z((u - 4) // 2)
             put_in_page(u // 2, HALF * (u % 2), HALF, h_lower[u][:], wgs_sb)
-            if u == 2:
-                quantize_w1(2)
-                quantize_w1(3)
             if u >= 4:
                 upper_step(u - 4)
             if u + 2 < 8:
                 lower_minus_d3(u + 2)
         lower_z(2)
-        for c in range(4, 9):
-            upper_step(c)
+        upper_turn(3)
+        for chunks in ((4, 5), (6, 7)):
+            for stage in (negated_products, excess_turned, excess_back, sum_turned):
+                for c in chunks:
+                    stage(c)
         for t in (1, 2):
             wgs_dealt[t] = load_dealt_wgs(t, placed(f"wgs_dealt{t}", [P, S], F32, W1_EARLY + 4096 * (t - 1)))
         raw["w4", 1] = load_rows(w4[512:1024, :], placed("w4_raw1", [P, 4, N], F32, TAB_LOW))
@@ -373,7 +408,7 @@ def tile_list_strata_contacts_kernel(
         rounded = []
 
         def late_grouped():
-            places = (LARGER + 3 * 4096, TAB_HIGH, LARGER + 2 * 4096, TAB_HIGH + 4096, STAGE, STAGE + 4096, STAGE + 8192)
+            places = (LARGER, TAB_HIGH, LARGER + 2 * 4096, TAB_HIGH + 4096, STAGE, STAGE + 4096, STAGE + 8192)
             rounded.append(placed(f"grouped{len(rounded)}", [P, 4 * 512], BF16, places[len(rounded)]))
             return rounded[-1]
 
@@ -416,7 +451,7 @@ def tile_list_strata_contacts_kernel(
             fetch_minus(4 + t, list4, 0, M, raw["g", 1][:, t, :], upper_below[t][:])
 
         def third_z(q):
-            z_back[q] = placed(f"z_back{q}", [P, 2, P], F32, Z_UPPER + 4096 + 1024 * q if q < 2 else TAB_LOW + 1024 * q)
+            z_back[q] = placed(f"z_back{q}", [P, 2, P], F32, Z_UPPER + 4096 + 1024 * q if q < 2 else LAST_WGS + 1024 * q)
             fetch_minus(6, list3, P * q, P, upper_below[2][:, P * q : P * (q + 1)], z_back[q][:, 0, :])
 
         for t in range(3):
@@ -442,7 +477,7 @@ def tile_list_strata_contacts_kernel(
         stage2_operand("w6", 1)
         stage2_operand("w4", 0)
         stage2_operand("w4", 1)
-        wgs_dealt[3] = load_dealt_wgs(3, placed("wgs_dealt3", [P, S], F32, TAB_LOW))
+        wgs_dealt[3] = load_dealt_wgs(3, placed("wgs_dealt3", [P, S], F32, LAST_WGS))
         put_in_page(7, 0, S, h_upper[:, 3, :], wgs_dealt[3])
         quant["g", 1] = quantize(g_grouped, "g1")
 

@@ -34,7 +34,7 @@ LARGER = Z_UPPER + 4 * 2048
 EARLY_D1 = LARGER + 8 * 2048
 W1_EARLY = EARLY_D1 + 2 * 2048
 THIRD_PAGE = W1_EARLY + 8192
-LAST_WGS = STAGE + 2 * 8192
+LAST_WGS = STAGE + 8192
 
 
 def tile_list_strata_contacts_kernel(
@@ -408,7 +408,7 @@ def tile_list_strata_contacts_kernel(
         rounded = []
 
         def late_grouped():
-            places = (LARGER, TAB_HIGH, LARGER + 2 * 4096, TAB_HIGH + 4096, STAGE, STAGE + 4096, STAGE + 8192)
+            places = (LARGER, TAB_HIGH, LARGER + 2 * 4096, TAB_HIGH + 4096, STAGE, STAGE + 4096, STAGE + 2 * 8192)
             rounded.append(placed(f"grouped{len(rounded)}", [P, 4 * 512], BF16, places[len(rounded)]))
             return rounded[-1]
 
@@ -454,32 +454,38 @@ def tile_list_strata_contacts_kernel(
             z_back[q] = placed(f"z_back{q}", [P, 2, P], F32, Z_UPPER + 4096 + 1024 * q if q < 2 else LAST_WGS + 1024 * q)
             fetch_minus(6, list3, P * q, P, upper_below[2][:, P * q : P * (q + 1)], z_back[q][:, 0, :])
 
-        for t in range(3):
-            put_in_page(4 + t, 0, HALF, h_upper[:, t, 0:HALF], wgs_dealt[t])
-            if t == 0:
-                lower_below(3)
-            else:
-                upper_fetch_below(t - 1)
-            put_in_page(4 + t, HALF, HALF, h_upper[:, t, HALF:S], wgs_dealt[t])
-            if t == 0:
-                lower_z(3)
-            else:
-                fetch_minus(3 + t, list3, 0, M, upper_below[t - 1][:], z_front[:, t - 1, :])
+        def upper_put(t, hf):
+            put_in_page(4 + t, HALF * hf, HALF, h_upper[:, t, HALF * hf : HALF * (hf + 1)], wgs_dealt[t])
+
+        def front_z(t):
+            fetch_minus(4 + t, list3, 0, M, upper_below[t][:], z_front[:, t, :])
+
+        upper_put(0, 0)
+        lower_below(3)
+        upper_put(1, 0)
+        lower_z(3)
+        upper_put(0, 1)
+        upper_put(1, 1)
+        upper_fetch_below(0)
+        upper_put(2, 0)
+        front_z(0)
+        upper_fetch_below(1)
+        upper_put(2, 1)
+        front_z(1)
         upper_fetch_below(2)
         third_z(0)
         third_z(1)
-        g_grouped = round_rows(raw["g", 0], late_grouped(), False)
+        g_grouped = round_rows(raw["g", 0][:], late_grouped(), False)
         stage2_operand("w6", 0)
         for b in range(4):
             turn_z_lower(b)
         quantize_z_lower()
-        g_grouped = round_rows(raw["g", 1], late_grouped(), False)
-        stage2_operand("w6", 1)
         stage2_operand("w4", 0)
-        stage2_operand("w4", 1)
+        stage2_operand("w6", 1)
         wgs_dealt[3] = load_dealt_wgs(3, placed("wgs_dealt3", [P, S], F32, LAST_WGS))
         put_in_page(7, 0, S, h_upper[:, 3, :], wgs_dealt[3])
-        quant["g", 1] = quantize(g_grouped, "g1")
+        quant["g", 1] = quantize(round_rows(raw["g", 1][:], late_grouped(), False), "g1")
+        stage2_operand("w4", 1)
 
         def round_pair(grouped, u, planes):
             nc.scalar.copy(

@@ -21,7 +21,7 @@ P = 128
 HALF = 512
 W1_WIDTHS = (256, 256, 256, 256)
 FIRST_PARTS = (slice(0, 256), slice(256, 512))
-RELU_FROM = 5
+RELU_FROM = 3
 W2_FIRST = 256
 GPSIMD_CLEARS = 576
 ROUND_GROUPS = 32
@@ -83,6 +83,7 @@ def tile_list_strata_contacts_kernel(
         nc.vector.memset(tab_s[:].bitcast(I32)[:, GPSIMD_CLEARS:], 0)
         nc.vector.memset(w3_s[:].bitcast(I32), 0)
         nc.vector.memset(w5_s[:].bitcast(I32), 0)
+        load_scale_rows(nc.gpsimd, w3_s, w3_scales[0])
         make_identity(nc, ident[:])
         for page in pages:
             nc.vector.memset(page[:], 0.0)
@@ -91,7 +92,7 @@ def tile_list_strata_contacts_kernel(
 
         def load_w1(i):
             shape = [P, 4, W1_WIDTHS[i]]
-            raw = placed(f"w1_raw{i}", shape, F32, TAB_LOW + 4096 * (i - 2) if i >= 2 else W1_EARLY + 4096 * i)
+            raw = placed(f"w1_raw{i}", shape, F32, STAGE + 4096 * (i - 2) if i >= 2 else W1_EARLY + 4096 * i)
             return load_rows(w1[:, w1_starts[i] : w1_starts[i] + W1_WIDTHS[i]], raw)
 
         tab_w_dram = tab_words[0].rearrange("p t i -> p (t i)").bitcast(I32)
@@ -109,7 +110,6 @@ def tile_list_strata_contacts_kernel(
         nc.sync.dma_start(out=w2_first[:], in_=w2_dram[:, 0:W2_FIRST])
         nc.sync.dma_start(out=w3_w[:].bitcast(I32), in_=w3_words[0].bitcast(I32))
         load_scale_rows(nc.sync, w2_s, w2_scales[0])
-        load_scale_rows(nc.sync, w3_s, w3_scales[0])
         nc.sync.dma_start(list2[:], offs2)
         nc.sync.dma_start(out=wgs_sb[:, 0:HALF], in_=wgs[:, 0:HALF])
         w1_raw[1] = load_w1(1)
@@ -251,10 +251,7 @@ def tile_list_strata_contacts_kernel(
                 return
             minus_d1 = lower_product(u, "d1", ("minus_w1",))
             d2 = lower_product(u, ("d2", "spare")[u % 2], ("w2",))
-            if u < 3:
-                d1_sb = placed(f"early_d1_{u}", [P, 512], F32, EARLY_D1 + 2048 * (u - 1))
-            else:
-                d1_sb = pair.tile([P, 512], F32, name="d1_sb")
+            d1_sb = placed(f"early_d1_{u}", [P, 512], F32, EARLY_D1 + 2048 * (u - 1))
             nc.scalar.activation(out=d1_sb[:], in_=minus_d1[:], func=ACT.Copy, scale=-1.0)
             nc.vector.tensor_tensor(out=larger[u][:], in0=d2[:], in1=d1_sb[:], op=ALU.max)
 
@@ -340,9 +337,8 @@ def tile_list_strata_contacts_kernel(
             nc.scalar.copy(out=h_upper[:, :, P * c : P * (c + 1)], in_=h_ps[:].rearrange("p (t j) -> p t j", t=4))
 
         def upper_step(c):
-            if c < 8:
-                upper_first(c)
-                upper_second(c)
+            upper_first(c)
+            upper_second(c)
             if c >= 1:
                 upper_turn(c - 1)
 
@@ -374,10 +370,10 @@ def tile_list_strata_contacts_kernel(
             out=w5_sd[:].rearrange("p a (t m) -> p a t m", t=4),
             in_=w5_s[:].rearrange("p a (m t) -> p a t m", t=4),
         )
-        lower_larger(3)
         lower_turn(1)
         put_in_page(0, HALF, HALF, h_lower[1][:], wgs_sb)
         lower_minus_d3(2)
+        lower_larger(3)
         lower_minus_d3(3)
         quantize_w1(2)
         quantize_w1(3)
@@ -390,13 +386,13 @@ def tile_list_strata_contacts_kernel(
             if u >= 4 and u % 2 == 0:
                 lower_z((u - 4) // 2)
             put_in_page(u // 2, HALF * (u % 2), HALF, h_lower[u][:], wgs_sb)
-            if u >= 4:
+            if u in (4, 5):
                 upper_step(u - 4)
             if u + 2 < 8:
                 lower_minus_d3(u + 2)
+        upper_turn(1)
         lower_z(2)
-        upper_turn(3)
-        for chunks in ((4, 5), (6, 7)):
+        for chunks in ((2, 3), (4, 5), (6, 7)):
             for stage in (negated_products, excess_turned, excess_back, sum_turned):
                 for c in chunks:
                     stage(c)

@@ -19,22 +19,28 @@ ACT = mybir.ActivationFunctionType
 
 P = 128
 HALF = 512
-W1_WIDTHS = (256, 256, 256, 256)
+W1_PIECE = 256
 FIRST_PARTS = (slice(0, 256), slice(256, 512))
-RELU_FROM = 3
 W2_FIRST = 256
 GPSIMD_CLEARS = 576
 ROUND_GROUPS = 32
+RELU_CHUNKS = ()
+VECTOR_MAX_UNITS = ()
 
-TAB_LOW, TAB_HIGH, TAB_SCALES = 0, 8192, 16384
-STAGE = 20480
-TERMS = STAGE + 3 * 8192
-Z_UPPER = TERMS + 8 * 2048
-LARGER = Z_UPPER + 4 * 2048
-EARLY_D1 = LARGER + 8 * 2048
-W1_EARLY = EARLY_D1 + 2 * 2048
-THIRD_PAGE = W1_EARLY + 8192
-LAST_WGS = STAGE + 8192
+TERM = 2048
+TAB_WORDS, TAB_SCALES = 0, 16384
+W1_RAW = 20480
+W1_GROUPED = W1_RAW + 16384
+LATE_RAW = W1_GROUPED + 8192
+STAGE1 = LATE_RAW + 16384
+FIRST_TERMS = STAGE1 + 6 * 4096
+SECOND_TERMS = FIRST_TERMS + 7 * TERM
+MINUS_D2 = SECOND_TERMS + 2 * TERM
+EXCESS = MINUS_D2 + 2 * TERM
+CHUNK_TERMS = EXCESS + 2 * TERM
+H_HALVES = CHUNK_TERMS + 12 * TERM
+H_FRONT = H_HALVES + 8 * TERM
+THIRD_PAGE = H_FRONT + 4 * TERM
 
 
 def tile_list_strata_contacts_kernel(
@@ -45,7 +51,6 @@ def tile_list_strata_contacts_kernel(
     with ExitStack() as ctx:
         keep = ctx.enter_context(tc.tile_pool(name="keep", bufs=1))
         shared = ctx.enter_context(tc.tile_pool(name="shared", bufs=1))
-        ring = ctx.enter_context(tc.tile_pool(name="ring", bufs=3))
         pair = ctx.enter_context(tc.tile_pool(name="pair", bufs=2))
         psum = ctx.enter_context(tc.psum_pool(name="psum", bufs=1))
 
@@ -70,11 +75,22 @@ def tile_list_strata_contacts_kernel(
         list2 = held("list2", [P, S // 16], U16)
         list3 = held("list3", [P, M // 16], U16)
         list4 = held("list4", [P, M // 16], U16)
-        tab_w = placed("tab_w", [P, T], I32, TAB_LOW)
+        tab_w = placed("tab_w", [P, T], I32, TAB_WORDS)
         tab_s = placed("tab_s", [P, T], U8, TAB_SCALES)
-        w2_s = held("w2_s", [P, H], U8)
-        w3_s = held("w3_s", [P, H], U8)
+        minus_w1_c = placed("minus_w1_c", [P, H], U32, STAGE1)
+        w2_first = placed("w2_first", [P, W2_FIRST], I32, STAGE1 + 4096)
+        w2_rest = placed("w2_rest", [P, H - W2_FIRST], I32, STAGE1 + 4096 + 4 * W2_FIRST)
+        v_w = [placed(f"v_w{hf}", [P, HALF], U32, STAGE1 + 2 * 4096 + TERM * hf) for hf in range(2)]
+        w3_w = placed("w3_w", [P, 2 * H], U8, STAGE1 + 3 * 4096)
+        minus_w1_s = placed("minus_w1_s", [P, H], U8, STAGE1 + 4 * 4096)
+        w2_s = placed("w2_s", [P, H], U8, STAGE1 + 4 * 4096 + H)
+        w3_s = placed("w3_s", [P, H], U8, STAGE1 + 5 * 4096)
+        v_s = [placed(f"v_s{hf}", [P, HALF], U8, STAGE1 + 5 * 4096 + H + HALF * hf) for hf in range(2)]
+        hiatus_rows = [placed(f"hiatus_rows{b}", [P, M], F32, STAGE1 + (3 + b) * 4096 + TERM) for b in range(3)]
+        hiatus_rows.append(held("hiatus_rows3", [P, M], F32))
         w5_s = held("w5_s", [P, 2, N], U8)
+        w5_w = held("w5_w", [P, 2, 2 * N], U8)
+        wgs_sb = held("wgs_sb", [P, S], F32)
         pages = [held(f"page{i}", [P, T2], F32) for i in range(2)]
         ident = held("ident", [P, P], F32)
 
@@ -88,37 +104,32 @@ def tile_list_strata_contacts_kernel(
         for page in pages:
             nc.vector.memset(page[:], 0.0)
 
-        w1_starts = [sum(W1_WIDTHS[:i]) for i in range(len(W1_WIDTHS))]
-
         def load_w1(i):
-            shape = [P, 4, W1_WIDTHS[i]]
-            raw = placed(f"w1_raw{i}", shape, F32, STAGE + 4096 * (i - 2) if i >= 2 else W1_EARLY + 4096 * i)
-            return load_rows(w1[:, w1_starts[i] : w1_starts[i] + W1_WIDTHS[i]], raw)
+            raw = placed(f"w1_raw{i}", [P, 4, W1_PIECE], F32, W1_RAW + 4096 * i)
+            return load_rows(w1[:, W1_PIECE * i : W1_PIECE * (i + 1)], raw)
 
         tab_w_dram = tab_words[0].rearrange("p t i -> p (t i)").bitcast(I32)
         w2_dram = w2_words[0].rearrange("p c i -> p (c i)").bitcast(I32)
-        w2_first = held("w2_first", [P, W2_FIRST], I32)
-        w2_rest = held("w2_rest", [P, H - W2_FIRST], I32)
-        w3_w = held("w3_w", [P, 2 * H], U8)
-        w5_w = held("w5_w", [P, 2, 2 * N], U8)
-        wgs_sb = held("wgs_sb", [P, S], F32)
         nc.sync.dma_start(list1[:], offs)
         nc.sync.dma_start(out=tab_w[:, 0 : T // 4], in_=tab_w_dram[:, 0 : T // 4])
         load_scale_rows(nc.sync, tab_s, tab_scales[0])
-        w1_raw = {0: load_w1(0)}
+        w1_raw = [load_w1(0)]
         nc.sync.dma_start(out=tab_w[:, T // 4 : T], in_=tab_w_dram[:, T // 4 : T])
         nc.sync.dma_start(out=w2_first[:], in_=w2_dram[:, 0:W2_FIRST])
         nc.sync.dma_start(out=w3_w[:].bitcast(I32), in_=w3_words[0].bitcast(I32))
         load_scale_rows(nc.sync, w2_s, w2_scales[0])
         nc.sync.dma_start(list2[:], offs2)
         nc.sync.dma_start(out=wgs_sb[:, 0:HALF], in_=wgs[:, 0:HALF])
-        w1_raw[1] = load_w1(1)
+        w1_raw.append(load_w1(1))
         nc.sync.dma_start(out=w5_w[:].bitcast(I32), in_=w5_words.rearrange("a p c -> p a c").bitcast(I32))
-        load_scale_rows(nc.sync, w5_s, w5_scales.rearrange("a q c -> q a c"))
         nc.sync.dma_start(out=wgs_sb[:, HALF:S], in_=wgs[:, HALF:S])
+        w1_raw.extend(load_w1(i) for i in (2, 3))
+        load_scale_rows(nc.sync, w5_s, w5_scales.rearrange("a q c -> q a c"))
         nc.sync.dma_start(out=w2_rest[:], in_=w2_dram[:, W2_FIRST:H])
-        nc.sync.dma_start(list3[:], offs3)
         nc.sync.dma_start(list4[:], offs4)
+        nc.sync.dma_start(list3[:], offs3)
+        for b in range(4):
+            nc.sync.dma_start(out=hiatus_rows[b][:], in_=hiatus[P * b : P * (b + 1), :])
 
         def round_rows(raw, grouped, dealt, negated=False):
             width = raw.shape[2]
@@ -137,55 +148,28 @@ def tile_list_strata_contacts_kernel(
 
         def quantize(grouped, name):
             width = grouped.shape[1] // 4
-            if name in ("g0", "g1"):
-                codes = placed(name + "_c", [P, width], U32, LARGER + 4096 + 1024 if name == "g0" else LAST_WGS)
-            else:
-                codes = held(name + "_c", [P, width], U32)
+            codes = held(name + "_c", [P, width], U32)
             scales = held(name + "_s", [P, width], U8)
             nc.vector.quantize_mx(out=codes[:].bitcast(FP8X4), scales=scales[:], in_=grouped[:])
             return codes, scales
 
-        minus_w1_c = held("minus_w1_c", [P, H], U32)
-        minus_w1_s = held("minus_w1_s", [P, H], U8)
-
         def quantize_w1(i):
-            shape = [P, 4 * W1_WIDTHS[i]]
-            if i == 0:
-                grouped = held(f"w1_grouped{i}", shape, BF16)
-            else:
-                grouped = placed(f"w1_grouped{i}", shape, BF16, (TAB_SCALES + 2 * N, LARGER + 2048, TERMS + 2048)[i - 1])
+            grouped = placed(f"w1_grouped{i}", [P, 4 * W1_PIECE], BF16, W1_GROUPED + TERM * i if i < 3 else TAB_SCALES + TERM)
             round_rows(w1_raw[i], grouped, False, True)
-            cols = slice(w1_starts[i], w1_starts[i] + W1_WIDTHS[i])
+            cols = slice(W1_PIECE * i, W1_PIECE * (i + 1))
             nc.vector.quantize_mx(out=minus_w1_c[:, cols].bitcast(FP8X4), scales=minus_w1_s[:, cols], in_=grouped[:])
 
-        v_s = [held(f"v_s{hf}", [P, HALF], U8) for hf in range(2)]
-        v_w = [held(f"v_w{hf}", [P, HALF], U32) for hf in range(2)]
         nc.vector.tensor_copy(out=v_s[0][:], in_=tab_s[:].indirect(list1[:, 0:32]))
         nc.vector.tensor_copy(out=v_s[1][:], in_=tab_s[:].indirect(list1[:, 32:64]))
         quantize_w1(0)
         nc.vector.tensor_copy(out=v_w[0][:], in_=tab_w[:].bitcast(U32).indirect(list1[:, 0:32]))
         nc.vector.tensor_copy(out=v_w[1][:], in_=tab_w[:].bitcast(U32).indirect(list1[:, 32:64]))
 
-        w1_raw[2] = load_w1(2)
-        w1_raw[3] = load_w1(3)
-        hiatus_rows = [held(f"hiatus_rows{b}", [P, M], F32) for b in range(4)]
-        for b in range(4):
-            nc.sync.dma_start(out=hiatus_rows[b][:], in_=hiatus[P * b : P * (b + 1), :])
-        raw = {
-            ("g", 0): load_rows(hiatus[0:512, :], placed("g_raw0", [P, 4, M], F32, TAB_HIGH)),
-            ("g", 1): load_rows(hiatus[512:1024, :], held("g_raw1", [P, 4, M], F32)),
-        }
         wgs_by_t = wgs.rearrange("(i t) j -> t i j", t=4)
-
-        def load_dealt_wgs(t, tile):
+        wgs_dealt = [placed(f"wgs_dealt{t}", [P, S], F32, TAB_WORDS + 4096 * t) for t in range(4)]
+        for t in range(4):
             for q in range(4):
-                nc.sync.dma_start(out=tile[32 * q : 32 * (q + 1), :], in_=wgs_by_t[t])
-            return tile
-
-        wgs_dealt = {0: load_dealt_wgs(0, held("wgs_dealt0", [P, S], F32))}
-        raw["w6", 0] = load_rows(w6[0:512, :], placed("w6_raw0", [P, 4, N], F32, STAGE))
-        raw["w6", 1] = load_rows(w6[512:1024, :], placed("w6_raw1", [P, 4, N], F32, STAGE + 8192))
-        raw["w4", 0] = load_rows(w4[0:512, :], placed("w4_raw0", [P, 4, N], F32, STAGE + 2 * 8192))
+                nc.sync.dma_start(out=wgs_dealt[t][32 * q : 32 * (q + 1), :], in_=wgs_by_t[t])
 
         def weights(name, r0, width):
             cols = slice(r0, r0 + width)
@@ -211,15 +195,24 @@ def tile_list_strata_contacts_kernel(
                     )
             return acc
 
-        def transposed_sum(acc, terms):
-            for n, term in enumerate(terms):
-                for c in range(4):
+        def turn_and_add(acc, blocks):
+            count = sum(len(column) for column in blocks)
+            done = 0
+            for x, column in enumerate(blocks):
+                for block in column:
                     nc.tensor.matmul(
-                        acc[:, P * c : P * (c + 1)], term[:, P * c : P * (c + 1)], ident[:], is_transpose=True,
-                        start=(n == 0 and c == 0), stop=(n == len(terms) - 1 and c == 3),
+                        acc[:, P * x : P * (x + 1)], block, ident[:], is_transpose=True,
+                        start=(done == 0), stop=(done == count - 1),
                     )
+                    done = done + 1
 
-        larger, minus_d3, h_lower = {}, {}, {}
+        def transposed_sum(acc, terms):
+            turn_and_add(acc, [[term[:, P * x : P * (x + 1)] for term in terms] for x in range(4)])
+
+        def term(name, offset):
+            return placed(name, [P, 512], F32, offset)
+
+        h_half, unit_terms = {}, {}
 
         def lower_product(u, tag, names):
             b, hf = divmod(u, 2)
@@ -227,50 +220,50 @@ def tile_list_strata_contacts_kernel(
 
         def first_unit():
             d = {}
-            for name, tag in (("minus_w1", "spare"), ("w2", "d1"), ("w3", "d3")):
+            for name, tag in (("minus_w1", "first"), ("w2", "second"), ("w3", "d3")):
                 codes, scales = weights(name, 0, P)
                 d[name] = bank(tag)
                 nc.tensor.matmul_mx(
                     out=d[name][:], lhsT=codes, lhsT_scale=scales,
                     rhs=v_w[0][:].bitcast(FP8X4), rhs_scale=v_s[0][:], start=True, stop=True,
                 )
-            d1_sb = placed("first_d1", [P, 512], F32, TAB_SCALES + 2 * N)
-            first_larger = placed("first_larger", [P, 512], F32, THIRD_PAGE)
-            h_lower[0] = ring.tile([P, HALF], F32, name="h_lower_sb", bufs=4)
+            d1_sb = term("first_d1", TAB_SCALES)
+            first_larger = term("first_larger", THIRD_PAGE)
+            h_half[0] = term("h_half0", H_HALVES)
             for cols in FIRST_PARTS:
                 nc.scalar.activation(out=d1_sb[:, cols], in_=d["minus_w1"][:, cols], func=ACT.Copy, scale=-1.0)
                 nc.vector.tensor_tensor(out=first_larger[:, cols], in0=d["w2"][:, cols], in1=d1_sb[:, cols], op=ALU.max)
             for cols in FIRST_PARTS:
-                nc.vector.tensor_tensor(out=h_lower[0][:, cols], in0=first_larger[:, cols], in1=d["w3"][:, cols], op=ALU.subtract)
+                nc.vector.tensor_tensor(out=h_half[0][:, cols], in0=first_larger[:, cols], in1=d["w3"][:, cols], op=ALU.subtract)
 
-        def lower_larger(u):
-            larger[u] = placed(f"larger{u}", [P, 512], F32, LARGER + 2048 * u)
-            if u >= RELU_FROM:
-                acc = lower_product(u, ("d2", "spare")[u % 2], ("w2", "minus_w1"))
-                nc.scalar.activation(out=larger[u][:], in_=acc[:], func=ACT.Relu)
-                return
-            minus_d1 = lower_product(u, "d1", ("minus_w1",))
-            d2 = lower_product(u, ("d2", "spare")[u % 2], ("w2",))
-            d1_sb = placed(f"early_d1_{u}", [P, 512], F32, EARLY_D1 + 2048 * (u - 1))
-            nc.scalar.activation(out=d1_sb[:], in_=minus_d1[:], func=ACT.Copy, scale=-1.0)
-            nc.vector.tensor_tensor(out=larger[u][:], in0=d2[:], in1=d1_sb[:], op=ALU.max)
+        def lower_terms(u):
+            first = term(f"first_term{u}", FIRST_TERMS + TERM * (u - 1))
+            second = term(f"second_term{u}", TAB_SCALES + TERM if u == 1 else SECOND_TERMS + TERM * (u % 2))
+            if u in VECTOR_MAX_UNITS:
+                d1_sb = term(f"lower_d1_{u}", MINUS_D2 + TERM * (u % 2))
+                nc.scalar.activation(out=d1_sb[:], in_=lower_product(u, "excess", ("minus_w1",))[:], func=ACT.Copy, scale=-1.0)
+                nc.vector.tensor_tensor(out=first[:], in0=lower_product(u, "first", ("w2",))[:], in1=d1_sb[:], op=ALU.max)
+                names = ("w3",)
+            else:
+                nc.scalar.activation(out=first[:], in_=lower_product(u, "first", ("w2", "minus_w1"))[:], func=ACT.Relu)
+                names = ("w3", "minus_w1")
+            nc.scalar.activation(out=second[:], in_=lower_product(u, "second", names)[:], func=ACT.Copy, scale=-1.0)
+            unit_terms[u] = (first, second)
 
-        def lower_minus_d3(u):
-            d3 = lower_product(u, "d3", ("w3", "minus_w1") if u >= RELU_FROM else ("w3",))
-            minus_d3[u] = placed(f"minus_d3_{u}", [P, 512], F32, TERMS + 2048 * u)
-            nc.scalar.activation(out=minus_d3[u][:], in_=d3[:], func=ACT.Copy, scale=-1.0)
+        def lower_sum(u):
+            acc = bank("sum")
+            transposed_sum(acc, unit_terms[u])
+            h_half[u] = term(f"h_half{u}", W1_RAW + 3 * 4096 if u == 2 else H_HALVES + TERM * u)
+            nc.scalar.copy(out=h_half[u][:], in_=acc[:])
 
-        def lower_turn(u):
-            h_ps = bank("h_lower")
-            transposed_sum(h_ps, (minus_d3[u], larger[u]))
-            h_lower[u] = ring.tile([P, HALF], F32, name="h_lower_sb", bufs=4)
-            nc.scalar.copy(out=h_lower[u][:], in_=h_ps[:])
-
-        def put_in_page(slab, j0, width, values, weights):
+        def put_in_page(slab, hf, values, weights):
             nc.vector.tensor_tensor(
-                out=pages[slab % 3][:].indirect(list2[:, j0 // 16 : (j0 + width) // 16]),
-                in0=values, in1=weights[:, j0 : j0 + width], op=ALU.mult,
+                out=pages[slab % 3][:].indirect(list2[:, 32 * hf : 32 * (hf + 1)]),
+                in0=values, in1=weights[:, HALF * hf : HALF * (hf + 1)], op=ALU.mult,
             )
+
+        def lower_put(u):
+            put_in_page(u // 2, u % 2, h_half[u][:], wgs_sb)
 
         def fetch_minus(slab, columns, m0, width, other, out):
             nc.vector.tensor_tensor(
@@ -278,143 +271,157 @@ def tile_list_strata_contacts_kernel(
                 in1=other, op=ALU.subtract,
             )
 
-        h_upper = held("h_upper", [P, 4, S], F32)
-        first_term, second_term = {}, {}
-
         def dealt(acc):
             return acc[:].rearrange("j (p t) -> j t p", t=4)
 
         def by_t(tile):
             return tile[:].rearrange("j (t p) -> j t p", t=4)
 
-        def upper_first(c):
-            first_term[c] = placed(f"first_term{c}", [P, 512], F32, LARGER + 2048 * (c % 2 + 3))
-            acc = product("first", ("w2", "minus_w1"), (c,), 512, 512)
-            nc.scalar.activation(out=by_t(first_term[c]), in_=dealt(acc), func=ACT.Relu)
+        def dealt_term(c, name, offset, tag, names, func, scale):
+            tile = term(f"{name}{c}", offset)
+            nc.scalar.activation(out=by_t(tile), in_=dealt(product(tag, names, (c,), 512, 512)), func=func, scale=scale)
+            return tile
 
-        def upper_second(c):
-            acc = product("second", ("w3", "minus_w1"), (c,), 512, 512)
-            second_term[c] = ring.tile([P, 512], F32, name="second_term")
-            nc.scalar.activation(out=by_t(second_term[c]), in_=dealt(acc), func=ACT.Copy, scale=-1.0)
+        chunk_terms, minus_d2, excess = {}, {}, {}
+        h_front = placed("h_front", [P, 4, HALF], F32, H_FRONT)
 
-        def upper_turn(c):
-            h_ps = bank("h_upper")
-            transposed_sum(h_ps, (second_term[c], first_term[c]))
-            nc.scalar.copy(out=h_upper[:, :, P * c : P * (c + 1)], in_=h_ps[:].rearrange("p (t j) -> p t j", t=4))
+        def chunk_slot(c, n):
+            return CHUNK_TERMS + TERM * (3 * (c % 4) + n)
 
-        turned = {}
+        def chunk_products(c):
+            if c in RELU_CHUNKS:
+                chunk_terms[c] = [
+                    dealt_term(c, "chunk_first", chunk_slot(c, 0), "d1", ("w2", "minus_w1"), ACT.Relu, 1.0),
+                    dealt_term(c, "chunk_second", chunk_slot(c, 1), "d2", ("w3", "minus_w1"), ACT.Copy, -1.0),
+                ]
+                return
+            chunk_terms[c] = [dealt_term(c, "chunk_d1_", chunk_slot(c, 0), "d1", ("minus_w1",), ACT.Copy, -1.0)]
+            minus_d2[c] = dealt_term(c, "minus_d2_", MINUS_D2 + TERM * (c % 2), "d2", ("w2",), ACT.Copy, -1.0)
 
-        def negated_products(c):
-            terms = (
-                placed(f"d1_upper{c}", [P, 512], F32, LARGER + 2048 * (c + 2)) if c < 6 else held(f"d1_upper{c}", [P, 512], F32),
-                pair.tile([P, 512], F32, name="d1_sb"),
-                ring.tile([P, 512], F32, name="second_term") if c < 7 else held("last_term", [P, 512], F32),
-            )
-            for term, name, tag in zip(terms, ("minus_w1", "w2", "w3"), ("first", "second", "h_lower")):
-                acc = product(tag, (name,), (c,), 512, 512)
-                nc.scalar.activation(out=by_t(term), in_=dealt(acc), func=ACT.Copy, scale=-1.0)
-            turned[c] = terms
+        def chunk_third(c):
+            if c not in RELU_CHUNKS:
+                chunk_terms[c].append(dealt_term(c, "minus_d3_", chunk_slot(c, 1), "d3", ("w3",), ACT.Copy, -1.0))
 
-        def excess_turned(c):
-            d1, minus_d2, minus_d3_c = turned[c]
-            acc = bank(("d2", "spare")[c % 2])
-            transposed_sum(acc, (d1, minus_d2))
-            excess = placed(f"excess{c}", [P, 512], F32, TAB_SCALES + 2048 * (c % 2))
-            nc.scalar.activation(out=excess[:], in_=acc[:], func=ACT.Relu, scale=-1.0)
-            turned[c] = (d1, minus_d3_c, excess)
+        def chunk_excess(c):
+            if c not in RELU_CHUNKS:
+                acc = bank("first" if c in (5, 7) else "excess")
+                transposed_sum(acc, (chunk_terms[c][0], minus_d2[c]))
+                excess[c] = term(f"excess{c}", FIRST_TERMS + TERM if c == 3 else EXCESS + TERM * (c % 2))
+                nc.scalar.activation(out=excess[c][:], in_=acc[:], func=ACT.Relu, scale=-1.0)
 
-        def excess_back(c):
-            d1, minus_d3_c, excess = turned[c]
-            acc = bank(("d3", "d1")[c % 2])
-            transposed_sum(acc, (excess,))
-            back = placed(f"excess_back{c}", [P, 512], F32, LARGER + 2048 * (c % 2))
-            nc.scalar.copy(out=back[:], in_=acc[:])
-            turned[c] = (d1, minus_d3_c, back)
+        def chunk_back(c):
+            if c not in RELU_CHUNKS:
+                acc = bank("second" if c in (5, 7) else "back")
+                transposed_sum(acc, (excess[c],))
+                back = term(f"back{c}", TAB_SCALES if c == 3 else chunk_slot(c, 2))
+                nc.scalar.copy(out=back[:], in_=acc[:])
+                chunk_terms[c].append(back)
 
-        def sum_turned(c):
-            h_ps = bank("h_upper")
-            transposed_sum(h_ps, turned[c])
-            nc.scalar.copy(out=h_upper[:, :, P * c : P * (c + 1)], in_=h_ps[:].rearrange("p (t j) -> p t j", t=4))
+        def chunk_sum(c):
+            acc = bank("sum")
+            transposed_sum(acc, chunk_terms[c])
+            nc.scalar.copy(out=h_front[:, :, P * c : P * (c + 1)], in_=acc[:].rearrange("p (t j) -> p t j", t=4))
 
-        def upper_step(c):
-            upper_first(c)
-            upper_second(c)
-            if c >= 1:
-                upper_turn(c - 1)
+        def slab_sum(t, tag):
+            acc = bank(tag)
+            turn_and_add(acc, [[tile[:, P * t : P * (t + 1)] for tile in chunk_terms[c]] for c in range(4, 8)])
+            h_half[8 + t] = term(f"h_back{t}", H_HALVES + TERM * (4 + t))
+            nc.scalar.copy(out=h_half[8 + t][:], in_=acc[:])
 
         below, z_lower = {}, {}
 
         def lower_below(b):
-            below[b] = placed(f"below{b}", [P, M], F32, TERMS + 2048 * ((2 * b + 3) % 8))
+            below[b] = term(f"below{b}", FIRST_TERMS + TERM * (2 * b + 2) if b < 3 else TAB_SCALES)
             fetch_minus(b, list4, 0, M, hiatus_rows[b][:], below[b][:])
 
         def lower_z(b):
-            z_lower[b] = placed(f"z_lower{b}", [P, M], F32, TERMS + 2048 * (2 * b + 4 if b < 2 else 2 * b - 4))
+            offset = (FIRST_TERMS + 3 * TERM, FIRST_TERMS + 5 * TERM, FIRST_TERMS + TERM, SECOND_TERMS)[b]
+            z_lower[b] = term(f"z_lower{b}", offset)
             fetch_minus(b, list3, 0, M, below[b][:], z_lower[b][:])
 
-        w5_wd = placed("w5_dealt_words", [P, 2, 2 * N], U8, EARLY_D1)
-        w5_sd = placed("w5_dealt_scales", [P, 2, N], U8, EARLY_D1 + 2048)
-        first_unit()
-        pages.append(placed("page2", [P, T2], F32, THIRD_PAGE))
-        nc.gpsimd.memset(pages[2][:], 0.0)
-        lower_larger(1)
-        lower_minus_d3(1)
-        quantize_w1(1)
-        put_in_page(0, 0, HALF, h_lower[0][:], wgs_sb)
-        nc.vector.tensor_copy(
-            out=w5_wd[:].bitcast(U16).rearrange("p a (t m) -> p a t m", t=4),
-            in_=w5_w[:].bitcast(U16).rearrange("p a (m t) -> p a t m", t=4),
-        )
-        lower_larger(2)
-        nc.vector.tensor_copy(
-            out=w5_sd[:].rearrange("p a (t m) -> p a t m", t=4),
-            in_=w5_s[:].rearrange("p a (m t) -> p a t m", t=4),
-        )
-        lower_turn(1)
-        put_in_page(0, HALF, HALF, h_lower[1][:], wgs_sb)
-        lower_minus_d3(2)
-        lower_larger(3)
-        lower_minus_d3(3)
-        quantize_w1(2)
-        quantize_w1(3)
-        for u in range(2, 8):
-            if u + 2 < 8:
-                lower_larger(u + 2)
-            lower_turn(u)
+        def lower_step(u):
+            lower_sum(u)
             if u >= 3 and u % 2 == 1:
                 lower_below((u - 3) // 2)
             if u >= 4 and u % 2 == 0:
                 lower_z((u - 4) // 2)
-            put_in_page(u // 2, HALF * (u % 2), HALF, h_lower[u][:], wgs_sb)
-            if u in (4, 5):
-                upper_step(u - 4)
-            if u + 2 < 8:
-                lower_minus_d3(u + 2)
-        upper_turn(1)
+            lower_put(u)
+
+        first_unit()
+        pages.append(placed("page2", [P, T2], F32, THIRD_PAGE))
+        nc.gpsimd.memset(pages[2][:], 0.0)
+        lower_terms(1)
+        lower_put(0)
+        lower_sum(1)
+        w5_wd = placed("w5_dealt_words", [P, 2, 2 * N], U8, FIRST_TERMS)
+        nc.vector.tensor_copy(
+            out=w5_wd[:].bitcast(U16).rearrange("p a (t m) -> p a t m", t=4),
+            in_=w5_w[:].bitcast(U16).rearrange("p a (m t) -> p a t m", t=4),
+        )
+        lower_put(1)
+        lower_terms(2)
+        for i in (1, 2, 3):
+            quantize_w1(i)
+        w5_sd = placed("w5_dealt_scales", [P, 2, N], U8, TAB_SCALES + TERM)
+        nc.vector.tensor_copy(
+            out=w5_sd[:].rearrange("p a (t m) -> p a t m", t=4),
+            in_=w5_s[:].rearrange("p a (m t) -> p a t m", t=4),
+        )
+        lower_terms(3)
+        lower_step(2)
+        raw = {}
+        for name, source, a, offset in (
+            ("g", hiatus, 0, LATE_RAW), ("w6", w6, 0, W1_RAW), ("w4", w4, 0, W1_GROUPED), ("g", hiatus, 1, None),
+            ("w6", w6, 1, W1_RAW + 8192), ("w4", w4, 1, LATE_RAW + 8192),
+        ):
+            shape = [P, 4, 512]
+            tile = held("g_raw1", shape, F32) if offset is None else placed(f"{name}_raw{a}", shape, F32, offset)
+            raw[name, a] = load_rows(source[512 * a : 512 * (a + 1), :], tile)
+        lower_step(3)
+        for c in range(4):
+            lower_terms(4 + c)
+            if c >= 1:
+                chunk_back(c - 1)
+            chunk_products(c)
+            lower_step(4 + c)
+            if c >= 1:
+                chunk_sum(c - 1)
+            chunk_third(c)
+            chunk_excess(c)
+        chunk_back(3)
         lower_z(2)
-        for chunks in ((2, 3), (4, 5), (6, 7)):
-            for stage in (negated_products, excess_turned, excess_back, sum_turned):
-                for c in chunks:
-                    stage(c)
+        chunk_sum(3)
+        lower_below(3)
+        put_in_page(4, 0, h_front[:, 0, :], wgs_dealt[0])
+        lower_z(3)
         for t in (1, 2):
-            wgs_dealt[t] = load_dealt_wgs(t, placed(f"wgs_dealt{t}", [P, S], F32, W1_EARLY + 4096 * (t - 1)))
-        raw["w4", 1] = load_rows(w4[512:1024, :], placed("w4_raw1", [P, 4, N], F32, TAB_LOW))
+            put_in_page(4 + t, 0, h_front[:, t, :], wgs_dealt[t])
+        for c in range(4, 8):
+            for stage in (chunk_products, chunk_third, chunk_excess, chunk_back):
+                stage(c)
 
-        quant = {}
-        rounded = []
+        quant, rounded = {}, {}
 
-        def late_grouped():
-            places = (LARGER, TAB_HIGH, LARGER + 2 * 4096, TAB_HIGH + 4096, STAGE, STAGE + 4096, STAGE + 2 * 8192)
-            rounded.append(placed(f"grouped{len(rounded)}", [P, 4 * 512], BF16, places[len(rounded)]))
-            return rounded[-1]
+        def round_operand(name, a):
+            grouped = placed(f"{name}_grouped{a}", [P, 4 * 512], BF16, STAGE1 + 4096 * len(rounded))
+            rounded[name, a] = round_rows(raw[name, a], grouped, name != "g")
 
-        def stage2_operand(name, a):
-            quant[name, a] = quantize(round_rows(raw[name, a], late_grouped(), name != "g"), f"{name}{a}")
+        def quantize_operand(name, a):
+            quant[name, a] = quantize(rounded[name, a], f"{name}{a}")
 
-        z_pairs = [placed(f"z_pairs{hf}", [P, 2, 2, 2 * P], BF16, LARGER + 4096 + 2048 * hf) for hf in range(2)]
+        def back_put(t):
+            put_in_page(4 + t, 1, h_half[8 + t][:], wgs_dealt[t])
+
+        upper_below = {}
+
+        def upper_fetch_below(t, offset):
+            upper_below[t] = term(f"upper_below{t}", offset)
+            fetch_minus(4 + t, list4, 0, M, raw["g", 1][:, t, :], upper_below[t][:])
+
+        z_pairs = [placed(f"z_pairs{hf}", [P, 2, 2, 2 * P], BF16, MINUS_D2 + TERM * hf) for hf in range(2)]
 
         def turn_z_lower(b):
-            z_ps = bank("h_lower")
+            z_ps = bank(("first", "second")[b % 2])
             transposed_sum(z_ps, (z_lower[b],))
             for x in range(2):
                 nc.scalar.copy(
@@ -422,11 +429,11 @@ def tile_list_strata_contacts_kernel(
                     in_=z_ps[:, 256 * x : 256 * (x + 1)].rearrange("m (c p u e) -> m c u p e", c=2, u=2, e=2),
                 )
 
-        def quantize_z_lower():
-            grouped = late_grouped()
+        def turn_z_back():
+            grouped = placed("z_lower_grouped", [P, 4 * M], BF16, EXCESS)
             for hf in range(2):
                 words = z_pairs[hf][:].bitcast(F32)
-                back = bank("h_upper")
+                back = bank(("d1", "d2")[hf])
                 for c in range(2):
                     for e in range(2):
                         col = P * (2 * c + e)
@@ -435,60 +442,52 @@ def tile_list_strata_contacts_kernel(
                     out=grouped[:, 1024 * hf : 1024 * (hf + 1)].bitcast(F32).rearrange("p (c m u) -> p c m u", c=2, u=2),
                     in_=back[:].rearrange("p (c u m) -> p c m u", c=2, u=2),
                 )
-            quant["g", 0] = quantize(g_grouped, "g0")
-            quant["z", 0] = quantize(grouped, "z0")
+            return grouped
 
-        z_front = placed("z_front", [P, 2, M], F32, Z_UPPER)
         z_back = {}
-        upper_below = {}
-
-        def upper_fetch_below(t):
-            upper_below[t] = pair.tile([P, M], F32, name="upper_below")
-            fetch_minus(4 + t, list4, 0, M, raw["g", 1][:, t, :], upper_below[t][:])
 
         def third_z(q):
-            z_back[q] = placed(f"z_back{q}", [P, 2, P], F32, Z_UPPER + 4096 + 1024 * q if q < 2 else LAST_WGS + 1024 * q)
+            offset = W1_GROUPED + 4096 + 1024 * q if q < 2 else H_HALVES + 7 * TERM + 1024 * (q - 2)
+            z_back[q] = placed(f"z_back{q}", [P, 2, P], F32, offset)
             fetch_minus(6, list3, P * q, P, upper_below[2][:, P * q : P * (q + 1)], z_back[q][:, 0, :])
 
-        def upper_put(t, hf):
-            put_in_page(4 + t, HALF * hf, HALF, h_upper[:, t, HALF * hf : HALF * (hf + 1)], wgs_dealt[t])
-
-        def front_z(t):
-            fetch_minus(4 + t, list3, 0, M, upper_below[t][:], z_front[:, t, :])
-
-        upper_put(0, 0)
-        lower_below(3)
-        upper_put(1, 0)
-        lower_z(3)
-        upper_put(0, 1)
-        upper_put(1, 1)
-        upper_fetch_below(0)
-        upper_put(2, 0)
-        front_z(0)
-        upper_fetch_below(1)
-        upper_put(2, 1)
-        front_z(1)
-        upper_fetch_below(2)
-        third_z(0)
-        third_z(1)
-        g_grouped = round_rows(raw["g", 0][:], late_grouped(), False)
-        stage2_operand("w6", 0)
+        slab_sum(0, "sum")
+        back_put(0)
+        slab_sum(1, "excess")
+        back_put(1)
         for b in range(4):
             turn_z_lower(b)
-        quantize_z_lower()
-        stage2_operand("w4", 0)
-        stage2_operand("w6", 1)
-        wgs_dealt[3] = load_dealt_wgs(3, placed("wgs_dealt3", [P, S], F32, LAST_WGS))
-        put_in_page(7, 0, S, h_upper[:, 3, :], wgs_dealt[3])
-        quant["g", 1] = quantize(round_rows(raw["g", 1][:], late_grouped(), False), "g1")
-        stage2_operand("w4", 1)
+        z_lower_grouped = turn_z_back()
+        upper_fetch_below(0, MINUS_D2 + TERM)
+        quant["z", 0] = quantize(z_lower_grouped, "z0")
+        round_operand("g", 0)
+        z_front = placed("z_front", [P, 2, M], F32, LATE_RAW)
+        fetch_minus(4, list3, 0, M, upper_below[0][:], z_front[:, 0, :])
+        quantize_operand("g", 0)
+        put_in_page(7, 0, h_front[:, 3, :], wgs_dealt[3])
+        slab_sum(2, "back")
+        back_put(2)
+        round_operand("w6", 0)
+        upper_fetch_below(1, W1_RAW)
+        quantize_operand("w6", 0)
+        fetch_minus(5, list3, 0, M, upper_below[1][:], z_front[:, 1, :])
+        round_operand("w4", 0)
+        upper_fetch_below(2, W1_GROUPED)
+        quantize_operand("w4", 0)
+        third_z(0)
+        third_z(1)
+        for name in ("g", "w6", "w4"):
+            round_operand(name, 1)
+            quantize_operand(name, 1)
+        slab_sum(3, "d3")
+        back_put(3)
 
         def round_pair(grouped, u, planes):
             nc.scalar.copy(
                 out=grouped[:].rearrange("p (m u e) -> p u m e", u=2, e=2)[:, u], in_=planes.rearrange("p e m -> p m e")
             )
 
-        z_grouped = [placed(f"z_grouped{q}", [P, 4 * P], BF16, TAB_LOW + 4096 + 1024 * q) for q in range(4)]
+        z_grouped = [placed(f"z_grouped{q}", [P, 4 * P], BF16, STAGE1 + 3 * 4096 + 1024 * q) for q in range(4)]
         for q in range(4):
             round_pair(z_grouped[q], 0, z_front[:, :, P * q : P * (q + 1)])
 
@@ -510,11 +509,12 @@ def tile_list_strata_contacts_kernel(
                 )
 
         sums, gates = {}, {}
-        for q, tag in enumerate(("d1", "d2", "d3", "first")):
+        for q, tag in enumerate(("first", "second", "d1", "d2")):
             sums[q] = bank(tag)
-            mx_passes(sums[q], "w6", 0, q, True, False)
-            mx_passes(sums[q], "w5", 0, q, False, False)
-        for q, tag in enumerate(("second", "spare", "h_lower", "h_upper")):
+            mx_passes(sums[q], "w5", 0, q, True, False)
+        for q in range(4):
+            mx_passes(sums[q], "w6", 0, q, False, False)
+        for q, tag in enumerate(("sum", "excess", "back", "d3")):
             gates[q] = bank(tag)
             mx_passes(gates[q], "w4", 0, q, True, False)
         for q in range(4):
@@ -526,7 +526,7 @@ def tile_list_strata_contacts_kernel(
             if q < 2:
                 last_below[q] = held(f"last_below{q}", [P, P], F32)
             else:
-                last_below[q] = placed(f"last_below{q}", [P, P], F32, Z_UPPER + 4096 + 512 * (q - 2))
+                last_below[q] = placed(f"last_below{q}", [P, P], F32, W1_GROUPED + 4096 + 512 * (q - 2))
             fetch_minus(7, list4, P * q, P, raw["g", 1][:, 3, P * q : P * (q + 1)], last_below[q][:])
 
         def last_z(q):
@@ -553,9 +553,9 @@ def tile_list_strata_contacts_kernel(
             if q < 3:
                 mx_passes(gates[q + 1], "w4", 1, q + 1, False, True)
             mx_passes(sums[q], "w5", 1, q, False, True)
-            gate = placed(f"gate{q}", [P, 512], F32, TERMS + 2048 * q)
+            gate = placed(f"gate{q}", [P, 512], F32, CHUNK_TERMS + TERM * q)
             nc.scalar.activation(out=gate[:], in_=gates[q][:], func=ACT.Tanh)
-            y = placed(f"y{q}", [P, 4, P], F32, STAGE + 2048 * q)
+            y = placed(f"y{q}", [P, 4, P], F32, CHUNK_TERMS + TERM * (4 + q))
             nc.vector.tensor_tensor(out=y[:].rearrange("p t m -> p (t m)"), in0=sums[q][:], in1=gate[:], op=ALU.mult)
             nc.sync.dma_start(out=out_rows[:, :, cols], in_=y[:])
             y_grouped = pair.tile([P, 4 * P], BF16, name="y_grouped", align_bytes=64)

@@ -24,8 +24,8 @@ FIRST_PARTS = (slice(0, 256), slice(256, 512))
 W2_FIRST = 256
 GPSIMD_CLEARS = 576
 ROUND_GROUPS = 32
-RELU_CHUNKS = ()
-VECTOR_MAX_UNITS = ()
+RELU_CHUNKS = (4, 6)
+VECTOR_MAX_UNITS = (2, 3)
 
 TERM = 2048
 TAB_WORDS, TAB_SCALES = 0, 16384
@@ -241,7 +241,7 @@ def tile_list_strata_contacts_kernel(
             second = term(f"second_term{u}", TAB_SCALES + TERM if u == 1 else SECOND_TERMS + TERM * (u % 2))
             if u in VECTOR_MAX_UNITS:
                 d1_sb = term(f"lower_d1_{u}", MINUS_D2 + TERM * (u % 2))
-                nc.scalar.activation(out=d1_sb[:], in_=lower_product(u, "excess", ("minus_w1",))[:], func=ACT.Copy, scale=-1.0)
+                nc.scalar.activation(out=d1_sb[:], in_=lower_product(u, "d3", ("minus_w1",))[:], func=ACT.Copy, scale=-1.0)
                 nc.vector.tensor_tensor(out=first[:], in0=lower_product(u, "first", ("w2",))[:], in1=d1_sb[:], op=ALU.max)
                 names = ("w3",)
             else:
@@ -352,6 +352,7 @@ def tile_list_strata_contacts_kernel(
         nc.gpsimd.memset(pages[2][:], 0.0)
         lower_terms(1)
         lower_put(0)
+        lower_terms(2)
         lower_sum(1)
         w5_wd = placed("w5_dealt_words", [P, 2, 2 * N], U8, FIRST_TERMS)
         nc.vector.tensor_copy(
@@ -359,7 +360,7 @@ def tile_list_strata_contacts_kernel(
             in_=w5_w[:].bitcast(U16).rearrange("p a (m t) -> p a t m", t=4),
         )
         lower_put(1)
-        lower_terms(2)
+        lower_terms(3)
         for i in (1, 2, 3):
             quantize_w1(i)
         w5_sd = placed("w5_dealt_scales", [P, 2, N], U8, TAB_SCALES + TERM)
@@ -367,7 +368,6 @@ def tile_list_strata_contacts_kernel(
             out=w5_sd[:].rearrange("p a (t m) -> p a t m", t=4),
             in_=w5_s[:].rearrange("p a (m t) -> p a t m", t=4),
         )
-        lower_terms(3)
         lower_step(2)
         raw = {}
         for name, source, a, offset in (

@@ -256,14 +256,14 @@ def tile_list_strata_contacts_kernel(
             h_half[u] = term(f"h_half{u}", W1_RAW + 3 * 4096 if u == 2 else H_HALVES + TERM * u)
             nc.scalar.copy(out=h_half[u][:], in_=acc[:])
 
-        def put_in_page(slab, hf, values, weights):
+        def put_in_page(slab, j0, width, values, weights):
             nc.vector.tensor_tensor(
-                out=pages[slab % 3][:].indirect(list2[:, 32 * hf : 32 * (hf + 1)]),
-                in0=values, in1=weights[:, HALF * hf : HALF * (hf + 1)], op=ALU.mult,
+                out=pages[slab % 3][:].indirect(list2[:, j0 // 16 : (j0 + width) // 16]),
+                in0=values, in1=weights[:, j0 : j0 + width], op=ALU.mult,
             )
 
         def lower_put(u):
-            put_in_page(u // 2, u % 2, h_half[u][:], wgs_sb)
+            put_in_page(u // 2, HALF * (u % 2), HALF, h_half[u][:], wgs_sb)
 
         def fetch_minus(slab, columns, m0, width, other, out):
             nc.vector.tensor_tensor(
@@ -283,7 +283,7 @@ def tile_list_strata_contacts_kernel(
             return tile
 
         chunk_terms, minus_d2, excess = {}, {}, {}
-        h_front = placed("h_front", [P, 4, HALF], F32, H_FRONT)
+        h_front = [placed(f"h_front{k}", [P, 4, 2 * P], F32, H_FRONT + 2 * TERM * k) for k in range(2)]
 
         def chunk_slot(c, n):
             return CHUNK_TERMS + TERM * (3 * (c % 4) + n)
@@ -306,27 +306,30 @@ def tile_list_strata_contacts_kernel(
             if c not in RELU_CHUNKS:
                 acc = bank("first" if c in (5, 7) else "excess")
                 transposed_sum(acc, (chunk_terms[c][0], minus_d2[c]))
-                excess[c] = term(f"excess{c}", FIRST_TERMS + TERM if c == 3 else EXCESS + TERM * (c % 2))
+                excess[c] = term(f"excess{c}", EXCESS + TERM * (c % 2))
                 nc.scalar.activation(out=excess[c][:], in_=acc[:], func=ACT.Relu, scale=-1.0)
 
         def chunk_back(c):
             if c not in RELU_CHUNKS:
                 acc = bank("second" if c in (5, 7) else "back")
                 transposed_sum(acc, (excess[c],))
-                back = term(f"back{c}", TAB_SCALES if c == 3 else chunk_slot(c, 2))
+                back = term(f"back{c}", chunk_slot(c, 2))
                 nc.scalar.copy(out=back[:], in_=acc[:])
                 chunk_terms[c].append(back)
 
         def chunk_sum(c):
             acc = bank("sum")
             transposed_sum(acc, chunk_terms[c])
-            nc.scalar.copy(out=h_front[:, :, P * c : P * (c + 1)], in_=acc[:].rearrange("p (t j) -> p t j", t=4))
+            nc.scalar.copy(out=h_front[c // 2][:, :, P * (c % 2) : P * (c % 2 + 1)], in_=acc[:].rearrange("p (t j) -> p t j", t=4))
 
         def slab_sum(t, tag):
             acc = bank(tag)
             turn_and_add(acc, [[tile[:, P * t : P * (t + 1)] for tile in chunk_terms[c]] for c in range(4, 8)])
             h_half[8 + t] = term(f"h_back{t}", H_HALVES + TERM * (4 + t))
             nc.scalar.copy(out=h_half[8 + t][:], in_=acc[:])
+
+        def front_put(t, k):
+            put_in_page(4 + t, 2 * P * k, 2 * P, h_front[k][:, t, :], wgs_dealt[t])
 
         below, z_lower = {}, {}
 
@@ -386,16 +389,19 @@ def tile_list_strata_contacts_kernel(
             lower_step(4 + c)
             if c >= 1:
                 chunk_sum(c - 1)
+            if c == 2:
+                front_put(0, 0)
             chunk_third(c)
             chunk_excess(c)
-        chunk_back(3)
         lower_z(2)
-        chunk_sum(3)
         lower_below(3)
-        put_in_page(4, 0, h_front[:, 0, :], wgs_dealt[0])
+        front_put(1, 0)
         lower_z(3)
-        for t in (1, 2):
-            put_in_page(4 + t, 0, h_front[:, t, :], wgs_dealt[t])
+        front_put(2, 0)
+        chunk_back(3)
+        chunk_sum(3)
+        for t in range(3):
+            front_put(t, 1)
         for c in range(4, 8):
             for stage in (chunk_products, chunk_third, chunk_excess, chunk_back):
                 stage(c)
@@ -410,7 +416,7 @@ def tile_list_strata_contacts_kernel(
             quant[name, a] = quantize(rounded[name, a], f"{name}{a}")
 
         def back_put(t):
-            put_in_page(4 + t, 1, h_half[8 + t][:], wgs_dealt[t])
+            put_in_page(4 + t, HALF, HALF, h_half[8 + t][:], wgs_dealt[t])
 
         upper_below = {}
 
@@ -464,7 +470,8 @@ def tile_list_strata_contacts_kernel(
         z_front = placed("z_front", [P, 2, M], F32, LATE_RAW)
         fetch_minus(4, list3, 0, M, upper_below[0][:], z_front[:, 0, :])
         quantize_operand("g", 0)
-        put_in_page(7, 0, h_front[:, 3, :], wgs_dealt[3])
+        front_put(3, 0)
+        front_put(3, 1)
         slab_sum(2, "back")
         back_put(2)
         round_operand("w6", 0)
@@ -476,11 +483,13 @@ def tile_list_strata_contacts_kernel(
         quantize_operand("w4", 0)
         third_z(0)
         third_z(1)
-        for name in ("g", "w6", "w4"):
-            round_operand(name, 1)
-            quantize_operand(name, 1)
+        round_operand("g", 1)
+        quantize_operand("g", 1)
         slab_sum(3, "d3")
         back_put(3)
+        for name in ("w4", "w6"):
+            round_operand(name, 1)
+            quantize_operand(name, 1)
 
         def round_pair(grouped, u, planes):
             nc.scalar.copy(
@@ -524,7 +533,7 @@ def tile_list_strata_contacts_kernel(
 
         def last_fetch_below(q):
             if q < 2:
-                last_below[q] = held(f"last_below{q}", [P, P], F32)
+                last_below[q] = placed(f"last_below{q}", [P, P], F32, (LATE_RAW + 8192, W1_RAW + 8192)[q])
             else:
                 last_below[q] = placed(f"last_below{q}", [P, P], F32, W1_GROUPED + 4096 + 512 * (q - 2))
             fetch_minus(7, list4, P * q, P, raw["g", 1][:, 3, P * q : P * (q + 1)], last_below[q][:])

@@ -41,6 +41,7 @@ CHUNK_TERMS = EXCESS + 2 * TERM
 H_HALVES = CHUNK_TERMS + 12 * TERM
 H_FRONT = H_HALVES + 8 * TERM
 THIRD_PAGE = H_FRONT + 4 * TERM
+Z_DEALT = THIRD_PAGE + 4 * TERM
 
 
 def tile_list_strata_contacts_kernel(
@@ -284,6 +285,7 @@ def tile_list_strata_contacts_kernel(
 
         chunk_terms, minus_d2, excess = {}, {}, {}
         h_front = [placed(f"h_front{k}", [P, 4, 2 * P], F32, H_FRONT + 2 * TERM * k) for k in range(2)]
+        h_front.append(placed("h_front2", [P, 3, 2 * P], F32, H_HALVES))
 
         def chunk_slot(c, n):
             return CHUNK_TERMS + TERM * (3 * (c % 4) + n)
@@ -317,16 +319,21 @@ def tile_list_strata_contacts_kernel(
                 nc.scalar.copy(out=back[:], in_=acc[:])
                 chunk_terms[c].append(back)
 
-        def chunk_sum(c):
+        def chunk_sum(c, slabs):
             acc = bank("sum")
-            transposed_sum(acc, chunk_terms[c])
-            nc.scalar.copy(out=h_front[c // 2][:, :, P * (c % 2) : P * (c % 2 + 1)], in_=acc[:].rearrange("p (t j) -> p t j", t=4))
+            turn_and_add(acc, [[tile[:, P * t : P * (t + 1)] for tile in chunk_terms[c]] for t in range(slabs)])
+            nc.scalar.copy(
+                out=h_front[c // 2][:, 0:slabs, P * (c % 2) : P * (c % 2 + 1)],
+                in_=acc[:, 0 : P * slabs].rearrange("p (t j) -> p t j", t=slabs),
+            )
 
         def slab_sum(t, tag):
             acc = bank(tag)
-            turn_and_add(acc, [[tile[:, P * t : P * (t + 1)] for tile in chunk_terms[c]] for c in range(4, 8)])
-            h_half[8 + t] = term(f"h_back{t}", H_HALVES + TERM * (4 + t))
-            nc.scalar.copy(out=h_half[8 + t][:], in_=acc[:])
+            chunks = range(6, 8) if t < 3 else range(4, 8)
+            turn_and_add(acc, [[tile[:, P * t : P * (t + 1)] for tile in chunk_terms[c]] for c in chunks])
+            width = P * len(chunks)
+            h_half[8 + t] = placed(f"h_back{t}", [P, width], F32, H_HALVES + TERM * (4 + t) if t < 3 else Z_DEALT + 4096)
+            nc.scalar.copy(out=h_half[8 + t][:], in_=acc[:, 0:width])
 
         def front_put(t, k):
             put_in_page(4 + t, 2 * P * k, 2 * P, h_front[k][:, t, :], wgs_dealt[t])
@@ -341,6 +348,8 @@ def tile_list_strata_contacts_kernel(
             offset = (FIRST_TERMS + 3 * TERM, FIRST_TERMS + 5 * TERM, FIRST_TERMS + TERM, SECOND_TERMS)[b]
             z_lower[b] = term(f"z_lower{b}", offset)
             fetch_minus(b, list3, 0, M, below[b][:], z_lower[b][:])
+            for t in range(4):
+                nc.sync.dma_start(out=raw["z", 0][32 * b : 32 * (b + 1), t, :], in_=z_lower[b][t:P:4, :])
 
         def lower_step(u):
             lower_sum(u)
@@ -372,7 +381,7 @@ def tile_list_strata_contacts_kernel(
             in_=w5_s[:].rearrange("p a (m t) -> p a t m", t=4),
         )
         lower_step(2)
-        raw = {}
+        raw = {("z", 0): placed("z_dealt", [P, 4, M], F32, Z_DEALT)}
         for name, source, a, offset in (
             ("g", hiatus, 0, LATE_RAW), ("w6", w6, 0, W1_RAW), ("w4", w4, 0, W1_GROUPED), ("g", hiatus, 1, None),
             ("w6", w6, 1, W1_RAW + 8192), ("w4", w4, 1, LATE_RAW + 8192),
@@ -388,7 +397,7 @@ def tile_list_strata_contacts_kernel(
             chunk_products(c)
             lower_step(4 + c)
             if c >= 1:
-                chunk_sum(c - 1)
+                chunk_sum(c - 1, 4)
             if c == 2:
                 front_put(0, 0)
             chunk_third(c)
@@ -399,24 +408,30 @@ def tile_list_strata_contacts_kernel(
         lower_z(3)
         front_put(2, 0)
         chunk_back(3)
-        chunk_sum(3)
+        chunk_sum(3, 4)
         for t in range(3):
             front_put(t, 1)
         for c in range(4, 8):
             for stage in (chunk_products, chunk_third, chunk_excess, chunk_back):
                 stage(c)
+            if c < 6:
+                chunk_sum(c, 3)
+            if c == 5:
+                for t in range(3):
+                    front_put(t, 2)
 
         quant, rounded = {}, {}
 
-        def round_operand(name, a):
-            grouped = placed(f"{name}_grouped{a}", [P, 4 * 512], BF16, STAGE1 + 4096 * len(rounded))
-            rounded[name, a] = round_rows(raw[name, a], grouped, name != "g")
+        def round_operand(name, a, offset):
+            grouped = placed(f"{name}_grouped{a}", [P, 4 * 512], BF16, offset)
+            rounded[name, a] = round_rows(raw[name, a], grouped, name in ("w4", "w6"))
 
         def quantize_operand(name, a):
             quant[name, a] = quantize(rounded[name, a], f"{name}{a}")
 
         def back_put(t):
-            put_in_page(4 + t, HALF, HALF, h_half[8 + t][:], wgs_dealt[t])
+            width = h_half[8 + t].shape[1]
+            put_in_page(4 + t, S - width, width, h_half[8 + t][:], wgs_dealt[t])
 
         upper_below = {}
 
@@ -424,36 +439,10 @@ def tile_list_strata_contacts_kernel(
             upper_below[t] = term(f"upper_below{t}", offset)
             fetch_minus(4 + t, list4, 0, M, raw["g", 1][:, t, :], upper_below[t][:])
 
-        z_pairs = [placed(f"z_pairs{hf}", [P, 2, 2, 2 * P], BF16, MINUS_D2 + TERM * hf) for hf in range(2)]
-
-        def turn_z_lower(b):
-            z_ps = bank(("first", "second")[b % 2])
-            transposed_sum(z_ps, (z_lower[b],))
-            for x in range(2):
-                nc.scalar.copy(
-                    out=z_pairs[x][:, :, :, 64 * b : 64 * (b + 1)].rearrange("m c u (p e) -> m c u p e", e=2),
-                    in_=z_ps[:, 256 * x : 256 * (x + 1)].rearrange("m (c p u e) -> m c u p e", c=2, u=2, e=2),
-                )
-
-        def turn_z_back():
-            grouped = placed("z_lower_grouped", [P, 4 * M], BF16, EXCESS)
-            for hf in range(2):
-                words = z_pairs[hf][:].bitcast(F32)
-                back = bank(("d1", "d2")[hf])
-                for c in range(2):
-                    for e in range(2):
-                        col = P * (2 * c + e)
-                        nc.tensor.transpose(back[:, col : col + P], words[:, c, e, :], ident[:])
-                nc.scalar.copy(
-                    out=grouped[:, 1024 * hf : 1024 * (hf + 1)].bitcast(F32).rearrange("p (c m u) -> p c m u", c=2, u=2),
-                    in_=back[:].rearrange("p (c u m) -> p c m u", c=2, u=2),
-                )
-            return grouped
-
         z_back = {}
 
         def third_z(q):
-            offset = W1_GROUPED + 4096 + 1024 * q if q < 2 else H_HALVES + 7 * TERM + 1024 * (q - 2)
+            offset = W1_GROUPED + 4096 + 1024 * q if q < 2 else Z_DEALT + 4096 + 1024 * (q - 2)
             z_back[q] = placed(f"z_back{q}", [P, 2, P], F32, offset)
             fetch_minus(6, list3, P * q, P, upper_below[2][:, P * q : P * (q + 1)], z_back[q][:, 0, :])
 
@@ -461,42 +450,36 @@ def tile_list_strata_contacts_kernel(
         back_put(0)
         slab_sum(1, "excess")
         back_put(1)
-        for b in range(4):
-            turn_z_lower(b)
-        z_lower_grouped = turn_z_back()
-        upper_fetch_below(0, MINUS_D2 + TERM)
-        quant["z", 0] = quantize(z_lower_grouped, "z0")
-        round_operand("g", 0)
-        z_front = placed("z_front", [P, 2, M], F32, LATE_RAW)
-        fetch_minus(4, list3, 0, M, upper_below[0][:], z_front[:, 0, :])
+        round_operand("g", 0, STAGE1)
+        upper_fetch_below(0, LATE_RAW)
         quantize_operand("g", 0)
+        round_operand("w6", 0, STAGE1 + 4096)
+        z_front = placed("z_front", [P, 2, M], F32, W1_RAW)
+        fetch_minus(4, list3, 0, M, upper_below[0][:], z_front[:, 0, :])
+        quantize_operand("w6", 0)
         front_put(3, 0)
+        upper_fetch_below(1, W1_RAW + 4096)
         front_put(3, 1)
+        fetch_minus(5, list3, 0, M, upper_below[1][:], z_front[:, 1, :])
         slab_sum(2, "back")
         back_put(2)
-        round_operand("w6", 0)
-        upper_fetch_below(1, W1_RAW)
-        quantize_operand("w6", 0)
-        fetch_minus(5, list3, 0, M, upper_below[1][:], z_front[:, 1, :])
-        round_operand("w4", 0)
+        for n, (name, a) in enumerate((("g", 1), ("w6", 1), ("w4", 1), ("z", 0))):
+            round_operand(name, a, STAGE1 + 4096 * (2 + n))
+            quantize_operand(name, a)
+        round_operand("w4", 0, Z_DEALT)
         upper_fetch_below(2, W1_GROUPED)
         quantize_operand("w4", 0)
         third_z(0)
         third_z(1)
-        round_operand("g", 1)
-        quantize_operand("g", 1)
         slab_sum(3, "d3")
         back_put(3)
-        for name in ("w4", "w6"):
-            round_operand(name, 1)
-            quantize_operand(name, 1)
 
         def round_pair(grouped, u, planes):
             nc.scalar.copy(
                 out=grouped[:].rearrange("p (m u e) -> p u m e", u=2, e=2)[:, u], in_=planes.rearrange("p e m -> p m e")
             )
 
-        z_grouped = [placed(f"z_grouped{q}", [P, 4 * P], BF16, STAGE1 + 3 * 4096 + 1024 * q) for q in range(4)]
+        z_grouped = [placed(f"z_grouped{q}", [P, 4 * P], BF16, Z_DEALT + 1024 * q) for q in range(4)]
         for q in range(4):
             round_pair(z_grouped[q], 0, z_front[:, :, P * q : P * (q + 1)])
 
@@ -520,20 +503,19 @@ def tile_list_strata_contacts_kernel(
         sums, gates = {}, {}
         for q, tag in enumerate(("first", "second", "d1", "d2")):
             sums[q] = bank(tag)
-            mx_passes(sums[q], "w5", 0, q, True, False)
-        for q in range(4):
-            mx_passes(sums[q], "w6", 0, q, False, False)
+            mx_passes(sums[q], "w6", 0, q, True, False)
+        for name, a in (("w6", 1), ("w5", 0)):
+            for q in range(4):
+                mx_passes(sums[q], name, a, q, False, False)
         for q, tag in enumerate(("sum", "excess", "back", "d3")):
             gates[q] = bank(tag)
             mx_passes(gates[q], "w4", 0, q, True, False)
-        for q in range(4):
-            mx_passes(sums[q], "w6", 1, q, False, False)
 
         last_below = {}
 
         def last_fetch_below(q):
             if q < 2:
-                last_below[q] = placed(f"last_below{q}", [P, P], F32, (LATE_RAW + 8192, W1_RAW + 8192)[q])
+                last_below[q] = held(f"last_below{q}", [P, P], F32)
             else:
                 last_below[q] = placed(f"last_below{q}", [P, P], F32, W1_GROUPED + 4096 + 512 * (q - 2))
             fetch_minus(7, list4, P * q, P, raw["g", 1][:, 3, P * q : P * (q + 1)], last_below[q][:])

@@ -52,7 +52,6 @@ def tile_list_strata_contacts_kernel(
     with ExitStack() as ctx:
         keep = ctx.enter_context(tc.tile_pool(name="keep", bufs=1))
         shared = ctx.enter_context(tc.tile_pool(name="shared", bufs=1))
-        pair = ctx.enter_context(tc.tile_pool(name="pair", bufs=2))
         psum = ctx.enter_context(tc.psum_pool(name="psum", bufs=1))
 
         def held(name, shape, dtype):
@@ -129,14 +128,17 @@ def tile_list_strata_contacts_kernel(
         nc.sync.dma_start(out=w2_rest[:], in_=w2_dram[:, W2_FIRST:H])
         nc.sync.dma_start(list4[:], offs4)
         nc.sync.dma_start(list3[:], offs3)
+        raw = {}
         for b in range(4):
             nc.sync.dma_start(out=hiatus_rows[b][:], in_=hiatus[P * b : P * (b + 1), :])
+            if b == 0:
+                raw["g", 0] = load_rows(hiatus[0:512, :], placed("g_raw0", [P, 4, M], F32, LATE_RAW))
 
         def round_rows(raw, grouped, dealt, negated=False):
             width = raw.shape[2]
             if dealt:
-                dst = grouped[:].rearrange("p (t m j) -> p m t j", t=4, j=4)
-                src = raw[:].rearrange("p j (m t) -> p m t j", t=4)
+                dst = grouped[:].rearrange("p (t m j) -> p m j t", t=4, j=4)
+                src = raw[:].rearrange("p j (m t) -> p m j t", t=4)
             else:
                 dst = grouped[:].rearrange("p (c i j) -> p c j i", i=4, j=4)
                 src = raw[:].rearrange("p j (c i) -> p c j i", i=4)
@@ -338,6 +340,15 @@ def tile_list_strata_contacts_kernel(
         def front_put(t, k):
             put_in_page(4 + t, 2 * P * k, 2 * P, h_front[k][:, t, :], wgs_dealt[t])
 
+        quant, rounded = {}, {}
+
+        def round_operand(name, a, offset):
+            grouped = placed(f"{name}_grouped{a}", [P, 4 * 512], BF16, offset)
+            rounded[name, a] = round_rows(raw[name, a], grouped, name in ("w4", "w6"))
+
+        def quantize_operand(name, a):
+            quant[name, a] = quantize(rounded[name, a], f"{name}{a}")
+
         below, z_lower = {}, {}
 
         def lower_below(b):
@@ -381,9 +392,9 @@ def tile_list_strata_contacts_kernel(
             in_=w5_s[:].rearrange("p a (m t) -> p a t m", t=4),
         )
         lower_step(2)
-        raw = {("z", 0): placed("z_dealt", [P, 4, M], F32, Z_DEALT)}
+        raw["z", 0] = placed("z_dealt", [P, 4, M], F32, Z_DEALT)
         for name, source, a, offset in (
-            ("g", hiatus, 0, LATE_RAW), ("w6", w6, 0, W1_RAW), ("w4", w4, 0, W1_GROUPED), ("g", hiatus, 1, None),
+            ("w6", w6, 0, W1_RAW), ("w4", w4, 0, W1_GROUPED), ("g", hiatus, 1, None),
             ("w6", w6, 1, W1_RAW + 8192), ("w4", w4, 1, LATE_RAW + 8192),
         ):
             shape = [P, 4, 512]
@@ -402,6 +413,9 @@ def tile_list_strata_contacts_kernel(
                 front_put(0, 0)
             chunk_third(c)
             chunk_excess(c)
+            if c == 1:
+                round_operand("g", 0, chunk_slot(3, 0))
+                quantize_operand("g", 0)
         lower_z(2)
         lower_below(3)
         front_put(1, 0)
@@ -420,15 +434,6 @@ def tile_list_strata_contacts_kernel(
                 for t in range(3):
                     front_put(t, 2)
 
-        quant, rounded = {}, {}
-
-        def round_operand(name, a, offset):
-            grouped = placed(f"{name}_grouped{a}", [P, 4 * 512], BF16, offset)
-            rounded[name, a] = round_rows(raw[name, a], grouped, name in ("w4", "w6"))
-
-        def quantize_operand(name, a):
-            quant[name, a] = quantize(rounded[name, a], f"{name}{a}")
-
         def back_put(t):
             width = h_half[8 + t].shape[1]
             put_in_page(4 + t, S - width, width, h_half[8 + t][:], wgs_dealt[t])
@@ -442,7 +447,7 @@ def tile_list_strata_contacts_kernel(
         z_back = {}
 
         def third_z(q):
-            offset = W1_GROUPED + 4096 + 1024 * q if q < 2 else Z_DEALT + 4096 + 1024 * (q - 2)
+            offset = W1_GROUPED + 4096 + 1024 * q
             z_back[q] = placed(f"z_back{q}", [P, 2, P], F32, offset)
             fetch_minus(6, list3, P * q, P, upper_below[2][:, P * q : P * (q + 1)], z_back[q][:, 0, :])
 
@@ -450,17 +455,15 @@ def tile_list_strata_contacts_kernel(
         back_put(0)
         slab_sum(1, "excess")
         back_put(1)
-        round_operand("g", 0, STAGE1)
-        upper_fetch_below(0, LATE_RAW)
-        quantize_operand("g", 0)
         round_operand("w6", 0, STAGE1 + 4096)
+        upper_fetch_below(0, W1_RAW + 3 * TERM)
+        quantize_operand("w6", 0)
         z_front = placed("z_front", [P, 2, M], F32, W1_RAW)
         fetch_minus(4, list3, 0, M, upper_below[0][:], z_front[:, 0, :])
-        quantize_operand("w6", 0)
+        upper_fetch_below(1, W1_RAW + 2 * TERM)
         front_put(3, 0)
-        upper_fetch_below(1, W1_RAW + 4096)
-        front_put(3, 1)
         fetch_minus(5, list3, 0, M, upper_below[1][:], z_front[:, 1, :])
+        front_put(3, 1)
         slab_sum(2, "back")
         back_put(2)
         for n, (name, a) in enumerate((("g", 1), ("w6", 1), ("w4", 1), ("z", 0))):
@@ -470,9 +473,9 @@ def tile_list_strata_contacts_kernel(
         upper_fetch_below(2, W1_GROUPED)
         quantize_operand("w4", 0)
         third_z(0)
-        third_z(1)
         slab_sum(3, "d3")
         back_put(3)
+        third_z(1)
 
         def round_pair(grouped, u, planes):
             nc.scalar.copy(
@@ -538,6 +541,7 @@ def tile_list_strata_contacts_kernel(
         out_words = out_1[0].rearrange("p m t -> p (m t)").bitcast(I32)
         y_c = held("y_c", [P, M], U32)
         y_s = held("y_s", [P, M], U8)
+        ys = []
         mx_passes(gates[0], "w4", 1, 0, False, True)
         for q in range(4):
             cols = slice(P * q, P * (q + 1))
@@ -546,16 +550,20 @@ def tile_list_strata_contacts_kernel(
             mx_passes(sums[q], "w5", 1, q, False, True)
             gate = placed(f"gate{q}", [P, 512], F32, CHUNK_TERMS + TERM * q)
             nc.scalar.activation(out=gate[:], in_=gates[q][:], func=ACT.Tanh)
-            y = placed(f"y{q}", [P, 4, P], F32, CHUNK_TERMS + TERM * (4 + q))
-            nc.vector.tensor_tensor(out=y[:].rearrange("p t m -> p (t m)"), in0=sums[q][:], in1=gate[:], op=ALU.mult)
-            nc.sync.dma_start(out=out_rows[:, :, cols], in_=y[:])
-            y_grouped = pair.tile([P, 4 * P], BF16, name="y_grouped", align_bytes=64)
+            ys.append(placed(f"y{q}", [P, 4, P], F32, CHUNK_TERMS + TERM * (4 + q)))
+            nc.vector.tensor_tensor(out=ys[q][:].rearrange("p t m -> p (t m)"), in0=sums[q][:], in1=gate[:], op=ALU.mult)
+            nc.sync.dma_start(out=out_rows[:, :, cols], in_=ys[q][:])
+        for q, y in enumerate(ys):
+            cols = slice(P * q, P * (q + 1))
+            y_grouped = placed(f"y_grouped{q}", [P, 4 * P], BF16, CHUNK_TERMS + 8 * TERM + 1024 * q)
             (nc.scalar.copy if q < 3 else nc.vector.tensor_copy)(
                 out=y_grouped[:].rearrange("p (c i t) -> p c t i", i=4, t=4),
                 in_=y[:].rearrange("p t (c i) -> p c t i", i=4),
             )
             nc.vector.quantize_mx(out=y_c[:, cols].bitcast(FP8X4), scales=y_s[:, cols], in_=y_grouped[:])
-            nc.sync.dma_start(out=out_words[:, cols], in_=y_c[:, cols].bitcast(I32))
+            if q % 2 == 1:
+                both = slice(P * (q - 1), P * (q + 1))
+                nc.sync.dma_start(out=out_words[:, both], in_=y_c[:, both].bitcast(I32))
         for q in range(4):
             queue = (nc.scalar, nc.sync)[q % 2]
             queue.dma_start(out=out_2[0][4 * q : 4 * q + 4].bitcast(I32), in_=y_s[32 * q : 32 * q + 4].bitcast(I32))

@@ -149,9 +149,9 @@ def tile_list_strata_contacts_kernel(
                     nc.scalar.copy(out=dst[:, c0 : c0 + ROUND_GROUPS], in_=src[:, c0 : c0 + ROUND_GROUPS])
             return grouped
 
-        def quantize(grouped, name):
+        def quantize(grouped, name, offset=None):
             width = grouped.shape[1] // 4
-            codes = held(name + "_c", [P, width], U32)
+            codes = held(name + "_c", [P, width], U32) if offset is None else placed(name + "_c", [P, width], U32, offset)
             scales = held(name + "_s", [P, width], U8)
             nc.vector.quantize_mx(out=codes[:].bitcast(FP8X4), scales=scales[:], in_=grouped[:])
             return codes, scales
@@ -446,10 +446,10 @@ def tile_list_strata_contacts_kernel(
 
         z_back = {}
 
-        def third_z(q):
-            offset = W1_GROUPED + 4096 + 1024 * q
-            z_back[q] = placed(f"z_back{q}", [P, 2, P], F32, offset)
-            fetch_minus(6, list3, P * q, P, upper_below[2][:, P * q : P * (q + 1)], z_back[q][:, 0, :])
+        def third_z(hf):
+            z_back[hf] = placed(f"z_back{hf}", [P, 2, 2 * P], F32, LATE_RAW + TERM * hf)
+            cols = slice(2 * P * hf, 2 * P * (hf + 1))
+            fetch_minus(6, list3, 2 * P * hf, 2 * P, upper_below[2][:, cols], z_back[hf][:, 0, :])
 
         slab_sum(0, "sum")
         back_put(0)
@@ -466,23 +466,25 @@ def tile_list_strata_contacts_kernel(
         front_put(3, 1)
         slab_sum(2, "back")
         back_put(2)
-        for n, (name, a) in enumerate((("g", 1), ("w6", 1), ("w4", 1), ("z", 0))):
-            round_operand(name, a, STAGE1 + 4096 * (2 + n))
-            quantize_operand(name, a)
-        round_operand("w4", 0, Z_DEALT)
-        upper_fetch_below(2, W1_GROUPED)
-        quantize_operand("w4", 0)
+        for n, name in enumerate(("g", "w6", "w4")):
+            round_operand(name, 1, STAGE1 + 4096 * (2 + n))
+            quantize_operand(name, 1)
+        round_operand("z", 0, STAGE1 + 5 * 4096)
+        upper_fetch_below(2, Z_DEALT + 3 * TERM)
+        quantize_operand("z", 0)
         third_z(0)
+        third_z(1)
         slab_sum(3, "d3")
         back_put(3)
-        third_z(1)
+        round_operand("w4", 0, Z_DEALT)
+        quantize_operand("w4", 0)
 
         def round_pair(grouped, u, planes):
             nc.scalar.copy(
                 out=grouped[:].rearrange("p (m u e) -> p u m e", u=2, e=2)[:, u], in_=planes.rearrange("p e m -> p m e")
             )
 
-        z_grouped = [placed(f"z_grouped{q}", [P, 4 * P], BF16, Z_DEALT + 1024 * q) for q in range(4)]
+        z_grouped = [placed(f"z_grouped{q}", [P, 4 * P], BF16, W1_GROUPED + 4096 + 1024 * q) for q in range(4)]
         for q in range(4):
             round_pair(z_grouped[q], 0, z_front[:, :, P * q : P * (q + 1)])
 
@@ -506,36 +508,30 @@ def tile_list_strata_contacts_kernel(
         sums, gates = {}, {}
         for q, tag in enumerate(("first", "second", "d1", "d2")):
             sums[q] = bank(tag)
-            mx_passes(sums[q], "w6", 0, q, True, False)
-        for name, a in (("w6", 1), ("w5", 0)):
+            mx_passes(sums[q], "w5", 0, q, True, False)
+        for a in range(2):
             for q in range(4):
-                mx_passes(sums[q], name, a, q, False, False)
+                mx_passes(sums[q], "w6", a, q, False, False)
         for q, tag in enumerate(("sum", "excess", "back", "d3")):
             gates[q] = bank(tag)
             mx_passes(gates[q], "w4", 0, q, True, False)
 
         last_below = {}
 
-        def last_fetch_below(q):
-            if q < 2:
-                last_below[q] = held(f"last_below{q}", [P, P], F32)
-            else:
-                last_below[q] = placed(f"last_below{q}", [P, P], F32, W1_GROUPED + 4096 + 512 * (q - 2))
-            fetch_minus(7, list4, P * q, P, raw["g", 1][:, 3, P * q : P * (q + 1)], last_below[q][:])
+        def last_fetch_below(hf):
+            last_below[hf] = placed(f"last_below{hf}", [P, 2 * P], F32, W1_GROUPED + 1024 * hf)
+            fetch_minus(7, list4, 2 * P * hf, 2 * P, raw["g", 1][:, 3, 2 * P * hf : 2 * P * (hf + 1)], last_below[hf][:])
 
         def last_z(q):
-            fetch_minus(7, list3, P * q, P, last_below[q][:], z_back[q][:, 1, :])
-            round_pair(z_grouped[q], 1, z_back[q][:])
-            quant["z", 1, q] = quantize(z_grouped[q], f"z1{q}")
+            hf, cols = q // 2, slice(P * (q % 2), P * (q % 2 + 1))
+            fetch_minus(7, list3, P * q, P, last_below[hf][:, cols], z_back[hf][:, 1, cols])
+            round_pair(z_grouped[q], 1, z_back[hf][:, :, cols])
+            quant["z", 1, q] = quantize(z_grouped[q], f"z1{q}", CHUNK_TERMS + 8 * TERM + 768 if q == 3 else None)
 
-        for q in range(2):
-            last_fetch_below(q)
-            third_z(q + 2)
+        last_fetch_below(0)
+        last_fetch_below(1)
+        for q in range(4):
             last_z(q)
-        last_fetch_below(2)
-        last_fetch_below(3)
-        last_z(2)
-        last_z(3)
 
         out_rows = out_0.rearrange("(p t) m -> p t m", t=4)
         out_words = out_1[0].rearrange("p m t -> p (m t)").bitcast(I32)
@@ -556,7 +552,7 @@ def tile_list_strata_contacts_kernel(
         for q, y in enumerate(ys):
             cols = slice(P * q, P * (q + 1))
             y_grouped = placed(f"y_grouped{q}", [P, 4 * P], BF16, CHUNK_TERMS + 8 * TERM + 1024 * q)
-            (nc.scalar.copy if q < 3 else nc.vector.tensor_copy)(
+            (nc.scalar.copy if q < 2 else nc.vector.tensor_copy)(
                 out=y_grouped[:].rearrange("p (c i t) -> p c t i", i=4, t=4),
                 in_=y[:].rearrange("p t (c i) -> p c t i", i=4),
             )

@@ -21,27 +21,24 @@ P = 128
 HALF = 512
 W1_PIECE = 256
 FIRST_PARTS = (slice(0, 256), slice(256, 512))
-W2_FIRST = 256
 GPSIMD_CLEARS = 576
 ROUND_GROUPS = 32
-RELU_CHUNKS = (4, 6)
-VECTOR_MAX_UNITS = (2, 3)
+UNITS = 16
+RELU_UNITS = (1, 2, 4, 6, 9, 11, 13)
+DEAL_UNIT = 5
+LATE_OPERANDS = {9: ("g", 0, 5), 11: ("w6", 0, 7), 12: ("g", 1, 9), 13: ("w6", 1, 11)}
 
 TERM = 2048
 TAB_WORDS, TAB_SCALES = 0, 16384
 W1_RAW = 20480
-W1_GROUPED = W1_RAW + 16384
-LATE_RAW = W1_GROUPED + 8192
-STAGE1 = LATE_RAW + 16384
-FIRST_TERMS = STAGE1 + 6 * 4096
-SECOND_TERMS = FIRST_TERMS + 7 * TERM
-MINUS_D2 = SECOND_TERMS + 2 * TERM
-EXCESS = MINUS_D2 + 2 * TERM
-CHUNK_TERMS = EXCESS + 2 * TERM
-H_HALVES = CHUNK_TERMS + 12 * TERM
-H_FRONT = H_HALVES + 8 * TERM
-THIRD_PAGE = H_FRONT + 4 * TERM
-Z_DEALT = THIRD_PAGE + 4 * TERM
+G_RAW = W1_RAW + 8 * TERM
+W6_RAW = G_RAW + 8 * TERM
+ODD_TERMS = W6_RAW + 8 * TERM
+EVEN_FIRST = ODD_TERMS + 16 * TERM
+EVEN_SECOND = EVEN_FIRST + 7 * TERM
+PRODUCTS = EVEN_SECOND + 7 * TERM
+H_RING = PRODUCTS + 9 * TERM
+Z_DEALT = H_RING + 6 * TERM
 
 
 def tile_list_strata_contacts_kernel(
@@ -60,6 +57,9 @@ def tile_list_strata_contacts_kernel(
         def placed(name, shape, dtype, offset):
             return shared.tile(shape, dtype, name=name, offset=offset, align_bytes=64)
 
+        def term(name, offset):
+            return placed(name, [P, 512], F32, offset)
+
         def bank(tag):
             return psum.tile([P, 512], F32, name=tag)
 
@@ -67,7 +67,8 @@ def tile_list_strata_contacts_kernel(
             for q in range(4):
                 queue.dma_start(out=plane[32 * q : 32 * q + 4].bitcast(I32), in_=rows[4 * q : 4 * q + 4].bitcast(I32))
 
-        def load_rows(rows, raw):
+        def load_rows(name, rows, offset):
+            raw = placed(name, [P, 4, rows.shape[1]], F32, offset)
             nc.sync.dma_start(out=raw[:], in_=rows.rearrange("(p j) w -> p j w", j=4))
             return raw
 
@@ -77,71 +78,64 @@ def tile_list_strata_contacts_kernel(
         list4 = held("list4", [P, M // 16], U16)
         tab_w = placed("tab_w", [P, T], I32, TAB_WORDS)
         tab_s = placed("tab_s", [P, T], U8, TAB_SCALES)
-        minus_w1_c = placed("minus_w1_c", [P, H], U32, STAGE1)
-        w2_first = placed("w2_first", [P, W2_FIRST], I32, STAGE1 + 4096)
-        w2_rest = placed("w2_rest", [P, H - W2_FIRST], I32, STAGE1 + 4096 + 4 * W2_FIRST)
-        v_w = [placed(f"v_w{hf}", [P, HALF], U32, STAGE1 + 2 * 4096 + TERM * hf) for hf in range(2)]
-        w3_w = placed("w3_w", [P, 2 * H], U8, STAGE1 + 3 * 4096)
-        minus_w1_s = placed("minus_w1_s", [P, H], U8, STAGE1 + 4 * 4096)
-        w2_s = placed("w2_s", [P, H], U8, STAGE1 + 4 * 4096 + H)
-        w3_s = placed("w3_s", [P, H], U8, STAGE1 + 5 * 4096)
-        v_s = [placed(f"v_s{hf}", [P, HALF], U8, STAGE1 + 5 * 4096 + H + HALF * hf) for hf in range(2)]
-        hiatus_rows = [placed(f"hiatus_rows{b}", [P, M], F32, STAGE1 + (3 + b) * 4096 + TERM) for b in range(3)]
-        hiatus_rows.append(held("hiatus_rows3", [P, M], F32))
+        v_w = [held(f"v_w{hf}", [P, HALF], U32) for hf in range(2)]
+        v_s = [held(f"v_s{hf}", [P, HALF], U8) for hf in range(2)]
+        minus_w1_c = held("minus_w1_c", [P, H], U32)
+        minus_w1_s = held("minus_w1_s", [P, H], U8)
+        w2_first = held("w2_first", [P, W1_PIECE], I32)
+        w2_rest = held("w2_rest", [P, H - W1_PIECE], I32)
+        w3_w = held("w3_w", [P, 2 * H], U8)
+        w23_s = held("w23_s", [P, 2 * H], U8)
         w5_s = held("w5_s", [P, 2, N], U8)
         w5_w = held("w5_w", [P, 2, 2 * N], U8)
         wgs_sb = held("wgs_sb", [P, S], F32)
+        hiatus_rows = [held(f"hiatus_rows{b}", [P, M], F32) for b in range(4)]
         pages = [held(f"page{i}", [P, T2], F32) for i in range(2)]
         ident = held("ident", [P, P], F32)
 
-        nc.gpsimd.memset(w2_s[:].bitcast(I32), 0)
+        nc.gpsimd.memset(w23_s[:, 0:H].bitcast(I32), 0)
         nc.gpsimd.memset(tab_s[:].bitcast(I32)[:, 0:GPSIMD_CLEARS], 0)
         nc.vector.memset(tab_s[:].bitcast(I32)[:, GPSIMD_CLEARS:], 0)
-        nc.vector.memset(w3_s[:].bitcast(I32), 0)
+        nc.vector.memset(w23_s[:, H : 2 * H].bitcast(I32), 0)
         nc.vector.memset(w5_s[:].bitcast(I32), 0)
-        load_scale_rows(nc.gpsimd, w3_s, w3_scales[0])
+        load_scale_rows(nc.gpsimd, w23_s[:, H : 2 * H], w3_scales[0])
         make_identity(nc, ident[:])
         for page in pages:
             nc.vector.memset(page[:], 0.0)
 
-        def load_w1(i):
-            raw = placed(f"w1_raw{i}", [P, 4, W1_PIECE], F32, W1_RAW + 4096 * i)
-            return load_rows(w1[:, W1_PIECE * i : W1_PIECE * (i + 1)], raw)
-
         tab_w_dram = tab_words[0].rearrange("p t i -> p (t i)").bitcast(I32)
         w2_dram = w2_words[0].rearrange("p c i -> p (c i)").bitcast(I32)
+        raw = {}
         nc.sync.dma_start(list1[:], offs)
         nc.sync.dma_start(out=tab_w[:, 0 : T // 4], in_=tab_w_dram[:, 0 : T // 4])
         load_scale_rows(nc.sync, tab_s, tab_scales[0])
-        w1_raw = [load_w1(0)]
+        raw["w1", 0] = load_rows("w1_raw0", w1[:, 0:W1_PIECE], W1_RAW)
         nc.sync.dma_start(out=tab_w[:, T // 4 : T], in_=tab_w_dram[:, T // 4 : T])
-        nc.sync.dma_start(out=w2_first[:], in_=w2_dram[:, 0:W2_FIRST])
+        nc.sync.dma_start(out=w2_first[:], in_=w2_dram[:, 0:W1_PIECE])
         nc.sync.dma_start(out=w3_w[:].bitcast(I32), in_=w3_words[0].bitcast(I32))
-        load_scale_rows(nc.sync, w2_s, w2_scales[0])
+        load_scale_rows(nc.sync, w23_s[:, 0:H], w2_scales[0])
         nc.sync.dma_start(list2[:], offs2)
         nc.sync.dma_start(out=wgs_sb[:, 0:HALF], in_=wgs[:, 0:HALF])
-        w1_raw.append(load_w1(1))
-        nc.sync.dma_start(out=w5_w[:].bitcast(I32), in_=w5_words.rearrange("a p c -> p a c").bitcast(I32))
+        raw["w1", 1] = load_rows("w1_raw1", w1[:, W1_PIECE:HALF], W1_RAW + 2 * TERM)
         nc.sync.dma_start(out=wgs_sb[:, HALF:S], in_=wgs[:, HALF:S])
-        w1_raw.extend(load_w1(i) for i in (2, 3))
         load_scale_rows(nc.sync, w5_s, w5_scales.rearrange("a q c -> q a c"))
-        nc.sync.dma_start(out=w2_rest[:], in_=w2_dram[:, W2_FIRST:H])
         nc.sync.dma_start(list4[:], offs4)
+        nc.sync.dma_start(out=hiatus_rows[0][:], in_=hiatus[0:P, :])
+        raw["w1", 2] = load_rows("w1_raw2", w1[:, HALF:H], W1_RAW + 4 * TERM)
+        nc.sync.dma_start(out=w2_rest[:], in_=w2_dram[:, W1_PIECE:H])
+        nc.sync.dma_start(out=w5_w[:].bitcast(I32), in_=w5_words.rearrange("a p c -> p a c").bitcast(I32))
         nc.sync.dma_start(list3[:], offs3)
-        raw = {}
-        for b in range(4):
-            nc.sync.dma_start(out=hiatus_rows[b][:], in_=hiatus[P * b : P * (b + 1), :])
-            if b == 0:
-                raw["g", 0] = load_rows(hiatus[0:512, :], placed("g_raw0", [P, 4, M], F32, LATE_RAW))
+        raw["g", 0] = load_rows("g_raw0", hiatus[0:512, :], G_RAW)
+        nc.sync.dma_start(out=hiatus_rows[1][:], in_=hiatus[P : 2 * P, :])
 
-        def round_rows(raw, grouped, dealt, negated=False):
-            width = raw.shape[2]
+        def round_rows(rows, grouped, dealt, negated=False):
+            width = rows.shape[2]
             if dealt:
                 dst = grouped[:].rearrange("p (t m j) -> p m j t", t=4, j=4)
-                src = raw[:].rearrange("p j (m t) -> p m j t", t=4)
+                src = rows.rearrange("p j (m t) -> p m j t", t=4)
             else:
                 dst = grouped[:].rearrange("p (c i j) -> p c j i", i=4, j=4)
-                src = raw[:].rearrange("p j (c i) -> p c j i", i=4)
+                src = rows.rearrange("p j (c i) -> p c j i", i=4)
             for c0 in range(0, width // 4, ROUND_GROUPS):
                 if negated:
                     nc.scalar.activation(out=dst[:, c0 : c0 + ROUND_GROUPS], in_=src[:, c0 : c0 + ROUND_GROUPS], func=ACT.Copy, scale=-1.0)
@@ -156,335 +150,252 @@ def tile_list_strata_contacts_kernel(
             nc.vector.quantize_mx(out=codes[:].bitcast(FP8X4), scales=scales[:], in_=grouped[:])
             return codes, scales
 
-        def quantize_w1(i):
-            grouped = placed(f"w1_grouped{i}", [P, 4 * W1_PIECE], BF16, W1_GROUPED + TERM * i if i < 3 else TAB_SCALES + TERM)
-            round_rows(w1_raw[i], grouped, False, True)
-            cols = slice(W1_PIECE * i, W1_PIECE * (i + 1))
+        def quantize_w1(i, c0, offset):
+            width = raw["w1", i].shape[2]
+            grouped = placed(f"w1_grouped{i}", [P, 4 * width], BF16, offset)
+            round_rows(raw["w1", i][:], grouped, c0 >= HALF, True)
+            cols = slice(c0, c0 + width)
             nc.vector.quantize_mx(out=minus_w1_c[:, cols].bitcast(FP8X4), scales=minus_w1_s[:, cols], in_=grouped[:])
 
         nc.vector.tensor_copy(out=v_s[0][:], in_=tab_s[:].indirect(list1[:, 0:32]))
         nc.vector.tensor_copy(out=v_s[1][:], in_=tab_s[:].indirect(list1[:, 32:64]))
-        quantize_w1(0)
+        quantize_w1(0, 0, H_RING + 4 * TERM)
         nc.vector.tensor_copy(out=v_w[0][:], in_=tab_w[:].bitcast(U32).indirect(list1[:, 0:32]))
         nc.vector.tensor_copy(out=v_w[1][:], in_=tab_w[:].bitcast(U32).indirect(list1[:, 32:64]))
 
         wgs_by_t = wgs.rearrange("(i t) j -> t i j", t=4)
-        wgs_dealt = [placed(f"wgs_dealt{t}", [P, S], F32, TAB_WORDS + 4096 * t) for t in range(4)]
-        for t in range(4):
+        wgs_dealt = [placed(f"wgs_dealt{t}", [P, S], F32, (G_RAW + 4 * TERM, G_RAW + 6 * TERM, W6_RAW + 4 * TERM, W6_RAW + 6 * TERM)[t]) for t in range(4)]
+
+        def load_wgs_dealt(t):
             for q in range(4):
                 nc.sync.dma_start(out=wgs_dealt[t][32 * q : 32 * (q + 1), :], in_=wgs_by_t[t])
 
-        def weights(name, r0, width):
-            cols = slice(r0, r0 + width)
+        nc.sync.dma_start(out=hiatus_rows[2][:], in_=hiatus[2 * P : 3 * P, :])
+        load_wgs_dealt(0)
+        raw["w6", 0] = load_rows("w6_raw0", w6[0:512, :], W6_RAW)
+        nc.sync.dma_start(out=hiatus_rows[3][:], in_=hiatus[3 * P : 4 * P, :])
+        load_wgs_dealt(1)
+        raw["g", 1] = load_rows("g_raw1", hiatus[512:1024, :], TAB_WORDS)
+        load_wgs_dealt(2)
+        raw["w6", 1] = load_rows("w6_raw1", w6[512:1024, :], TAB_WORDS + 4 * TERM)
+        load_wgs_dealt(3)
+
+        moved = {}
+
+        def deal(engine, name, source, dtype, offset):
+            planes, width = source.shape[1], source.shape[2]
+            walk = "p a t m" if dtype == U8 else "p a m t"
+            moved[name] = placed(name, [P, planes, width], dtype, offset)
+            engine(
+                out=moved[name][:].rearrange(f"p a (t m) -> {walk}", t=4),
+                in_=source.rearrange(f"p a (m t) -> {walk}", t=4),
+            )
+
+        def weights(name, slab):
+            cols = slice(P * slab, P * (slab + 1))
+            upper = slice(P * (slab - 4), P * (slab - 3))
             if name == "minus_w1":
                 return minus_w1_c[:, cols].bitcast(FP8X4), minus_w1_s[:, cols]
             if name == "w3":
-                return w3_w[:, 2 * r0 : 2 * (r0 + width)].bitcast(FP4X4), w3_s[:, cols]
-            words = w2_first[:, cols] if r0 < W2_FIRST else w2_rest[:, r0 - W2_FIRST : r0 - W2_FIRST + width]
-            return words.bitcast(FP8X4), w2_s[:, cols]
+                if slab >= 4:
+                    return moved["w3_dealt"][:, 0, upper].bitcast(FP4X4), moved["w23_s_dealt"][:, 1, upper]
+                return w3_w[:, 2 * P * slab : 2 * P * (slab + 1)].bitcast(FP4X4), w23_s[:, H + P * slab : H + P * (slab + 1)]
+            if slab >= 4:
+                return moved["w2_dealt"][:, 0, upper].bitcast(FP8X4), moved["w23_s_dealt"][:, 0, upper]
+            words = w2_first[:, cols] if slab < 2 else w2_rest[:, P * (slab - 2) : P * (slab - 1)]
+            return words.bitcast(FP8X4), w23_s[:, cols]
 
-        def product(tag, names, chunks, r0, width):
-            moving = {name: weights(name, r0, width) for name in names}
+        def by_rows(u, tag, name):
+            slab, hf = divmod(u, 2)
+            codes, scales = weights(name, slab)
             acc = bank(tag)
-            for x, chunk in enumerate(chunks):
-                hf, c = divmod(chunk, 4)
+            nc.tensor.matmul_mx(
+                out=acc[:], lhsT=codes, lhsT_scale=scales,
+                rhs=v_w[hf][:].bitcast(FP8X4), rhs_scale=v_s[hf][:], start=True, stop=True,
+            )
+            return acc
+
+        def by_entries(u, tag, names):
+            slab, hf = divmod(u, 2)
+            acc = bank(tag)
+            for x in range(4):
+                cols = slice(P * x, P * (x + 1))
                 for n, name in enumerate(names):
+                    codes, scales = weights(name, slab)
                     nc.tensor.matmul_mx(
-                        out=acc[:, width * x : width * (x + 1)],
-                        lhsT=v_w[hf][:, P * c : P * (c + 1)].bitcast(FP8X4),
-                        lhsT_scale=v_s[hf][:, P * c : P * (c + 1)],
-                        rhs=moving[name][0], rhs_scale=moving[name][1],
-                        start=(n == 0), stop=(n == len(names) - 1),
+                        out=acc[:, cols], lhsT=v_w[hf][:, cols].bitcast(FP8X4), lhsT_scale=v_s[hf][:, cols],
+                        rhs=codes, rhs_scale=scales, start=(n == 0), stop=(n == len(names) - 1),
                     )
             return acc
 
-        def turn_and_add(acc, blocks):
-            count = sum(len(column) for column in blocks)
-            done = 0
-            for x, column in enumerate(blocks):
-                for block in column:
+        def transposed_sum(tag, terms):
+            acc = bank(tag)
+            for x in range(4):
+                for n, tile in enumerate(terms):
                     nc.tensor.matmul(
-                        acc[:, P * x : P * (x + 1)], block, ident[:], is_transpose=True,
-                        start=(done == 0), stop=(done == count - 1),
+                        acc[:, P * x : P * (x + 1)], tile[:, P * x : P * (x + 1)], ident[:], is_transpose=True,
+                        start=(x == 0 and n == 0), stop=(x == 3 and n == len(terms) - 1),
                     )
-                    done = done + 1
+            return acc
 
-        def transposed_sum(acc, terms):
-            turn_and_add(acc, [[term[:, P * x : P * (x + 1)] for term in terms] for x in range(4)])
+        z_front = placed("z_front", [P, 2, M], F32, EVEN_SECOND + 5 * TERM)
+        z_dealt = placed("z_dealt", [P, 4, M], F32, Z_DEALT)
+        unit_terms, unit_products, h = {}, {}, {}
 
-        def term(name, offset):
-            return placed(name, [P, 512], F32, offset)
+        def last_terms(u):
+            if u % 2 == 1:
+                offset = ODD_TERMS + TERM * (u - 1)
+                return term(f"first_term{u}", offset)[:], term(f"second_term{u}", offset + TERM)[:]
+            i = u // 2 - 1
+            second = term(f"second_term{u}", EVEN_SECOND + TERM * i)[:] if i < 5 else z_front[:, i - 5, :]
+            return term(f"first_term{u}", EVEN_FIRST + TERM * i)[:], second
 
-        h_half, unit_terms = {}, {}
+        def by_relu(u):
+            return u in RELU_UNITS
 
-        def lower_product(u, tag, names):
-            b, hf = divmod(u, 2)
-            return product(tag, names, range(4 * hf, 4 * hf + 4), P * b, P)
+        def products(u):
+            if by_relu(u):
+                first, second = last_terms(u)
+                nc.scalar.activation(out=first, in_=by_entries(u, "p0", ("w2", "minus_w1"))[:], func=ACT.Relu)
+                nc.scalar.activation(out=second, in_=by_entries(u, "p1", ("w3", "minus_w1"))[:], func=ACT.Copy, scale=-1.0)
+                unit_terms[u] = (first, second)
+                return
+            slot = 2 if u == DEAL_UNIT else len(unit_products) % 2
+            tags = ("p2", "p3", "p4") if by_relu(u - 1) else ("p2", "p0", "p1")
+            if u == 8:
+                tags = ("sum",) + tags[1:]
+            unit_products[u] = {}
+            for n, name in enumerate(("minus_w1", "w2", "w3")):
+                tile = term(f"{name}_product{u}", PRODUCTS + TERM * (3 * slot + n))
+                nc.scalar.copy(out=tile[:], in_=by_rows(u, tags[n], name)[:])
+                unit_products[u][name] = tile[:]
+
+        def differences(u):
+            if by_relu(u):
+                return
+            d = unit_products[u]
+            first, second = last_terms(u)
+            nc.scalar.activation(out=first, in_=transposed_sum("e", (d["minus_w1"], d["w2"]))[:], func=ACT.Relu)
+            nc.scalar.activation(out=second, in_=transposed_sum("x", (d["minus_w1"], d["w3"]))[:], func=ACT.Copy, scale=-1.0)
+            unit_terms[u] = (first, second)
+
+        def read_h(u, acc):
+            slab, hf = divmod(u, 2)
+            if slab == 7:
+                out = z_dealt[:, hf, :]
+            elif slab == 0:
+                h[0, 1] = term("h0_back", H_RING + TERM)
+                out = h[0, 1][:]
+            else:
+                if hf == 0:
+                    h[slab] = placed(f"h{slab}", [P, S], F32, H_RING + 2 * TERM * (slab % 3))
+                out = h[slab][:, HALF * hf : HALF * (hf + 1)]
+            nc.scalar.copy(out=out, in_=acc[:])
 
         def first_unit():
-            d = {}
-            for name, tag in (("minus_w1", "first"), ("w2", "second"), ("w3", "d3")):
-                codes, scales = weights(name, 0, P)
-                d[name] = bank(tag)
-                nc.tensor.matmul_mx(
-                    out=d[name][:], lhsT=codes, lhsT_scale=scales,
-                    rhs=v_w[0][:].bitcast(FP8X4), rhs_scale=v_s[0][:], start=True, stop=True,
-                )
+            d = {name: by_rows(0, tag, name) for name, tag in (("minus_w1", "p0"), ("w2", "p1"), ("w3", "p2"))}
             d1_sb = term("first_d1", TAB_SCALES)
-            first_larger = term("first_larger", THIRD_PAGE)
-            h_half[0] = term("h_half0", H_HALVES)
+            first_larger = term("first_larger", TAB_SCALES + TERM)
+            h[0, 0] = term("h0_front", H_RING)
             for cols in FIRST_PARTS:
                 nc.scalar.activation(out=d1_sb[:, cols], in_=d["minus_w1"][:, cols], func=ACT.Copy, scale=-1.0)
                 nc.vector.tensor_tensor(out=first_larger[:, cols], in0=d["w2"][:, cols], in1=d1_sb[:, cols], op=ALU.max)
             for cols in FIRST_PARTS:
-                nc.vector.tensor_tensor(out=h_half[0][:, cols], in0=first_larger[:, cols], in1=d["w3"][:, cols], op=ALU.subtract)
+                nc.vector.tensor_tensor(out=h[0, 0][:, cols], in0=first_larger[:, cols], in1=d["w3"][:, cols], op=ALU.subtract)
 
-        def lower_terms(u):
-            first = term(f"first_term{u}", FIRST_TERMS + TERM * (u - 1))
-            second = term(f"second_term{u}", TAB_SCALES + TERM if u == 1 else SECOND_TERMS + TERM * (u % 2))
-            if u in VECTOR_MAX_UNITS:
-                d1_sb = term(f"lower_d1_{u}", MINUS_D2 + TERM * (u % 2))
-                nc.scalar.activation(out=d1_sb[:], in_=lower_product(u, "d3", ("minus_w1",))[:], func=ACT.Copy, scale=-1.0)
-                nc.vector.tensor_tensor(out=first[:], in0=lower_product(u, "first", ("w2",))[:], in1=d1_sb[:], op=ALU.max)
-                names = ("w3",)
-            else:
-                nc.scalar.activation(out=first[:], in_=lower_product(u, "first", ("w2", "minus_w1"))[:], func=ACT.Relu)
-                names = ("w3", "minus_w1")
-            nc.scalar.activation(out=second[:], in_=lower_product(u, "second", names)[:], func=ACT.Copy, scale=-1.0)
-            unit_terms[u] = (first, second)
+        def put_in_page(slab, entries, values, factors):
+            nc.vector.tensor_tensor(out=pages[slab % 2][:].indirect(entries), in0=values, in1=factors, op=ALU.mult)
 
-        def lower_sum(u):
-            acc = bank("sum")
-            transposed_sum(acc, unit_terms[u])
-            h_half[u] = term(f"h_half{u}", W1_RAW + 3 * 4096 if u == 2 else H_HALVES + TERM * u)
-            nc.scalar.copy(out=h_half[u][:], in_=acc[:])
-
-        def put_in_page(slab, j0, width, values, weights):
-            nc.vector.tensor_tensor(
-                out=pages[slab % 3][:].indirect(list2[:, j0 // 16 : (j0 + width) // 16]),
-                in0=values, in1=weights[:, j0 : j0 + width], op=ALU.mult,
-            )
-
-        def lower_put(u):
-            put_in_page(u // 2, HALF * (u % 2), HALF, h_half[u][:], wgs_sb)
+        def put_slab(slab):
+            values = h[slab][:] if slab < 7 else z_dealt[:, 0:2, :].rearrange("p a m -> p (a m)")
+            put_in_page(slab, list2[:], values, (wgs_sb if slab < 4 else wgs_dealt[slab - 4])[:])
 
         def fetch_minus(slab, columns, m0, width, other, out):
             nc.vector.tensor_tensor(
-                out=out, in0=pages[slab % 3][:].indirect(columns[:, m0 // 16 : (m0 + width) // 16]),
+                out=out, in0=pages[slab % 2][:].indirect(columns[:, m0 // 16 : (m0 + width) // 16]),
                 in1=other, op=ALU.subtract,
             )
 
-        def dealt(acc):
-            return acc[:].rearrange("j (p t) -> j t p", t=4)
+        below = {}
 
-        def by_t(tile):
-            return tile[:].rearrange("j (t p) -> j t p", t=4)
+        def fetch_below(slab):
+            below[slab] = term(f"below{slab}", EVEN_FIRST + TERM * slab)
+            given = hiatus_rows[slab][:] if slab < 4 else raw["g", 1][:, slab - 4, :]
+            fetch_minus(slab, list4, 0, M, given, below[slab][:])
 
-        def dealt_term(c, name, offset, tag, names, func, scale):
-            tile = term(f"{name}{c}", offset)
-            nc.scalar.activation(out=by_t(tile), in_=dealt(product(tag, names, (c,), 512, 512)), func=func, scale=scale)
-            return tile
-
-        chunk_terms, minus_d2, excess = {}, {}, {}
-        h_front = [placed(f"h_front{k}", [P, 4, 2 * P], F32, H_FRONT + 2 * TERM * k) for k in range(2)]
-        h_front.append(placed("h_front2", [P, 3, 2 * P], F32, H_HALVES))
-
-        def chunk_slot(c, n):
-            return CHUNK_TERMS + TERM * (3 * (c % 4) + n)
-
-        def chunk_products(c):
-            if c in RELU_CHUNKS:
-                chunk_terms[c] = [
-                    dealt_term(c, "chunk_first", chunk_slot(c, 0), "d1", ("w2", "minus_w1"), ACT.Relu, 1.0),
-                    dealt_term(c, "chunk_second", chunk_slot(c, 1), "d2", ("w3", "minus_w1"), ACT.Copy, -1.0),
-                ]
+        def fetch_z(slab):
+            if slab >= 4:
+                out = z_front[:, slab - 4, :] if slab < 6 else z_dealt[:, 2, :]
+                fetch_minus(slab, list3, 0, M, below[slab][:], out)
                 return
-            chunk_terms[c] = [dealt_term(c, "chunk_d1_", chunk_slot(c, 0), "d1", ("minus_w1",), ACT.Copy, -1.0)]
-            minus_d2[c] = dealt_term(c, "minus_d2_", MINUS_D2 + TERM * (c % 2), "d2", ("w2",), ACT.Copy, -1.0)
-
-        def chunk_third(c):
-            if c not in RELU_CHUNKS:
-                chunk_terms[c].append(dealt_term(c, "minus_d3_", chunk_slot(c, 1), "d3", ("w3",), ACT.Copy, -1.0))
-
-        def chunk_excess(c):
-            if c not in RELU_CHUNKS:
-                acc = bank("first" if c in (5, 7) else "excess")
-                transposed_sum(acc, (chunk_terms[c][0], minus_d2[c]))
-                excess[c] = term(f"excess{c}", EXCESS + TERM * (c % 2))
-                nc.scalar.activation(out=excess[c][:], in_=acc[:], func=ACT.Relu, scale=-1.0)
-
-        def chunk_back(c):
-            if c not in RELU_CHUNKS:
-                acc = bank("second" if c in (5, 7) else "back")
-                transposed_sum(acc, (excess[c],))
-                back = term(f"back{c}", chunk_slot(c, 2))
-                nc.scalar.copy(out=back[:], in_=acc[:])
-                chunk_terms[c].append(back)
-
-        def chunk_sum(c, slabs):
-            acc = bank("sum")
-            turn_and_add(acc, [[tile[:, P * t : P * (t + 1)] for tile in chunk_terms[c]] for t in range(slabs)])
-            nc.scalar.copy(
-                out=h_front[c // 2][:, 0:slabs, P * (c % 2) : P * (c % 2 + 1)],
-                in_=acc[:, 0 : P * slabs].rearrange("p (t j) -> p t j", t=slabs),
-            )
-
-        def slab_sum(t, tag):
-            acc = bank(tag)
-            chunks = range(6, 8) if t < 3 else range(4, 8)
-            turn_and_add(acc, [[tile[:, P * t : P * (t + 1)] for tile in chunk_terms[c]] for c in chunks])
-            width = P * len(chunks)
-            h_half[8 + t] = placed(f"h_back{t}", [P, width], F32, H_HALVES + TERM * (4 + t) if t < 3 else Z_DEALT + 4096)
-            nc.scalar.copy(out=h_half[8 + t][:], in_=acc[:, 0:width])
-
-        def front_put(t, k):
-            put_in_page(4 + t, 2 * P * k, 2 * P, h_front[k][:, t, :], wgs_dealt[t])
-
-        quant, rounded = {}, {}
-
-        def round_operand(name, a, offset):
-            grouped = placed(f"{name}_grouped{a}", [P, 4 * 512], BF16, offset)
-            rounded[name, a] = round_rows(raw[name, a], grouped, name in ("w4", "w6"))
-
-        def quantize_operand(name, a):
-            quant[name, a] = quantize(rounded[name, a], f"{name}{a}")
-
-        below, z_lower = {}, {}
-
-        def lower_below(b):
-            below[b] = term(f"below{b}", FIRST_TERMS + TERM * (2 * b + 2) if b < 3 else TAB_SCALES)
-            fetch_minus(b, list4, 0, M, hiatus_rows[b][:], below[b][:])
-
-        def lower_z(b):
-            offset = (FIRST_TERMS + 3 * TERM, FIRST_TERMS + 5 * TERM, FIRST_TERMS + TERM, SECOND_TERMS)[b]
-            z_lower[b] = term(f"z_lower{b}", offset)
-            fetch_minus(b, list3, 0, M, below[b][:], z_lower[b][:])
+            z_rows = term(f"z_rows{slab}", EVEN_SECOND + TERM * (slab + 1))
+            fetch_minus(slab, list3, 0, M, below[slab][:], z_rows[:])
             for t in range(4):
-                nc.sync.dma_start(out=raw["z", 0][32 * b : 32 * (b + 1), t, :], in_=z_lower[b][t:P:4, :])
+                nc.sync.dma_start(out=z_dealt[32 * slab : 32 * (slab + 1), t, :], in_=z_rows[t:P:4, :])
 
-        def lower_step(u):
-            lower_sum(u)
-            if u >= 3 and u % 2 == 1:
-                lower_below((u - 3) // 2)
-            if u >= 4 and u % 2 == 0:
-                lower_z((u - 4) // 2)
-            lower_put(u)
+        quant = {}
+
+        def quantize_operand(name, a, rows, offset):
+            grouped = placed(f"{name}_grouped{a}", [P, 4 * 512], BF16, offset)
+            quant[name, a] = quantize(round_rows(rows, grouped, name in ("w4", "w6")), f"{name}{a}")
+
+        def behind_unit(u):
+            own = PRODUCTS + 6 * TERM
+            if u == 2:
+                deal(nc.vector.tensor_copy, "w5_s_dealt", w5_s[:], U8, EVEN_SECOND)
+            if u == DEAL_UNIT:
+                quantize_w1(2, HALF, ODD_TERMS + 2 * TERM)
+                for a in range(2):
+                    raw["w4", a] = load_rows(f"w4_raw{a}", w4[512 * a : 512 * (a + 1), :], W1_RAW + 4 * TERM * a)
+                deal(nc.scalar.copy, "w2_dealt", w2_rest[:, W1_PIECE:].bitcast(U32).unsqueeze(1), U32, own)
+                deal(nc.scalar.copy, "w3_dealt", w3_w[:, H:].bitcast(U16).unsqueeze(1), U16, own + TERM)
+            if u in LATE_OPERANDS:
+                name, a, behind = LATE_OPERANDS[u]
+                quantize_operand(name, a, raw[name, a][:], ODD_TERMS + TERM * (behind - 1))
+            if u == 13:
+                deal(nc.scalar.copy, "w5_dealt", w5_w[:].bitcast(U16), U16, own + 2 * TERM)
 
         first_unit()
-        pages.append(placed("page2", [P, T2], F32, THIRD_PAGE))
-        nc.gpsimd.memset(pages[2][:], 0.0)
-        lower_terms(1)
-        lower_put(0)
-        lower_terms(2)
-        lower_sum(1)
-        w5_wd = placed("w5_dealt_words", [P, 2, 2 * N], U8, FIRST_TERMS)
-        nc.vector.tensor_copy(
-            out=w5_wd[:].bitcast(U16).rearrange("p a (t m) -> p a t m", t=4),
-            in_=w5_w[:].bitcast(U16).rearrange("p a (m t) -> p a t m", t=4),
-        )
-        lower_put(1)
-        lower_terms(3)
-        for i in (1, 2, 3):
-            quantize_w1(i)
-        w5_sd = placed("w5_dealt_scales", [P, 2, N], U8, TAB_SCALES + TERM)
-        nc.vector.tensor_copy(
-            out=w5_sd[:].rearrange("p a (t m) -> p a t m", t=4),
-            in_=w5_s[:].rearrange("p a (m t) -> p a t m", t=4),
-        )
-        lower_step(2)
-        raw["z", 0] = placed("z_dealt", [P, 4, M], F32, Z_DEALT)
-        for name, source, a, offset in (
-            ("w6", w6, 0, W1_RAW), ("w4", w4, 0, W1_GROUPED), ("g", hiatus, 1, None),
-            ("w6", w6, 1, W1_RAW + 8192), ("w4", w4, 1, LATE_RAW + 8192),
-        ):
-            shape = [P, 4, 512]
-            tile = held("g_raw1", shape, F32) if offset is None else placed(f"{name}_raw{a}", shape, F32, offset)
-            raw[name, a] = load_rows(source[512 * a : 512 * (a + 1), :], tile)
-        lower_step(3)
-        for c in range(4):
-            lower_terms(4 + c)
-            if c >= 1:
-                chunk_back(c - 1)
-            chunk_products(c)
-            lower_step(4 + c)
-            if c >= 1:
-                chunk_sum(c - 1, 4)
-            if c == 2:
-                front_put(0, 0)
-            chunk_third(c)
-            chunk_excess(c)
-            if c == 1:
-                round_operand("g", 0, chunk_slot(3, 0))
-                quantize_operand("g", 0)
-        lower_z(2)
-        lower_below(3)
-        front_put(1, 0)
-        lower_z(3)
-        front_put(2, 0)
-        chunk_back(3)
-        chunk_sum(3, 4)
-        for t in range(3):
-            front_put(t, 1)
-        for c in range(4, 8):
-            for stage in (chunk_products, chunk_third, chunk_excess, chunk_back):
-                stage(c)
-            if c < 6:
-                chunk_sum(c, 3)
-            if c == 5:
-                for t in range(3):
-                    front_put(t, 2)
-
-        def back_put(t):
-            width = h_half[8 + t].shape[1]
-            put_in_page(4 + t, S - width, width, h_half[8 + t][:], wgs_dealt[t])
-
-        upper_below = {}
-
-        def upper_fetch_below(t, offset):
-            upper_below[t] = term(f"upper_below{t}", offset)
-            fetch_minus(4 + t, list4, 0, M, raw["g", 1][:, t, :], upper_below[t][:])
-
-        z_back = {}
-
-        def third_z(hf):
-            z_back[hf] = placed(f"z_back{hf}", [P, 2, 2 * P], F32, LATE_RAW + TERM * hf)
-            cols = slice(2 * P * hf, 2 * P * (hf + 1))
-            fetch_minus(6, list3, 2 * P * hf, 2 * P, upper_below[2][:, cols], z_back[hf][:, 0, :])
-
-        slab_sum(0, "sum")
-        back_put(0)
-        slab_sum(1, "excess")
-        back_put(1)
-        round_operand("w6", 0, STAGE1 + 4096)
-        upper_fetch_below(0, W1_RAW + 3 * TERM)
-        quantize_operand("w6", 0)
-        z_front = placed("z_front", [P, 2, M], F32, W1_RAW)
-        fetch_minus(4, list3, 0, M, upper_below[0][:], z_front[:, 0, :])
-        upper_fetch_below(1, W1_RAW + 2 * TERM)
-        front_put(3, 0)
-        fetch_minus(5, list3, 0, M, upper_below[1][:], z_front[:, 1, :])
-        front_put(3, 1)
-        slab_sum(2, "back")
-        back_put(2)
-        for n, name in enumerate(("g", "w6", "w4")):
-            round_operand(name, 1, STAGE1 + 4096 * (2 + n))
-            quantize_operand(name, 1)
-        round_operand("z", 0, STAGE1 + 5 * 4096)
-        upper_fetch_below(2, Z_DEALT + 3 * TERM)
-        quantize_operand("z", 0)
-        third_z(0)
-        third_z(1)
-        slab_sum(3, "d3")
-        back_put(3)
-        round_operand("w4", 0, Z_DEALT)
-        quantize_operand("w4", 0)
+        products(1)
+        put_in_page(0, list2[:, 0:32], h[0, 0][:], wgs_sb[:, 0:HALF])
+        quantize_w1(1, W1_PIECE, TAB_SCALES)
+        products(2)
+        read_h(1, transposed_sum("sum", unit_terms[1]))
+        upper_scales = w23_s[:].rearrange("p (a hf c) -> p a hf c", a=2, hf=2)[:, :, 1, :]
+        deal(nc.vector.tensor_copy, "w23_s_dealt", upper_scales, U8, ODD_TERMS)
+        put_in_page(0, list2[:, 32:64], h[0, 1][:], wgs_sb[:, HALF:S])
+        differences(2)
+        products(3)
+        for u in range(2, UNITS - 2):
+            read_h(u, transposed_sum("sum", unit_terms[u]))
+            products(u + 2)
+            differences(u + 1)
+            behind_unit(u)
+            if u % 2 == 1:
+                put_slab(u // 2)
+            else:
+                if u >= 4:
+                    fetch_z(u // 2 - 2)
+                fetch_below(u // 2 - 1)
+        last_sums = [transposed_sum("sum", unit_terms[14])]
+        differences(15)
+        last_sums.append(transposed_sum("e", unit_terms[15]))
+        quantize_operand("w4", 1, raw["w4", 1][:], ODD_TERMS + 12 * TERM)
+        fetch_z(5)
+        fetch_below(6)
+        quantize_operand("z", 0, z_dealt[:], ODD_TERMS + 14 * TERM)
+        fetch_z(6)
+        read_h(14, last_sums[0])
+        read_h(15, last_sums[1])
+        put_slab(7)
+        quantize_operand("w4", 0, raw["w4", 0][:], EVEN_FIRST + 5 * TERM)
 
         def round_pair(grouped, u, planes):
             nc.scalar.copy(
                 out=grouped[:].rearrange("p (m u e) -> p u m e", u=2, e=2)[:, u], in_=planes.rearrange("p e m -> p m e")
             )
 
-        z_grouped = [placed(f"z_grouped{q}", [P, 4 * P], BF16, W1_GROUPED + 4096 + 1024 * q) for q in range(4)]
+        z_grouped = [placed(f"z_grouped{q}", [P, 4 * P], BF16, W1_RAW + 4096 + 1024 * q) for q in range(4)]
         for q in range(4):
             round_pair(z_grouped[q], 0, z_front[:, :, P * q : P * (q + 1)])
 
@@ -492,8 +403,8 @@ def tile_list_strata_contacts_kernel(
             for t in range(4):
                 cols = slice(P * t, P * (t + 1))
                 if name == "w5":
-                    lhsT = w5_wd[:, a, 2 * P * t : 2 * P * (t + 1)].bitcast(FP4X4)
-                    lhsT_scale = w5_sd[:, a, cols]
+                    lhsT = moved["w5_dealt"][:, a, cols].bitcast(FP4X4)
+                    lhsT_scale = moved["w5_s_dealt"][:, a, cols]
                 else:
                     lhsT = quant[name, a][0][:, cols].bitcast(FP8X4)
                     lhsT_scale = quant[name, a][1][:, cols]
@@ -506,32 +417,26 @@ def tile_list_strata_contacts_kernel(
                 )
 
         sums, gates = {}, {}
-        for q, tag in enumerate(("first", "second", "d1", "d2")):
+        for q, tag in enumerate(("p0", "p1", "p2", "p3")):
             sums[q] = bank(tag)
             mx_passes(sums[q], "w5", 0, q, True, False)
         for a in range(2):
             for q in range(4):
                 mx_passes(sums[q], "w6", a, q, False, False)
-        for q, tag in enumerate(("sum", "excess", "back", "d3")):
+        for q, tag in enumerate(("p4", "x", "sum", "e")):
             gates[q] = bank(tag)
             mx_passes(gates[q], "w4", 0, q, True, False)
 
         last_below = {}
-
-        def last_fetch_below(hf):
-            last_below[hf] = placed(f"last_below{hf}", [P, 2 * P], F32, W1_GROUPED + 1024 * hf)
+        for hf in range(2):
+            last_below[hf] = placed(f"last_below{hf}", [P, 2 * P], F32, W1_RAW + 1024 * hf)
             fetch_minus(7, list4, 2 * P * hf, 2 * P, raw["g", 1][:, 3, 2 * P * hf : 2 * P * (hf + 1)], last_below[hf][:])
-
-        def last_z(q):
-            hf, cols = q // 2, slice(P * (q % 2), P * (q % 2 + 1))
-            fetch_minus(7, list3, P * q, P, last_below[hf][:, cols], z_back[hf][:, 1, cols])
-            round_pair(z_grouped[q], 1, z_back[hf][:, :, cols])
-            quant["z", 1, q] = quantize(z_grouped[q], f"z1{q}", CHUNK_TERMS + 8 * TERM + 768 if q == 3 else None)
-
-        last_fetch_below(0)
-        last_fetch_below(1)
+        y_grouped_at = PRODUCTS + 4 * TERM
         for q in range(4):
-            last_z(q)
+            cols = slice(P * q, P * (q + 1))
+            fetch_minus(7, list3, P * q, P, last_below[q // 2][:, P * (q % 2) : P * (q % 2 + 1)], z_dealt[:, 3, cols])
+            round_pair(z_grouped[q], 1, z_dealt[:, 2:4, cols])
+            quant["z", 1, q] = quantize(z_grouped[q], f"z1{q}", y_grouped_at + 768 if q == 3 else None)
 
         out_rows = out_0.rearrange("(p t) m -> p t m", t=4)
         out_words = out_1[0].rearrange("p m t -> p (m t)").bitcast(I32)
@@ -544,14 +449,14 @@ def tile_list_strata_contacts_kernel(
             if q < 3:
                 mx_passes(gates[q + 1], "w4", 1, q + 1, False, True)
             mx_passes(sums[q], "w5", 1, q, False, True)
-            gate = placed(f"gate{q}", [P, 512], F32, CHUNK_TERMS + TERM * q)
+            gate = placed(f"gate{q}", [P, 512], F32, PRODUCTS + TERM * q)
             nc.scalar.activation(out=gate[:], in_=gates[q][:], func=ACT.Tanh)
-            ys.append(placed(f"y{q}", [P, 4, P], F32, CHUNK_TERMS + TERM * (4 + q)))
+            ys.append(placed(f"y{q}", [P, 4, P], F32, H_RING + TERM * q))
             nc.vector.tensor_tensor(out=ys[q][:].rearrange("p t m -> p (t m)"), in0=sums[q][:], in1=gate[:], op=ALU.mult)
             nc.sync.dma_start(out=out_rows[:, :, cols], in_=ys[q][:])
         for q, y in enumerate(ys):
             cols = slice(P * q, P * (q + 1))
-            y_grouped = placed(f"y_grouped{q}", [P, 4 * P], BF16, CHUNK_TERMS + 8 * TERM + 1024 * q)
+            y_grouped = placed(f"y_grouped{q}", [P, 4 * P], BF16, y_grouped_at + 1024 * q)
             (nc.scalar.copy if q < 2 else nc.vector.tensor_copy)(
                 out=y_grouped[:].rearrange("p (c i t) -> p c t i", i=4, t=4),
                 in_=y[:].rearrange("p t (c i) -> p c t i", i=4),

@@ -24,9 +24,10 @@ FIRST_PARTS = (slice(0, 256), slice(256, 512))
 GPSIMD_CLEARS = 576
 ROUND_GROUPS = 32
 UNITS = 16
-RELU_UNITS = (1, 2, 4, 6, 9, 11, 13)
-DEAL_UNIT = 5
-LATE_OPERANDS = {9: ("g", 0, 5), 11: ("w6", 0, 7), 12: ("g", 1, 9), 13: ("w6", 1, 11)}
+RELU_UNITS = (1, 2, 3, 5, 7, 9, 11)
+DEAL_UNIT = 4
+FIRST_BANKS = (0, 1, 2, 0, 1, 3, 2, 4, 5, 1, 6, 7, 0)
+LATE_OPERANDS = {3: ("g", 0), 4: ("w6", 0), 5: ("g", 1), 6: ("w6", 1)}
 
 TERM = 2048
 TAB_WORDS, TAB_SCALES = 0, 16384
@@ -60,8 +61,11 @@ def tile_list_strata_contacts_kernel(
         def term(name, offset):
             return placed(name, [P, 512], F32, offset)
 
-        def bank(tag):
-            return psum.tile([P, 512], F32, name=tag)
+        taken = []
+
+        def bank():
+            taken.append(FIRST_BANKS[len(taken)] if len(taken) < len(FIRST_BANKS) else taken[-8])
+            return psum.tile([P, 512], F32, name=f"bank{taken[-1]}")
 
         def load_scale_rows(queue, plane, rows):
             for q in range(4):
@@ -205,19 +209,19 @@ def tile_list_strata_contacts_kernel(
             words = w2_first[:, cols] if slab < 2 else w2_rest[:, P * (slab - 2) : P * (slab - 1)]
             return words.bitcast(FP8X4), w23_s[:, cols]
 
-        def by_rows(u, tag, name):
+        def by_rows(u, name):
             slab, hf = divmod(u, 2)
             codes, scales = weights(name, slab)
-            acc = bank(tag)
+            acc = bank()
             nc.tensor.matmul_mx(
                 out=acc[:], lhsT=codes, lhsT_scale=scales,
                 rhs=v_w[hf][:].bitcast(FP8X4), rhs_scale=v_s[hf][:], start=True, stop=True,
             )
             return acc
 
-        def by_entries(u, tag, names):
+        def by_entries(u, names):
             slab, hf = divmod(u, 2)
-            acc = bank(tag)
+            acc = bank()
             for x in range(4):
                 cols = slice(P * x, P * (x + 1))
                 for n, name in enumerate(names):
@@ -228,8 +232,8 @@ def tile_list_strata_contacts_kernel(
                     )
             return acc
 
-        def transposed_sum(tag, terms):
-            acc = bank(tag)
+        def transposed_sum(terms):
+            acc = bank()
             for x in range(4):
                 for n, tile in enumerate(terms):
                     nc.tensor.matmul(
@@ -256,18 +260,15 @@ def tile_list_strata_contacts_kernel(
         def products(u):
             if by_relu(u):
                 first, second = last_terms(u)
-                nc.scalar.activation(out=first, in_=by_entries(u, "p0", ("w2", "minus_w1"))[:], func=ACT.Relu)
-                nc.scalar.activation(out=second, in_=by_entries(u, "p1", ("w3", "minus_w1"))[:], func=ACT.Copy, scale=-1.0)
+                nc.scalar.activation(out=first, in_=by_entries(u, ("w2", "minus_w1"))[:], func=ACT.Relu)
+                nc.scalar.activation(out=second, in_=by_entries(u, ("w3", "minus_w1"))[:], func=ACT.Copy, scale=-1.0)
                 unit_terms[u] = (first, second)
                 return
             slot = 2 if u == DEAL_UNIT else len(unit_products) % 2
-            tags = ("p2", "p3", "p4") if by_relu(u - 1) else ("p2", "p0", "p1")
-            if u == 8:
-                tags = ("sum",) + tags[1:]
             unit_products[u] = {}
             for n, name in enumerate(("minus_w1", "w2", "w3")):
                 tile = term(f"{name}_product{u}", PRODUCTS + TERM * (3 * slot + n))
-                nc.scalar.copy(out=tile[:], in_=by_rows(u, tags[n], name)[:])
+                nc.scalar.copy(out=tile[:], in_=by_rows(u, name)[:])
                 unit_products[u][name] = tile[:]
 
         def differences(u):
@@ -275,8 +276,8 @@ def tile_list_strata_contacts_kernel(
                 return
             d = unit_products[u]
             first, second = last_terms(u)
-            nc.scalar.activation(out=first, in_=transposed_sum("e", (d["minus_w1"], d["w2"]))[:], func=ACT.Relu)
-            nc.scalar.activation(out=second, in_=transposed_sum("x", (d["minus_w1"], d["w3"]))[:], func=ACT.Copy, scale=-1.0)
+            nc.scalar.activation(out=first, in_=transposed_sum((d["minus_w1"], d["w2"]))[:], func=ACT.Relu)
+            nc.scalar.activation(out=second, in_=transposed_sum((d["minus_w1"], d["w3"]))[:], func=ACT.Copy, scale=-1.0)
             unit_terms[u] = (first, second)
 
         def read_h(u, acc):
@@ -293,7 +294,7 @@ def tile_list_strata_contacts_kernel(
             nc.scalar.copy(out=out, in_=acc[:])
 
         def first_unit():
-            d = {name: by_rows(0, tag, name) for name, tag in (("minus_w1", "p0"), ("w2", "p1"), ("w3", "p2"))}
+            d = {name: by_rows(0, name) for name in ("minus_w1", "w2", "w3")}
             d1_sb = term("first_d1", TAB_SCALES)
             first_larger = term("first_larger", TAB_SCALES + TERM)
             h[0, 0] = term("h0_front", H_RING)
@@ -339,48 +340,53 @@ def tile_list_strata_contacts_kernel(
             grouped = placed(f"{name}_grouped{a}", [P, 4 * 512], BF16, offset)
             quant[name, a] = quantize(round_rows(rows, grouped, name in ("w4", "w6")), f"{name}{a}")
 
-        def behind_unit(u):
-            own = PRODUCTS + 6 * TERM
-            if u == 2:
-                deal(nc.vector.tensor_copy, "w5_s_dealt", w5_s[:], U8, EVEN_SECOND)
-            if u == DEAL_UNIT:
-                quantize_w1(2, HALF, ODD_TERMS + 2 * TERM)
-                for a in range(2):
-                    raw["w4", a] = load_rows(f"w4_raw{a}", w4[512 * a : 512 * (a + 1), :], W1_RAW + 4 * TERM * a)
-                deal(nc.scalar.copy, "w2_dealt", w2_rest[:, W1_PIECE:].bitcast(U32).unsqueeze(1), U32, own)
-                deal(nc.scalar.copy, "w3_dealt", w3_w[:, H:].bitcast(U16).unsqueeze(1), U16, own + TERM)
-            if u in LATE_OPERANDS:
-                name, a, behind = LATE_OPERANDS[u]
-                quantize_operand(name, a, raw[name, a][:], ODD_TERMS + TERM * (behind - 1))
-            if u == 13:
-                deal(nc.scalar.copy, "w5_dealt", w5_w[:].bitcast(U16), U16, own + 2 * TERM)
+        def first_stage(slab, relu):
+            for u in (2 * slab, 2 * slab + 1):
+                if u < UNITS and by_relu(u) == relu:
+                    products(u)
+
+        def second_stage(slab):
+            first_stage(slab, True)
+            for u in (2 * slab, 2 * slab + 1):
+                differences(u)
 
         first_unit()
         products(1)
         put_in_page(0, list2[:, 0:32], h[0, 0][:], wgs_sb[:, 0:HALF])
         quantize_w1(1, W1_PIECE, TAB_SCALES)
         products(2)
-        read_h(1, transposed_sum("sum", unit_terms[1]))
+        read_h(1, transposed_sum(unit_terms[1]))
         upper_scales = w23_s[:].rearrange("p (a hf c) -> p a hf c", a=2, hf=2)[:, :, 1, :]
         deal(nc.vector.tensor_copy, "w23_s_dealt", upper_scales, U8, ODD_TERMS)
         put_in_page(0, list2[:, 32:64], h[0, 1][:], wgs_sb[:, HALF:S])
-        differences(2)
         products(3)
-        for u in range(2, UNITS - 2):
-            read_h(u, transposed_sum("sum", unit_terms[u]))
-            products(u + 2)
-            differences(u + 1)
-            behind_unit(u)
-            if u % 2 == 1:
-                put_slab(u // 2)
+        first_stage(2, False)
+        for slab in range(1, 7):
+            if slab > 1:
+                second_stage(slab + 1)
+            read_h(2 * slab, transposed_sum(unit_terms[2 * slab]))
+            if slab == 1:
+                deal(nc.vector.tensor_copy, "w5_s_dealt", w5_s[:], U8, EVEN_SECOND)
             else:
-                if u >= 4:
-                    fetch_z(u // 2 - 2)
-                fetch_below(u // 2 - 1)
-        last_sums = [transposed_sum("sum", unit_terms[14])]
-        differences(15)
-        last_sums.append(transposed_sum("e", unit_terms[15]))
-        quantize_operand("w4", 1, raw["w4", 1][:], ODD_TERMS + 12 * TERM)
+                fetch_z(slab - 2)
+            fetch_below(slab - 1)
+            read_h(2 * slab + 1, transposed_sum(unit_terms[2 * slab + 1]))
+            put_slab(slab)
+            if slab == 1:
+                second_stage(2)
+                quantize_w1(2, HALF, ODD_TERMS + 2 * TERM)
+                for a in range(2):
+                    raw["w4", a] = load_rows(f"w4_raw{a}", w4[512 * a : 512 * (a + 1), :], W1_RAW + 4 * TERM * a)
+            if slab == 2:
+                own = PRODUCTS + 6 * TERM
+                deal(nc.scalar.copy, "w2_dealt", w2_rest[:, W1_PIECE:].bitcast(U32).unsqueeze(1), U32, own)
+                deal(nc.scalar.copy, "w3_dealt", w3_w[:, H:].bitcast(U16).unsqueeze(1), U16, own + TERM)
+            first_stage(slab + 2, False)
+            if slab in LATE_OPERANDS:
+                name, a = LATE_OPERANDS[slab]
+                quantize_operand(name, a, raw[name, a][:], ODD_TERMS + TERM * (2 * slab - 2))
+        deal(nc.scalar.copy, "w5_dealt", w5_w[:].bitcast(U16), U16, PRODUCTS + 8 * TERM)
+        last_sums = [transposed_sum(unit_terms[u]) for u in (14, 15)]
         fetch_z(5)
         fetch_below(6)
         quantize_operand("z", 0, z_dealt[:], ODD_TERMS + 14 * TERM)
@@ -388,6 +394,7 @@ def tile_list_strata_contacts_kernel(
         read_h(14, last_sums[0])
         read_h(15, last_sums[1])
         put_slab(7)
+        quantize_operand("w4", 1, raw["w4", 1][:], ODD_TERMS + 12 * TERM)
         quantize_operand("w4", 0, raw["w4", 0][:], EVEN_FIRST + 5 * TERM)
 
         def round_pair(grouped, u, planes):
@@ -417,14 +424,14 @@ def tile_list_strata_contacts_kernel(
                 )
 
         sums, gates = {}, {}
-        for q, tag in enumerate(("p0", "p1", "p2", "p3")):
-            sums[q] = bank(tag)
+        for q in range(4):
+            sums[q] = bank()
             mx_passes(sums[q], "w5", 0, q, True, False)
         for a in range(2):
             for q in range(4):
                 mx_passes(sums[q], "w6", a, q, False, False)
-        for q, tag in enumerate(("p4", "x", "sum", "e")):
-            gates[q] = bank(tag)
+        for q in range(4):
+            gates[q] = bank()
             mx_passes(gates[q], "w4", 0, q, True, False)
 
         last_below = {}

@@ -157,8 +157,18 @@ def tile_list_strata_contacts_kernel(
         def quantize_w1(i, c0, offset):
             width = raw["w1", i].shape[2]
             grouped = placed(f"w1_grouped{i}", [P, 4 * width], BF16, offset)
-            round_rows(raw["w1", i][:], grouped, c0 >= HALF, True)
+            round_rows(raw["w1", i][:], grouped, False, True)
             cols = slice(c0, c0 + width)
+            nc.vector.quantize_mx(out=minus_w1_c[:, cols].bitcast(FP8X4), scales=minus_w1_s[:, cols], in_=grouped[:])
+
+        def quantize_upper_w1(pair):
+            grouped = placed(f"w1_upper{pair}", [P, 4 * W1_PIECE], BF16, ODD_TERMS + TERM * (2 + pair))
+            dst = grouped[:].rearrange("p (t m j) -> p m j t", t=2, j=4)
+            src = raw["w1", 2][:].rearrange("p j (m t) -> p m j t", t=4)[:, :, :, 2 * pair : 2 * pair + 2]
+            for c0 in range(0, P, 2 * ROUND_GROUPS):
+                part = slice(c0, c0 + 2 * ROUND_GROUPS)
+                nc.scalar.activation(out=dst[:, part], in_=src[:, part], func=ACT.Copy, scale=-1.0)
+            cols = slice(HALF + W1_PIECE * pair, HALF + W1_PIECE * (pair + 1))
             nc.vector.quantize_mx(out=minus_w1_c[:, cols].bitcast(FP8X4), scales=minus_w1_s[:, cols], in_=grouped[:])
 
         nc.vector.tensor_copy(out=v_s[0][:], in_=tab_s[:].indirect(list1[:, 0:32]))
@@ -360,9 +370,8 @@ def tile_list_strata_contacts_kernel(
         deal(nc.vector.tensor_copy, "w23_s_dealt", upper_scales, U8, ODD_TERMS)
         put_in_page(0, list2[:, 32:64], h[0, 1][:], wgs_sb[:, HALF:S])
         products(3)
-        first_stage(2, False)
         for slab in range(1, 7):
-            if slab > 1:
+            if slab > 2:
                 second_stage(slab + 1)
             read_h(2 * slab, transposed_sum(unit_terms[2 * slab]))
             if slab == 1:
@@ -373,11 +382,14 @@ def tile_list_strata_contacts_kernel(
             read_h(2 * slab + 1, transposed_sum(unit_terms[2 * slab + 1]))
             put_slab(slab)
             if slab == 1:
+                first_stage(2, False)
                 second_stage(2)
-                quantize_w1(2, HALF, ODD_TERMS + 2 * TERM)
+                quantize_upper_w1(0)
+            if slab == 2:
+                second_stage(3)
+                quantize_upper_w1(1)
                 for a in range(2):
                     raw["w4", a] = load_rows(f"w4_raw{a}", w4[512 * a : 512 * (a + 1), :], W1_RAW + 4 * TERM * a)
-            if slab == 2:
                 own = PRODUCTS + 6 * TERM
                 deal(nc.scalar.copy, "w2_dealt", w2_rest[:, W1_PIECE:].bitcast(U32).unsqueeze(1), U32, own)
                 deal(nc.scalar.copy, "w3_dealt", w3_w[:, H:].bitcast(U16).unsqueeze(1), U16, own + TERM)

@@ -67,9 +67,10 @@ def tile_list_strata_contacts_kernel(
             taken.append(FIRST_BANKS[len(taken)] if len(taken) < len(FIRST_BANKS) else taken[-8])
             return psum.tile([P, 512], F32, name=f"bank{taken[-1]}")
 
-        def load_scale_rows(queue, plane, rows):
+        def load_scale_rows(queue, plane, rows, first=0):
             for q in range(4):
-                queue.dma_start(out=plane[32 * q : 32 * q + 4].bitcast(I32), in_=rows[4 * q : 4 * q + 4].bitcast(I32))
+                live = slice(32 * q + first, 32 * q + first + 4)
+                queue.dma_start(out=plane[live].bitcast(I32), in_=rows[4 * q : 4 * q + 4].bitcast(I32))
 
         def load_rows(name, rows, offset):
             raw = placed(name, [P, 4, rows.shape[1]], F32, offset)
@@ -89,7 +90,7 @@ def tile_list_strata_contacts_kernel(
         w2_first = held("w2_first", [P, W1_PIECE], I32)
         w2_rest = held("w2_rest", [P, H - W1_PIECE], I32)
         w3_w = held("w3_w", [P, 2 * H], U8)
-        w23_s = held("w23_s", [P, 2 * H], U8)
+        packed_s = held("packed_s", [P, H], U8)
         w5_s = held("w5_s", [P, 2, N], U8)
         w5_w = held("w5_w", [P, 2, 2 * N], U8)
         wgs_sb = held("wgs_sb", [P, S], F32)
@@ -97,12 +98,11 @@ def tile_list_strata_contacts_kernel(
         pages = [held(f"page{i}", [P, T2], F32) for i in range(2)]
         ident = held("ident", [P, P], F32)
 
-        nc.gpsimd.memset(w23_s[:, 0:H].bitcast(I32), 0)
+        nc.gpsimd.memset(packed_s[:].bitcast(I32), 0)
         nc.gpsimd.memset(tab_s[:].bitcast(I32)[:, 0:GPSIMD_CLEARS], 0)
         nc.vector.memset(tab_s[:].bitcast(I32)[:, GPSIMD_CLEARS:], 0)
-        nc.vector.memset(w23_s[:, H : 2 * H].bitcast(I32), 0)
         nc.vector.memset(w5_s[:].bitcast(I32), 0)
-        load_scale_rows(nc.gpsimd, w23_s[:, H : 2 * H], w3_scales[0])
+        load_scale_rows(nc.gpsimd, packed_s, w3_scales[0])
         make_identity(nc, ident[:])
         for page in pages:
             nc.vector.memset(page[:], 0.0)
@@ -117,12 +117,16 @@ def tile_list_strata_contacts_kernel(
         nc.sync.dma_start(out=tab_w[:, T // 4 : T], in_=tab_w_dram[:, T // 4 : T])
         nc.sync.dma_start(out=w2_first[:], in_=w2_dram[:, 0:W1_PIECE])
         nc.sync.dma_start(out=w3_w[:].bitcast(I32), in_=w3_words[0].bitcast(I32))
-        load_scale_rows(nc.sync, w23_s[:, 0:H], w2_scales[0])
+        load_scale_rows(nc.sync, packed_s, w2_scales[0], 4)
         nc.sync.dma_start(list2[:], offs2)
         nc.sync.dma_start(out=wgs_sb[:, 0:HALF], in_=wgs[:, 0:HALF])
         raw["w1", 1] = load_rows("w1_raw1", w1[:, W1_PIECE:HALF], W1_RAW + 2 * TERM)
         nc.sync.dma_start(out=wgs_sb[:, HALF:S], in_=wgs[:, HALF:S])
-        load_scale_rows(nc.sync, w5_s, w5_scales.rearrange("a q c -> q a c"))
+        for q in range(4):
+            nc.sync.dma_start(
+                out=packed_s[32 * q + 8 : 32 * q + 16, HALF:H].bitcast(I32),
+                in_=w5_scales[:, 4 * q : 4 * q + 4, :].bitcast(I32),
+            )
         nc.sync.dma_start(list4[:], offs4)
         nc.sync.dma_start(out=hiatus_rows[0][:], in_=hiatus[0:P, :])
         raw["w1", 2] = load_rows("w1_raw2", w1[:, HALF:H], W1_RAW + 4 * TERM)
@@ -212,12 +216,12 @@ def tile_list_strata_contacts_kernel(
                 return minus_w1_c[:, cols].bitcast(FP8X4), minus_w1_s[:, cols]
             if name == "w3":
                 if slab >= 4:
-                    return moved["w3_dealt"][:, 0, upper].bitcast(FP4X4), moved["w23_s_dealt"][:, 1, upper]
-                return w3_w[:, 2 * P * slab : 2 * P * (slab + 1)].bitcast(FP4X4), w23_s[:, H + P * slab : H + P * (slab + 1)]
+                    return moved["w3_dealt"][:, 0, upper].bitcast(FP4X4), moved["dealt_s"][:, 0, upper]
+                return w3_w[:, 2 * P * slab : 2 * P * (slab + 1)].bitcast(FP4X4), packed_s[:, cols]
             if slab >= 4:
-                return moved["w2_dealt"][:, 0, upper].bitcast(FP8X4), moved["w23_s_dealt"][:, 0, upper]
+                return moved["w2_dealt"][:, 0, upper].bitcast(FP8X4), moved["dealt_s"][4:P, 0, upper]
             words = w2_first[:, cols] if slab < 2 else w2_rest[:, P * (slab - 2) : P * (slab - 1)]
-            return words.bitcast(FP8X4), w23_s[:, cols]
+            return words.bitcast(FP8X4), packed_s[4:P, cols]
 
         def by_rows(u, name):
             slab, hf = divmod(u, 2)
@@ -366,8 +370,6 @@ def tile_list_strata_contacts_kernel(
         quantize_w1(1, W1_PIECE, TAB_SCALES)
         products(2)
         read_h(1, transposed_sum(unit_terms[1]))
-        upper_scales = w23_s[:].rearrange("p (a hf c) -> p a hf c", a=2, hf=2)[:, :, 1, :]
-        deal(nc.vector.tensor_copy, "w23_s_dealt", upper_scales, U8, ODD_TERMS)
         put_in_page(0, list2[:, 32:64], h[0, 1][:], wgs_sb[:, HALF:S])
         products(3)
         for slab in range(1, 7):
@@ -375,7 +377,14 @@ def tile_list_strata_contacts_kernel(
                 second_stage(slab + 1)
             read_h(2 * slab, transposed_sum(unit_terms[2 * slab]))
             if slab == 1:
-                deal(nc.vector.tensor_copy, "w5_s_dealt", w5_s[:], U8, EVEN_SECOND)
+                deal(nc.vector.tensor_copy, "dealt_s", packed_s[:, HALF:H].unsqueeze(1), U8, EVEN_SECOND)
+                for a in range(2):
+                    for q in range(4):
+                        first = 32 * q + 8 + 4 * a
+                        nc.sync.dma_start(
+                            out=w5_s[32 * q : 32 * q + 4, a, :].bitcast(I32),
+                            in_=moved["dealt_s"][first : first + 4, 0, :].bitcast(I32),
+                        )
             else:
                 fetch_z(slab - 2)
             fetch_below(slab - 1)
@@ -423,7 +432,7 @@ def tile_list_strata_contacts_kernel(
                 cols = slice(P * t, P * (t + 1))
                 if name == "w5":
                     lhsT = moved["w5_dealt"][:, a, cols].bitcast(FP4X4)
-                    lhsT_scale = moved["w5_s_dealt"][:, a, cols]
+                    lhsT_scale = w5_s[:, a, cols]
                 else:
                     lhsT = quant[name, a][0][:, cols].bitcast(FP8X4)
                     lhsT_scale = quant[name, a][1][:, cols]

@@ -375,7 +375,7 @@ def tile_list_strata_contacts_kernel(
         for slab in range(1, 7):
             if slab > 2:
                 second_stage(slab + 1)
-            read_h(2 * slab, transposed_sum(unit_terms[2 * slab]))
+            read_h(2 * slab, transposed_sum(unit_terms[2 * slab][::-1]))
             if slab == 1:
                 deal(nc.vector.tensor_copy, "dealt_s", packed_s[:, HALF:H].unsqueeze(1), U8, EVEN_SECOND)
                 for a in range(2):
@@ -407,7 +407,7 @@ def tile_list_strata_contacts_kernel(
                 name, a = LATE_OPERANDS[slab]
                 quantize_operand(name, a, raw[name, a][:], ODD_TERMS + TERM * (2 * slab - 2))
         deal(nc.scalar.copy, "w5_dealt", w5_w[:].bitcast(U16), U16, PRODUCTS + 8 * TERM)
-        last_sums = [transposed_sum(unit_terms[u]) for u in (14, 15)]
+        last_sums = [transposed_sum(unit_terms[u][::-1]) for u in (14, 15)]
         fetch_z(5)
         fetch_below(6)
         quantize_operand("z", 0, z_dealt[:], ODD_TERMS + 14 * TERM)

@@ -19,9 +19,10 @@ ACT = mybir.ActivationFunctionType
 
 P = 128
 HALF = 512
+QUARTER = 256
 W1_PIECE = 256
 FIRST_PARTS = (slice(0, 256), slice(256, 512))
-GPSIMD_CLEARS = 576
+GPSIMD_CLEARS = 320
 ROUND_GROUPS = 32
 UNITS = 16
 RELU_UNITS = (1, 2, 3, 5, 7, 9, 11)
@@ -40,6 +41,7 @@ EVEN_SECOND = EVEN_FIRST + 7 * TERM
 PRODUCTS = EVEN_SECOND + 7 * TERM
 H_RING = PRODUCTS + 9 * TERM
 Z_DEALT = H_RING + 6 * TERM
+W1_FIRST = Z_DEALT + 4 * TERM
 
 
 def tile_list_strata_contacts_kernel(
@@ -83,7 +85,8 @@ def tile_list_strata_contacts_kernel(
         list4 = held("list4", [P, M // 16], U16)
         tab_w = placed("tab_w", [P, T], I32, TAB_WORDS)
         tab_s = placed("tab_s", [P, T], U8, TAB_SCALES)
-        v_w = [held(f"v_w{hf}", [P, HALF], U32) for hf in range(2)]
+        v_front = held("v_front", [P, HALF], U32)
+        v_third = held("v_third", [P, QUARTER], U32)
         v_s = [held(f"v_s{hf}", [P, HALF], U8) for hf in range(2)]
         minus_w1_c = held("minus_w1_c", [P, H], U32)
         minus_w1_s = held("minus_w1_s", [P, H], U8)
@@ -98,8 +101,8 @@ def tile_list_strata_contacts_kernel(
         pages = [held(f"page{i}", [P, T2], F32) for i in range(2)]
         ident = held("ident", [P, P], F32)
 
-        nc.gpsimd.memset(packed_s[:].bitcast(I32), 0)
         nc.gpsimd.memset(tab_s[:].bitcast(I32)[:, 0:GPSIMD_CLEARS], 0)
+        nc.gpsimd.memset(packed_s[:].bitcast(I32), 0)
         nc.vector.memset(tab_s[:].bitcast(I32)[:, GPSIMD_CLEARS:], 0)
         nc.vector.memset(w5_s[:].bitcast(I32), 0)
         load_scale_rows(nc.gpsimd, packed_s, w3_scales[0])
@@ -113,11 +116,12 @@ def tile_list_strata_contacts_kernel(
         nc.sync.dma_start(list1[:], offs)
         nc.sync.dma_start(out=tab_w[:, 0 : T // 4], in_=tab_w_dram[:, 0 : T // 4])
         load_scale_rows(nc.sync, tab_s, tab_scales[0])
-        raw["w1", 0] = load_rows("w1_raw0", w1[:, 0:W1_PIECE], W1_RAW)
         nc.sync.dma_start(out=tab_w[:, T // 4 : T], in_=tab_w_dram[:, T // 4 : T])
+        raw["w1", 0] = load_rows("w1_raw0", w1[:, 0:P], W1_FIRST)
         nc.sync.dma_start(out=w2_first[:], in_=w2_dram[:, 0:W1_PIECE])
         nc.sync.dma_start(out=w3_w[:].bitcast(I32), in_=w3_words[0].bitcast(I32))
         load_scale_rows(nc.sync, packed_s, w2_scales[0], 4)
+        raw["w1", 3] = load_rows("w1_raw3", w1[:, P:W1_PIECE], W1_RAW + TERM)
         nc.sync.dma_start(list2[:], offs2)
         nc.sync.dma_start(out=wgs_sb[:, 0:HALF], in_=wgs[:, 0:HALF])
         raw["w1", 1] = load_rows("w1_raw1", w1[:, W1_PIECE:HALF], W1_RAW + 2 * TERM)
@@ -177,9 +181,16 @@ def tile_list_strata_contacts_kernel(
 
         nc.vector.tensor_copy(out=v_s[0][:], in_=tab_s[:].indirect(list1[:, 0:32]))
         nc.vector.tensor_copy(out=v_s[1][:], in_=tab_s[:].indirect(list1[:, 32:64]))
+        nc.vector.tensor_copy(out=v_front[:], in_=tab_w[:].bitcast(U32).indirect(list1[:, 0:32]))
+        nc.vector.tensor_copy(out=v_third[:], in_=tab_w[:].bitcast(U32).indirect(list1[:, 32:48]))
         quantize_w1(0, 0, H_RING + 4 * TERM)
-        nc.vector.tensor_copy(out=v_w[0][:], in_=tab_w[:].bitcast(U32).indirect(list1[:, 0:32]))
-        nc.vector.tensor_copy(out=v_w[1][:], in_=tab_w[:].bitcast(U32).indirect(list1[:, 32:64]))
+        v_last = placed("v_last", [P, QUARTER], U32, W1_FIRST)
+        nc.vector.tensor_copy(out=v_last[:], in_=tab_w[:].bitcast(U32).indirect(list1[:, 48:64]))
+
+        def v_words(hf, c0, width):
+            if hf == 0:
+                return v_front[:, c0 : c0 + width].bitcast(FP8X4)
+            return (v_third, v_last)[c0 // QUARTER][:, c0 % QUARTER : c0 % QUARTER + width].bitcast(FP8X4)
 
         wgs_by_t = wgs.rearrange("(i t) j -> t i j", t=4)
         wgs_dealt = [placed(f"wgs_dealt{t}", [P, S], F32, (G_RAW + 4 * TERM, G_RAW + 6 * TERM, W6_RAW + 4 * TERM, W6_RAW + 6 * TERM)[t]) for t in range(4)]
@@ -227,10 +238,12 @@ def tile_list_strata_contacts_kernel(
             slab, hf = divmod(u, 2)
             codes, scales = weights(name, slab)
             acc = bank()
-            nc.tensor.matmul_mx(
-                out=acc[:], lhsT=codes, lhsT_scale=scales,
-                rhs=v_w[hf][:].bitcast(FP8X4), rhs_scale=v_s[hf][:], start=True, stop=True,
-            )
+            width = QUARTER if hf else HALF
+            for c0 in range(0, HALF, width):
+                nc.tensor.matmul_mx(
+                    out=acc[:, c0 : c0 + width], lhsT=codes, lhsT_scale=scales,
+                    rhs=v_words(hf, c0, width), rhs_scale=v_s[hf][:, c0 : c0 + width], start=True, stop=True,
+                )
             return acc
 
         def by_entries(u, names):
@@ -241,7 +254,7 @@ def tile_list_strata_contacts_kernel(
                 for n, name in enumerate(names):
                     codes, scales = weights(name, slab)
                     nc.tensor.matmul_mx(
-                        out=acc[:, cols], lhsT=v_w[hf][:, cols].bitcast(FP8X4), lhsT_scale=v_s[hf][:, cols],
+                        out=acc[:, cols], lhsT=v_words(hf, P * x, P), lhsT_scale=v_s[hf][:, cols],
                         rhs=codes, rhs_scale=scales, start=(n == 0), stop=(n == len(names) - 1),
                     )
             return acc
@@ -315,6 +328,7 @@ def tile_list_strata_contacts_kernel(
             for cols in FIRST_PARTS:
                 nc.scalar.activation(out=d1_sb[:, cols], in_=d["minus_w1"][:, cols], func=ACT.Copy, scale=-1.0)
                 nc.vector.tensor_tensor(out=first_larger[:, cols], in0=d["w2"][:, cols], in1=d1_sb[:, cols], op=ALU.max)
+            quantize_w1(3, P, H_RING + 5 * TERM)
             for cols in FIRST_PARTS:
                 nc.vector.tensor_tensor(out=h[0, 0][:, cols], in0=first_larger[:, cols], in1=d["w3"][:, cols], op=ALU.subtract)
 

from contextlib import ExitStack

import concourse.mybir as mybir
from concourse.masks import make_identity

K, T, S, T2, M, H, N = 512, 4096, 1024, 2048, 512, 1024, 512
FLOPS = 2 * (3 * K * H * S + 3 * H * N * M)

F32 = mybir.dt.float32
BF16 = mybir.dt.bfloat16
I32 = mybir.dt.int32
U32 = mybir.dt.uint32
U16 = mybir.dt.uint16
U8 = mybir.dt.uint8
FP8X4 = mybir.dt.float8_e4m3fn_x4
FP4X4 = mybir.dt.float4_e2m1fn_x4
ALU = mybir.AluOpType
ACT = mybir.ActivationFunctionType

P = 128
HALF = 512
QUARTER = 256
W1_PIECE = 256
FIRST_PARTS = (slice(0, 256), slice(256, 512))
GPSIMD_CLEARS = 320
ROUND_GROUPS = 32
UNITS = 16
RELU_UNITS = (1, 2, 3, 5, 7, 9, 11)
DEAL_UNIT = 4
FIRST_BANKS = (0, 1, 2, 0, 1, 3, 2, 4, 5, 1, 6, 7, 0)
LATE_OPERANDS = {3: ("g", 0), 4: ("w6", 0), 5: ("g", 1), 6: ("w6", 1)}

TERM = 2048
TAB_WORDS, TAB_SCALES = 0, 16384
W1_RAW = 20480
G_RAW = W1_RAW + 8 * TERM
W6_RAW = G_RAW + 8 * TERM
ODD_TERMS = W6_RAW + 8 * TERM
EVEN_FIRST = ODD_TERMS + 16 * TERM
EVEN_SECOND = EVEN_FIRST + 7 * TERM
PRODUCTS = EVEN_SECOND + 7 * TERM
H_RING = PRODUCTS + 9 * TERM
Z_DEALT = H_RING + 6 * TERM
W1_FIRST = Z_DEALT + 4 * TERM


def tile_list_strata_contacts_kernel(
    tc, tab_words, tab_scales, offs, w1, w2_words, w2_scales, w3_words, w3_scales, offs2, wgs,
    offs3, offs4, hiatus, w4, w5_words, w5_scales, w6, out_0, out_1, out_2,
):
    nc = tc.nc
    with ExitStack() as ctx:
        keep = ctx.enter_context(tc.tile_pool(name="keep", bufs=1))
        shared = ctx.enter_context(tc.tile_pool(name="shared", bufs=1))
        psum = ctx.enter_context(tc.psum_pool(name="psum", bufs=1))

        def held(name, shape, dtype):
            return keep.tile(shape, dtype, name=name, align_bytes=64)

        def placed(name, shape, dtype, offset):
            return shared.tile(shape, dtype, name=name, offset=offset, align_bytes=64)

        def term(name, offset):
            return placed(name, [P, 512], F32, offset)

        taken = []

        def bank():
            taken.append(FIRST_BANKS[len(taken)] if len(taken) < len(FIRST_BANKS) else taken[-8])
            return psum.tile([P, 512], F32, name=f"bank{taken[-1]}")

        def load_scale_rows(queue, plane, rows, first=0):
            for q in range(4):
                live = slice(32 * q + first, 32 * q + first + 4)
                queue.dma_start(out=plane[live].bitcast(I32), in_=rows[4 * q : 4 * q + 4].bitcast(I32))

        def load_rows(name, rows, offset):
            raw = placed(name, [P, 4, rows.shape[1]], F32, offset)
            nc.sync.dma_start(out=raw[:], in_=rows.rearrange("(p j) w -> p j w", j=4))
            return raw

        list1 = held("list1", [P, S // 16], U16)
        list2 = held("list2", [P, S // 16], U16)
        list3 = held("list3", [P, M // 16], U16)
        list4 = held("list4", [P, M // 16], U16)
        tab_w = placed("tab_w", [P, T], I32, TAB_WORDS)
        tab_s = placed("tab_s", [P, T], U8, TAB_SCALES)
        v_front = held("v_front", [P, HALF], U32)
        v_third = held("v_third", [P, QUARTER], U32)
        v_s = [held(f"v_s{hf}", [P, HALF], U8) for hf in range(2)]
        minus_w1_c = held("minus_w1_c", [P, H], U32)
        minus_w1_s = held("minus_w1_s", [P, H], U8)
        w2_first = held("w2_first", [P, W1_PIECE], I32)
        w2_rest = held("w2_rest", [P, H - W1_PIECE], I32)
        w3_w = held("w3_w", [P, 2 * H], U8)
        packed_s = held("packed_s", [P, H], U8)
        w5_s = held("w5_s", [P, 2, N], U8)
        w5_w = held("w5_w", [P, 2, 2 * N], U8)
        wgs_sb = held("wgs_sb", [P, S], F32)
        hiatus_rows = [held(f"hiatus_rows{b}", [P, M], F32) for b in range(4)]
        pages = [held(f"page{i}", [P, T2], F32) for i in range(2)]
        ident = held("ident", [P, P], F32)

        nc.gpsimd.memset(tab_s[:].bitcast(I32)[:, 0:GPSIMD_CLEARS], 0)
        nc.gpsimd.memset(packed_s[:].bitcast(I32), 0)
        nc.vector.memset(tab_s[:].bitcast(I32)[:, GPSIMD_CLEARS:], 0)
        nc.vector.memset(w5_s[:].bitcast(I32), 0)
        load_scale_rows(nc.gpsimd, packed_s, w3_scales[0])
        make_identity(nc, ident[:])
        for page in pages:
            nc.vector.memset(page[:], 0.0)

        tab_w_dram = tab_words[0].rearrange("p t i -> p (t i)").bitcast(I32)
        w2_dram = w2_words[0].rearrange("p c i -> p (c i)").bitcast(I32)
        raw = {}
        nc.sync.dma_start(list1[:], offs)
        nc.sync.dma_start(out=tab_w[:, 0 : T // 4], in_=tab_w_dram[:, 0 : T // 4])
        load_scale_rows(nc.sync, tab_s, tab_scales[0])
        nc.sync.dma_start(out=tab_w[:, T // 4 : T], in_=tab_w_dram[:, T // 4 : T])
        raw["w1", 0] = load_rows("w1_raw0", w1[:, 0:P], W1_FIRST)
        nc.sync.dma_start(out=w2_first[:], in_=w2_dram[:, 0:W1_PIECE])
        nc.sync.dma_start(out=w3_w[:].bitcast(I32), in_=w3_words[0].bitcast(I32))
        load_scale_rows(nc.sync, packed_s, w2_scales[0], 4)
        raw["w1", 3] = load_rows("w1_raw3", w1[:, P:W1_PIECE], W1_RAW + TERM)
        nc.sync.dma_start(list2[:], offs2)
        nc.sync.dma_start(out=wgs_sb[:, 0:HALF], in_=wgs[:, 0:HALF])
        raw["w1", 1] = load_rows("w1_raw1", w1[:, W1_PIECE:HALF], W1_RAW + 2 * TERM)
        nc.sync.dma_start(out=wgs_sb[:, HALF:S], in_=wgs[:, HALF:S])
        for q in range(4):
            nc.sync.dma_start(
                out=packed_s[32 * q + 8 : 32 * q + 16, HALF:H].bitcast(I32),
                in_=w5_scales[:, 4 * q : 4 * q + 4, :].bitcast(I32),
            )
        nc.sync.dma_start(list4[:], offs4)
        nc.sync.dma_start(out=hiatus_rows[0][:], in_=hiatus[0:P, :])
        raw["w1", 2] = load_rows("w1_raw2", w1[:, HALF:H], W1_RAW + 4 * TERM)
        nc.sync.dma_start(out=w2_rest[:], in_=w2_dram[:, W1_PIECE:H])
        nc.sync.dma_start(out=w5_w[:].bitcast(I32), in_=w5_words.rearrange("a p c -> p a c").bitcast(I32))
        nc.sync.dma_start(list3[:], offs3)
        raw["g", 0] = load_rows("g_raw0", hiatus[0:512, :], G_RAW)
        nc.sync.dma_start(out=hiatus_rows[1][:], in_=hiatus[P : 2 * P, :])

        def round_rows(rows, grouped, dealt, negated=False):
            width = rows.shape[2]
            if dealt:
                dst = grouped[:].rearrange("p (t m j) -> p m j t", t=4, j=4)
                src = rows.rearrange("p j (m t) -> p m j t", t=4)
            else:
                dst = grouped[:].rearrange("p (c i j) -> p c j i", i=4, j=4)
                src = rows.rearrange("p j (c i) -> p c j i", i=4)
            for c0 in range(0, width // 4, ROUND_GROUPS):
                if negated:
                    nc.scalar.activation(out=dst[:, c0 : c0 + ROUND_GROUPS], in_=src[:, c0 : c0 + ROUND_GROUPS], func=ACT.Copy, scale=-1.0)
                else:
                    nc.scalar.copy(out=dst[:, c0 : c0 + ROUND_GROUPS], in_=src[:, c0 : c0 + ROUND_GROUPS])
            return grouped

        def quantize(grouped, name, offset=None):
            width = grouped.shape[1] // 4
            codes = held(name + "_c", [P, width], U32) if offset is None else placed(name + "_c", [P, width], U32, offset)
            scales = held(name + "_s", [P, width], U8)
            nc.vector.quantize_mx(out=codes[:].bitcast(FP8X4), scales=scales[:], in_=grouped[:])
            return codes, scales

        def quantize_w1(i, c0, offset):
            width = raw["w1", i].shape[2]
            grouped = placed(f"w1_grouped{i}", [P, 4 * width], BF16, offset)
            round_rows(raw["w1", i][:], grouped, False, True)
            cols = slice(c0, c0 + width)
            nc.vector.quantize_mx(out=minus_w1_c[:, cols].bitcast(FP8X4), scales=minus_w1_s[:, cols], in_=grouped[:])

        def quantize_upper_w1(pair):
            grouped = placed(f"w1_upper{pair}", [P, 4 * W1_PIECE], BF16, ODD_TERMS + TERM * (2 + pair))
            dst = grouped[:].rearrange("p (t m j) -> p m j t", t=2, j=4)
            src = raw["w1", 2][:].rearrange("p j (m t) -> p m j t", t=4)[:, :, :, 2 * pair : 2 * pair + 2]
            for c0 in range(0, P, 2 * ROUND_GROUPS):
                part = slice(c0, c0 + 2 * ROUND_GROUPS)
                nc.scalar.activation(out=dst[:, part], in_=src[:, part], func=ACT.Copy, scale=-1.0)
            cols = slice(HALF + W1_PIECE * pair, HALF + W1_PIECE * (pair + 1))
            nc.vector.quantize_mx(out=minus_w1_c[:, cols].bitcast(FP8X4), scales=minus_w1_s[:, cols], in_=grouped[:])

        nc.vector.tensor_copy(out=v_s[0][:], in_=tab_s[:].indirect(list1[:, 0:32]))
        nc.vector.tensor_copy(out=v_s[1][:], in_=tab_s[:].indirect(list1[:, 32:64]))
        nc.vector.tensor_copy(out=v_front[:], in_=tab_w[:].bitcast(U32).indirect(list1[:, 0:32]))
        nc.vector.tensor_copy(out=v_third[:], in_=tab_w[:].bitcast(U32).indirect(list1[:, 32:48]))
        quantize_w1(0, 0, H_RING + 4 * TERM)
        v_last = placed("v_last", [P, QUARTER], U32, W1_FIRST)
        nc.vector.tensor_copy(out=v_last[:], in_=tab_w[:].bitcast(U32).indirect(list1[:, 48:64]))

        def v_words(hf, c0, width):
            if hf == 0:
                return v_front[:, c0 : c0 + width].bitcast(FP8X4)
            return (v_third, v_last)[c0 // QUARTER][:, c0 % QUARTER : c0 % QUARTER + width].bitcast(FP8X4)

        wgs_by_t = wgs.rearrange("(i t) j -> t i j", t=4)
        wgs_dealt = [placed(f"wgs_dealt{t}", [P, S], F32, (G_RAW + 4 * TERM, G_RAW + 6 * TERM, W6_RAW + 4 * TERM, W6_RAW + 6 * TERM)[t]) for t in range(4)]

        def load_wgs_dealt(t):
            for q in range(4):
                nc.sync.dma_start(out=wgs_dealt[t][32 * q : 32 * (q + 1), :], in_=wgs_by_t[t])

        nc.sync.dma_start(out=hiatus_rows[2][:], in_=hiatus[2 * P : 3 * P, :])
        load_wgs_dealt(0)
        raw["w6", 0] = load_rows("w6_raw0", w6[0:512, :], W6_RAW)
        nc.sync.dma_start(out=hiatus_rows[3][:], in_=hiatus[3 * P : 4 * P, :])
        load_wgs_dealt(1)
        raw["g", 1] = load_rows("g_raw1", hiatus[512:1024, :], TAB_WORDS)
        load_wgs_dealt(2)
        raw["w6", 1] = load_rows("w6_raw1", w6[512:1024, :], TAB_WORDS + 4 * TERM)
        load_wgs_dealt(3)

        moved = {}

        def deal(engine, name, source, dtype, offset):
            planes, width = source.shape[1], source.shape[2]
            walk = "p a t m" if dtype == U8 else "p a m t"
            moved[name] = placed(name, [P, planes, width], dtype, offset)
            engine(
                out=moved[name][:].rearrange(f"p a (t m) -> {walk}", t=4),
                in_=source.rearrange(f"p a (m t) -> {walk}", t=4),
            )

        def weights(name, slab):
            cols = slice(P * slab, P * (slab + 1))
            upper = slice(P * (slab - 4), P * (slab - 3))
            if name == "minus_w1":
                return minus_w1_c[:, cols].bitcast(FP8X4), minus_w1_s[:, cols]
            if name == "w3":
                if slab >= 4:
                    return moved["w3_dealt"][:, 0, upper].bitcast(FP4X4), moved["dealt_s"][:, 0, upper]
                return w3_w[:, 2 * P * slab : 2 * P * (slab + 1)].bitcast(FP4X4), packed_s[:, cols]
            if slab >= 4:
                return moved["w2_dealt"][:, 0, upper].bitcast(FP8X4), moved["dealt_s"][4:P, 0, upper]
            words = w2_first[:, cols] if slab < 2 else w2_rest[:, P * (slab - 2) : P * (slab - 1)]
            return words.bitcast(FP8X4), packed_s[4:P, cols]

        def by_rows(u, name):
            slab, hf = divmod(u, 2)
            codes, scales = weights(name, slab)
            acc = bank()
            width = QUARTER if hf else HALF
            for c0 in range(0, HALF, width):
                nc.tensor.matmul_mx(
                    out=acc[:, c0 : c0 + width], lhsT=codes, lhsT_scale=scales,
                    rhs=v_words(hf, c0, width), rhs_scale=v_s[hf][:, c0 : c0 + width], start=True, stop=True,
                )
            return acc

        def by_entries(u, names):
            slab, hf = divmod(u, 2)
            acc = bank()
            for x in range(4):
                cols = slice(P * x, P * (x + 1))
                for n, name in enumerate(names):
                    codes, scales = weights(name, slab)
                    nc.tensor.matmul_mx(
                        out=acc[:, cols], lhsT=v_words(hf, P * x, P), lhsT_scale=v_s[hf][:, cols],
                        rhs=codes, rhs_scale=scales, start=(n == 0), stop=(n == len(names) - 1),
                    )
            return acc

        def transposed_sum(terms):
            acc = bank()
            for x in range(4):
                for n, tile in enumerate(terms):
                    nc.tensor.matmul(
                        acc[:, P * x : P * (x + 1)], tile[:, P * x : P * (x + 1)], ident[:], is_transpose=True,
                        start=(x == 0 and n == 0), stop=(x == 3 and n == len(terms) - 1),
                    )
            return acc

        z_front = placed("z_front", [P, 2, M], F32, EVEN_SECOND + 5 * TERM)
        z_dealt = placed("z_dealt", [P, 4, M], F32, Z_DEALT)
        unit_terms, unit_products, h = {}, {}, {}

        def last_terms(u):
            if u % 2 == 1:
                offset = ODD_TERMS + TERM * (u - 1)
                return term(f"first_term{u}", offset)[:], term(f"second_term{u}", offset + TERM)[:]
            i = u // 2 - 1
            second = term(f"second_term{u}", EVEN_SECOND + TERM * i)[:] if i < 5 else z_front[:, i - 5, :]
            return term(f"first_term{u}", EVEN_FIRST + TERM * i)[:], second

        def by_relu(u):
            return u in RELU_UNITS

        def products(u):
            if by_relu(u):
                first, second = last_terms(u)
                nc.scalar.activation(out=first, in_=by_entries(u, ("w2", "minus_w1"))[:], func=ACT.Relu)
                nc.scalar.activation(out=second, in_=by_entries(u, ("w3", "minus_w1"))[:], func=ACT.Copy, scale=-1.0)
                unit_terms[u] = (first, second)
                return
            slot = 2 if u == DEAL_UNIT else len(unit_products) % 2
            unit_products[u] = {}
            for n, name in enumerate(("minus_w1", "w2", "w3")):
                tile = term(f"{name}_product{u}", PRODUCTS + TERM * (3 * slot + n))
                nc.scalar.copy(out=tile[:], in_=by_rows(u, name)[:])
                unit_products[u][name] = tile[:]

        def differences(u):
            if by_relu(u):
                return
            d = unit_products[u]
            first, second = last_terms(u)
            nc.scalar.activation(out=first, in_=transposed_sum((d["minus_w1"], d["w2"]))[:], func=ACT.Relu)
            nc.scalar.activation(out=second, in_=transposed_sum((d["minus_w1"], d["w3"]))[:], func=ACT.Copy, scale=-1.0)
            unit_terms[u] = (first, second)

        def read_h(u, acc):
            slab, hf = divmod(u, 2)
            if slab == 7:
                out = z_dealt[:, hf, :]
            elif slab == 0:
                h[0, 1] = term("h0_back", H_RING + TERM)
                out = h[0, 1][:]
            else:
                if hf == 0:
                    h[slab] = placed(f"h{slab}", [P, S], F32, H_RING + 2 * TERM * (slab % 3))
                out = h[slab][:, HALF * hf : HALF * (hf + 1)]
            nc.scalar.copy(out=out, in_=acc[:])

        def first_unit():
            d = {name: by_rows(0, name) for name in ("minus_w1", "w2", "w3")}
            d1_sb = term("first_d1", TAB_SCALES)
            first_larger = term("first_larger", TAB_SCALES + TERM)
            h[0, 0] = term("h0_front", H_RING)
            for cols in FIRST_PARTS:
                nc.scalar.activation(out=d1_sb[:, cols], in_=d["minus_w1"][:, cols], func=ACT.Copy, scale=-1.0)
                nc.vector.tensor_tensor(out=first_larger[:, cols], in0=d["w2"][:, cols], in1=d1_sb[:, cols], op=ALU.max)
            quantize_w1(3, P, H_RING + 5 * TERM)
            for cols in FIRST_PARTS:
                nc.vector.tensor_tensor(out=h[0, 0][:, cols], in0=first_larger[:, cols], in1=d["w3"][:, cols], op=ALU.subtract)

        def put_in_page(slab, entries, values, factors):
            nc.vector.tensor_tensor(out=pages[slab % 2][:].indirect(entries), in0=values, in1=factors, op=ALU.mult)

        def put_slab(slab):
            values = h[slab][:] if slab < 7 else z_dealt[:, 0:2, :].rearrange("p a m -> p (a m)")
            put_in_page(slab, list2[:], values, (wgs_sb if slab < 4 else wgs_dealt[slab - 4])[:])

        def fetch_minus(slab, columns, m0, width, other, out):
            nc.vector.tensor_tensor(
                out=out, in0=pages[slab % 2][:].indirect(columns[:, m0 // 16 : (m0 + width) // 16]),
                in1=other, op=ALU.subtract,
            )

        below = {}

        def fetch_below(slab):
            below[slab] = term(f"below{slab}", EVEN_FIRST + TERM * slab)
            given = hiatus_rows[slab][:] if slab < 4 else raw["g", 1][:, slab - 4, :]
            fetch_minus(slab, list4, 0, M, given, below[slab][:])

        def fetch_z(slab):
            if slab >= 4:
                out = z_front[:, slab - 4, :] if slab < 6 else z_dealt[:, 2, :]
                fetch_minus(slab, list3, 0, M, below[slab][:], out)
                return
            z_rows = term(f"z_rows{slab}", EVEN_SECOND + TERM * (slab + 1))
            fetch_minus(slab, list3, 0, M, below[slab][:], z_rows[:])
            for t in range(4):
                nc.sync.dma_start(out=z_dealt[32 * slab : 32 * (slab + 1), t, :], in_=z_rows[t:P:4, :])

        quant = {}

        def quantize_operand(name, a, rows, offset):
            grouped = placed(f"{name}_grouped{a}", [P, 4 * 512], BF16, offset)
            quant[name, a] = quantize(round_rows(rows, grouped, name in ("w4", "w6")), f"{name}{a}")

        def first_stage(slab, relu):
            for u in (2 * slab, 2 * slab + 1):
                if u < UNITS and by_relu(u) == relu:
                    products(u)

        def second_stage(slab):
            first_stage(slab, True)
            for u in (2 * slab, 2 * slab + 1):
                differences(u)

        first_unit()
        products(1)
        put_in_page(0, list2[:, 0:32], h[0, 0][:], wgs_sb[:, 0:HALF])
        quantize_w1(1, W1_PIECE, TAB_SCALES)
        products(2)
        read_h(1, transposed_sum(unit_terms[1]))
        put_in_page(0, list2[:, 32:64], h[0, 1][:], wgs_sb[:, HALF:S])
        products(3)
        for slab in range(1, 7):
            if slab > 2:
                second_stage(slab + 1)
            read_h(2 * slab, transposed_sum(unit_terms[2 * slab][::-1]))
            if slab == 1:
                deal(nc.vector.tensor_copy, "dealt_s", packed_s[:, HALF:H].unsqueeze(1), U8, EVEN_SECOND)
                for a in range(2):
                    for q in range(4):
                        first = 32 * q + 8 + 4 * a
                        nc.sync.dma_start(
                            out=w5_s[32 * q : 32 * q + 4, a, :].bitcast(I32),
                            in_=moved["dealt_s"][first : first + 4, 0, :].bitcast(I32),
                        )
            else:
                fetch_z(slab - 2)
            fetch_below(slab - 1)
            read_h(2 * slab + 1, transposed_sum(unit_terms[2 * slab + 1]))
            put_slab(slab)
            if slab == 1:
                first_stage(2, False)
                second_stage(2)
                quantize_upper_w1(0)
            if slab == 2:
                second_stage(3)
                quantize_upper_w1(1)
                for a in range(2):
                    raw["w4", a] = load_rows(f"w4_raw{a}", w4[512 * a : 512 * (a + 1), :], W1_RAW + 4 * TERM * a)
                own = PRODUCTS + 6 * TERM
                deal(nc.scalar.copy, "w2_dealt", w2_rest[:, W1_PIECE:].bitcast(U32).unsqueeze(1), U32, own)
                deal(nc.scalar.copy, "w3_dealt", w3_w[:, H:].bitcast(U16).unsqueeze(1), U16, own + TERM)
            first_stage(slab + 2, False)
            if slab in LATE_OPERANDS:
                name, a = LATE_OPERANDS[slab]
                quantize_operand(name, a, raw[name, a][:], ODD_TERMS + TERM * (2 * slab - 2))
        deal(nc.scalar.copy, "w5_dealt", w5_w[:].bitcast(U16), U16, PRODUCTS + 8 * TERM)
        last_sums = [transposed_sum(unit_terms[u][::-1]) for u in (14, 15)]
        fetch_z(5)
        fetch_below(6)
        quantize_operand("z", 0, z_dealt[:], ODD_TERMS + 14 * TERM)
        fetch_z(6)
        read_h(14, last_sums[0])
        read_h(15, last_sums[1])
        put_slab(7)
        quantize_operand("w4", 1, raw["w4", 1][:], ODD_TERMS + 12 * TERM)
        quantize_operand("w4", 0, raw["w4", 0][:], EVEN_FIRST + 5 * TERM)

        def round_pair(grouped, u, planes):
            nc.scalar.copy(
                out=grouped[:].rearrange("p (m u e) -> p u m e", u=2, e=2)[:, u], in_=planes.rearrange("p e m -> p m e")
            )

        z_grouped = [placed(f"z_grouped{q}", [P, 4 * P], BF16, W1_RAW + 4096 + 1024 * q) for q in range(4)]
        for q in range(4):
            round_pair(z_grouped[q], 0, z_front[:, :, P * q : P * (q + 1)])

        def mx_passes(acc, name, a, q, start, stop):
            for t in range(4):
                cols = slice(P * t, P * (t + 1))
                if name == "w5":
                    lhsT = moved["w5_dealt"][:, a, cols].bitcast(FP4X4)
                    lhsT_scale = w5_s[:, a, cols]
                else:
                    lhsT = quant[name, a][0][:, cols].bitcast(FP8X4)
                    lhsT_scale = quant[name, a][1][:, cols]
                codes, scales = quant["g", a] if name == "w6" else quant["z", a] if a == 0 else quant["z", a, q]
                m_cols = slice(0, P) if (name != "w6" and a == 1) else slice(P * q, P * (q + 1))
                nc.tensor.matmul_mx(
                    out=acc[:, cols], lhsT=lhsT, lhsT_scale=lhsT_scale,
                    rhs=codes[:, m_cols].bitcast(FP8X4), rhs_scale=scales[:, m_cols],
                    start=(start and t == 0), stop=(stop and t == 3),
                )

        sums, gates = {}, {}
        for q in range(4):
            sums[q] = bank()
            mx_passes(sums[q], "w5", 0, q, True, False)
        for a in range(2):
            for q in range(4):
                mx_passes(sums[q], "w6", a, q, False, False)
        for q in range(4):
            gates[q] = bank()
            mx_passes(gates[q], "w4", 0, q, True, False)

        last_below = {}
        for hf in range(2):
            last_below[hf] = placed(f"last_below{hf}", [P, 2 * P], F32, W1_RAW + 1024 * hf)
            fetch_minus(7, list4, 2 * P * hf, 2 * P, raw["g", 1][:, 3, 2 * P * hf : 2 * P * (hf + 1)], last_below[hf][:])
        y_grouped_at = PRODUCTS + 4 * TERM
        for q in range(4):
            cols = slice(P * q, P * (q + 1))
            fetch_minus(7, list3, P * q, P, last_below[q // 2][:, P * (q % 2) : P * (q % 2 + 1)], z_dealt[:, 3, cols])
            round_pair(z_grouped[q], 1, z_dealt[:, 2:4, cols])
            quant["z", 1, q] = quantize(z_grouped[q], f"z1{q}", y_grouped_at + 768 if q == 3 else None)

        out_rows = out_0.rearrange("(p t) m -> p t m", t=4)
        out_words = out_1[0].rearrange("p m t -> p (m t)").bitcast(I32)
        y_c = held("y_c", [P, M], U32)
        y_s = held("y_s", [P, M], U8)
        ys = []
        mx_passes(gates[0], "w4", 1, 0, False, True)
        for q in range(4):
            cols = slice(P * q, P * (q + 1))
            if q < 3:
                mx_passes(gates[q + 1], "w4", 1, q + 1, False, True)
            mx_passes(sums[q], "w5", 1, q, False, True)
            gate = placed(f"gate{q}", [P, 512], F32, PRODUCTS + TERM * q)
            nc.scalar.activation(out=gate[:], in_=gates[q][:], func=ACT.Tanh)
            ys.append(placed(f"y{q}", [P, 4, P], F32, H_RING + TERM * q))
            nc.vector.tensor_tensor(out=ys[q][:].rearrange("p t m -> p (t m)"), in0=sums[q][:], in1=gate[:], op=ALU.mult)
            nc.sync.dma_start(out=out_rows[:, :, cols], in_=ys[q][:])
        for q, y in enumerate(ys):
            cols = slice(P * q, P * (q + 1))
            y_grouped = placed(f"y_grouped{q}", [P, 4 * P], BF16, y_grouped_at + 1024 * q)
            (nc.scalar.copy if q < 2 else nc.vector.tensor_copy)(
                out=y_grouped[:].rearrange("p (c i t) -> p c t i", i=4, t=4),
                in_=y[:].rearrange("p t (c i) -> p c t i", i=4),
            )
            nc.vector.quantize_mx(out=y_c[:, cols].bitcast(FP8X4), scales=y_s[:, cols], in_=y_grouped[:])
            if q % 2 == 1:
                both = slice(P * (q - 1), P * (q + 1))
                nc.sync.dma_start(out=out_words[:, both], in_=y_c[:, both].bitcast(I32))
        for q in range(4):
            queue = (nc.scalar, nc.sync)[q % 2]
            queue.dma_start(out=out_2[0][4 * q : 4 * q + 4].bitcast(I32), in_=y_s[32 * q : 32 * q + 4].bitcast(I32))
